import numpy as np
import ml_dtypes


def mxq(x, axis, fmt="e4m3"):
    dtype, down = {"e4m3": (ml_dtypes.float8_e4m3fn, 7), "e5m2": (ml_dtypes.float8_e5m2, 14)}[fmt]
    v = np.moveaxis(np.asarray(x, np.float32).astype(ml_dtypes.bfloat16).astype(np.float64), axis, -1)
    blocks = v.reshape(v.shape[:-1] + (-1, 32))
    amax = np.abs(blocks).max(-1, keepdims=True)
    byte = np.maximum(np.where(amax > 0, np.frexp(amax)[1] - 1 + 127, 0) - down, 1)
    scale = np.exp2(byte - 127.0)
    codes = (blocks / scale).astype(np.float32).astype(dtype).astype(np.float64)
    return np.moveaxis((codes * scale).reshape(v.shape), -1, axis)


WIDE = False


def mx_kscale(k):
    if not WIDE:
        return np.ones(k)
    levels = np.array([10, -10, 5, -5, 0])
    if k % 512:
        return np.exp2(np.random.permutation(np.resize(levels, k // 32))).repeat(32)
    a = np.empty((k // 512, 16))
    for p in range(k // 512):
        a[p, :8] = np.random.permutation(np.resize(levels, 8))
        for g in range(8):
            far = levels[np.abs(levels - a[p, g]) >= 10]
            a[p, g + 8] = far[np.random.randint(len(far))]
    return np.exp2(a.ravel()).repeat(32)


def f64(x):
    return np.asarray(x).astype(np.float64)


def striped(idx):
    return np.tile(idx.reshape(-1, 16).T, (8, 1)).astype(np.uint16)


def unstriped(offs):
    return offs[:16].T.reshape(-1).astype(np.int64)


E2M1 = np.array([0.0, 0.5, 1.0, 1.5, 2.0, 3.0, 4.0, 6.0, -0.0, -0.5, -1.0, -1.5, -2.0, -3.0, -4.0, -6.0])


def pack_weight(w, fmt):
    k, n = w.shape
    w = f64(np.asarray(w, np.float32).astype(ml_dtypes.bfloat16)).reshape(k // 32, 32, n)
    amax = np.abs(w).max(1)
    if fmt == "e4m3":
        byte = np.frexp(amax)[1] - 1 + 127 - 7
    else:
        mant, ex = np.frexp(amax / 6.0)
        byte = np.where(mant > 0.5, ex, ex - 1) + 127
    byte = np.clip(np.where(amax > 0, byte, 1), 1, 254)
    scaled = (w * np.exp2(127.0 - byte)[:, None, :]).reshape(k, n).astype(np.float32)
    by_word = np.ascontiguousarray(scaled.reshape(k // 512, 128, 4, n).transpose(0, 1, 3, 2))
    if fmt == "e4m3":
        words = by_word.astype(ml_dtypes.float8_e4m3fn).view(np.uint8)
    else:
        c = by_word.astype(ml_dtypes.float4_e2m1fn).view(np.uint8) & 0xF
        words = (c[..., 0::2] | (c[..., 1::2] << 4)).reshape(k // 512, 128, 2 * n)
    return np.ascontiguousarray(words), np.ascontiguousarray(byte.astype(np.uint8).reshape(k // 512, 16, n))


def unpack_weight(words, scales, fmt):
    g, _, n = scales.shape
    words = np.ascontiguousarray(words).reshape(g, 128, n, -1)
    if fmt == "e4m3":
        vals = words.view(ml_dtypes.float8_e4m3fn).astype(np.float64)
    else:
        nib = np.empty((g, 128, n, 4), np.uint8)
        nib[..., 0::2] = words & 0xF
        nib[..., 1::2] = words >> 4
        vals = E2M1[nib]
    vals = vals * np.repeat(np.exp2(scales.astype(np.float64) - 127.0), 8, axis=1)[..., None]
    return vals.transpose(0, 1, 3, 2).reshape(g * 512, n)


def gelu(v):
    return 0.5 * v * (1.0 + np.tanh(np.sqrt(2.0 / np.pi) * (v + 0.044715 * v**3)))


K, H, N, T, S, T2, P = 512, 1024, 512, 4096, 1024, 2048, 1024


def setup_inputs():
    n = np.random.standard_normal
    s = mx_kscale(K)[:, None]
    u = mx_kscale(H)[:, None]
    tab_words, tab_scales = pack_weight(n((K, T)) * s, "e4m3")
    w2_words, w2_scales = pack_weight(n((K, H)) / np.sqrt(K) / s * u.T, "e2m1")
    w4_words, w4_scales = pack_weight(n((H, N)) / np.sqrt(H) / u, "e4m3")
    return {
        "tab_words": tab_words, "tab_scales": tab_scales,
        "offs": striped(np.random.permutation(T)[:S]),
        "w1": (0.45 * n((K, H)) / np.sqrt(K) / s).astype(np.float32),
        "w2_words": w2_words, "w2_scales": w2_scales,
        "w3": (n((K, H)) / np.sqrt(K) / s * u.T).astype(np.float32),
        "wgs": np.exp(0.3 * n((128, S))).astype(np.float32),
        "offs2": striped(np.random.permutation(T2)[:S]),
        "offs3": striped(np.random.permutation(T2)[:P]),
        "ref": (0.7 * n((H, P)) * u).astype(np.float32),
        "w4_words": w4_words, "w4_scales": w4_scales,
    }


def reference(tab_words, tab_scales, offs, w1, w2_words, w2_scales, w3, wgs, offs2, offs3, ref, w4_words, w4_scales):
    v = unpack_weight(tab_words, tab_scales, "e4m3")[:, unstriped(offs)]
    w2 = unpack_weight(w2_words, w2_scales, "e2m1")
    w4 = unpack_weight(w4_words, w4_scales, "e4m3")
    phase = mxq(f64(w1), 0, "e4m3").T @ v
    inph = w2.T @ v
    quad = mxq(f64(w3), 0, "e4m3").T @ v
    h = np.cos(phase) * inph + np.sin(phase) * quad
    page = np.zeros((H, T2))
    page[:, unstriped(offs2)] = np.tile(f64(wgs), (H // 128, 1)) * h
    x = page[:, unstriped(offs3)]
    z = x + f64(ref)
    return w4.T @ mxq(z, 0, "e4m3")

@@ -1,0 +1,233 @@
+import math
+from contextlib import ExitStack
+
+import concourse.mybir as mybir
+from concourse.masks import make_identity
+
+K, H, N, T, S, T2, PICKS = 512, 1024, 512, 4096, 1024, 2048, 1024
+FLOPS = 2 * 3 * K * H * S + 2 * H * N * PICKS
+
+F32 = mybir.dt.float32
+BF16 = mybir.dt.bfloat16
+I32 = mybir.dt.int32
+U32 = mybir.dt.uint32
+U16 = mybir.dt.uint16
+U8 = mybir.dt.uint8
+FP8X4 = mybir.dt.float8_e4m3fn_x4
+FP4X4 = mybir.dt.float4_e2m1fn_x4
+ACT = mybir.ActivationFunctionType
+MULT = mybir.AluOpType.mult
+ADD = mybir.AluOpType.add
+
+P = 128
+PACK = 4
+PASS = P * PACK
+PASSES = H // PASS
+BLOCKS = S // P
+
+
+def load_scale_rows(nc, plane, rows):
+    for q in range(4):
+        nc.sync.dma_start(out=plane[32 * q : 32 * q + 4].bitcast(I32), in_=rows[4 * q : 4 * q + 4].bitcast(I32))
+
+
+def interleave(copy, dst, src):
+    copy(out=dst.rearrange("p (c i) t -> p c t i", i=4), in_=src.rearrange("p t (c i) -> p c t i", i=4))
+
+
+def tile_list_burst_derotation_kernel(
+    tc, tab_words, tab_scales, offs, w1, w2_words, w2_scales, w3, wgs, offs2, offs3, ref, w4_words, w4_scales, out
+):
+    nc = tc.nc
+    with ExitStack() as ctx:
+        lists = ctx.enter_context(tc.tile_pool(name="lists", bufs=1))
+        keep = ctx.enter_context(tc.tile_pool(name="keep", bufs=1))
+        stage = ctx.enter_context(tc.tile_pool(name="stage", bufs=3))
+        half = ctx.enter_context(tc.tile_pool(name="half", bufs=2))
+        work = ctx.enter_context(tc.tile_pool(name="work", bufs=3))
+        psum = ctx.enter_context(tc.psum_pool(name="psum", bufs=2))
+
+        tab_plane = keep.tile([P, T], U8, align_bytes=64)
+        nc.vector.memset(tab_plane[:].bitcast(I32), 0)
+        w2_plane = keep.tile([P, H], U8, align_bytes=64)
+        nc.vector.memset(w2_plane[:].bitcast(I32), 0)
+        w4_plane = keep.tile([P, PASSES, N], U8, align_bytes=64)
+        nc.vector.memset(w4_plane[:].rearrange("p a n -> p (a n)").bitcast(I32), 0)
+        pages = [keep.tile([P, T2], F32, name="page%d" % t) for t in range(PACK)]
+        for page in pages:
+            nc.vector.memset(page[:], 0.0)
+        ident = keep.tile([P, P], F32)
+        make_identity(nc, ident[:])
+
+        def load_weight(w, b, c0, c1):
+            if b == 0:
+                raw = keep.tile([P, PACK, c1 - c0], F32, name="first", tag="first", bufs=4, align_bytes=64)
+            else:
+                raw = stage.tile([P, PACK, c1 - c0], F32, name="raw", tag="stage", align_bytes=64)
+            nc.sync.dma_start(out=raw[:], in_=w[:, PASS * b + c0 : PASS * b + c1].rearrange("(p i) c -> p i c", i=PACK))
+            return raw
+
+        def quantise(copy, raw, codes, plane):
+            width = raw.shape[2]
+            grouped = half.tile([P, width, PACK], BF16, name="grouped", tag="half", align_bytes=64)
+            interleave(copy, grouped[:], raw[:])
+            nc.vector.quantize_mx(out=codes.bitcast(FP8X4), scales=plane, in_=grouped[:].rearrange("p c t -> p (c t)"))
+
+        def quantise_late(raw, codes, plane, c0):
+            grouped = work.tile([P, 256, PACK], BF16, name="grouped", tag="short", bufs=2, align_bytes=64)
+            interleave(nc.scalar.copy, grouped[:], raw[:, :, c0 : c0 + 256])
+            nc.vector.quantize_mx(out=codes[:, c0 : c0 + 256].bitcast(FP8X4), scales=plane[:, c0 : c0 + 256], in_=grouped[:].rearrange("p c t -> p (c t)"))
+
+        def mx_tiles(name, width):
+            codes = keep.tile([P, width], U32, name=name + "_codes", align_bytes=64)
+            plane = keep.tile([P, width], U8, name=name + "_plane", align_bytes=64)
+            return codes, plane
+
+        idx = lists.tile([P, S // 16], U16)
+        nc.sync.dma_start(idx[:], offs)
+        idx2 = lists.tile([P, S // 16], U16)
+        nc.sync.dma_start(idx2[:], offs2)
+        raw_w1 = [load_weight(w1, 0, c0, c0 + 256) for c0 in (0, 256)]
+        w2_codes = keep.tile([P, 2 * H], U8, align_bytes=64)
+        nc.sync.dma_start(out=w2_codes[:].bitcast(I32), in_=w2_words[0].bitcast(I32))
+        load_scale_rows(nc, tab_plane, tab_scales[0])
+        tab = keep.tile([P, T], I32, tag="wide", align_bytes=64)
+        words = tab_words[0].rearrange("p t i -> p (t i)").bitcast(I32)
+        for c in range(0, T, T // 4):
+            nc.sync.dma_start(out=tab[:, c : c + T // 4], in_=words[:, c : c + T // 4])
+        raw_w3 = [load_weight(w3, 0, c0, c0 + 256) for c0 in (0, 256)]
+        load_scale_rows(nc, w2_plane, w2_scales[0])
+        clock2 = keep.tile([P, 16], F32)
+        gains = keep.tile([P, PACK, S], F32)
+        for q in range(4):
+            nc.sync.dma_start(out=gains[32 * q : 32 * q + 32], in_=wgs.rearrange("(p t) j -> p t j", t=PACK))
+        raw_w1b = load_weight(w1, 1, 0, PASS)
+        raw_w3b = load_weight(w3, 1, 0, PASS)
+        idx3 = lists.tile([P, PICKS // 16], U16)
+        nc.sync.dma_start(idx3[:], offs3)
+        ref0 = keep.tile([P, PACK, PICKS], F32)
+        nc.sync.dma_start(out=ref0[:], in_=ref[0:PASS].rearrange("(p t) m -> p t m", t=PACK))
+        w4_codes = keep.tile([P, PASSES, N], I32, align_bytes=64)
+        nc.sync.dma_start(out=w4_codes[:], in_=w4_words.rearrange("a p c i -> p a (c i)").bitcast(I32))
+        load_scale_rows(nc, w4_plane, w4_scales.rearrange("a q n -> q a n"))
+
+        w1q = [mx_tiles("w1_%d" % b, PASS) for b in range(PASSES)]
+        w3q = [mx_tiles("w3_%d" % b, PASS) for b in range(PASSES)]
+        for c, raw in enumerate(raw_w1):
+            quantise(nc.vector.tensor_copy, raw, w1q[0][0][:, 256 * c : 256 * c + 256], w1q[0][1][:, 256 * c : 256 * c + 256])
+        v_plane = keep.tile([P, S], U8, align_bytes=64)
+        nc.vector.tensor_copy(v_plane[:], tab_plane[:].indirect(idx[:]))
+        v_codes = [keep.tile([P, S // 2], U32, name="v_codes%d" % g, align_bytes=64) for g in range(2)]
+
+        def gather_words(g):
+            nc.vector.tensor_copy(v_codes[g][:], tab[:].bitcast(U32).indirect(idx[:, 32 * g : 32 * g + 32]))
+
+        gather_words(0)
+        for c, raw in enumerate(raw_w3):
+            quantise(nc.vector.tensor_copy, raw, w3q[0][0][:, 256 * c : 256 * c + 256], w3q[0][1][:, 256 * c : 256 * c + 256])
+        ref1 = keep.tile([P, PACK, PICKS], F32, tag="wide", align_bytes=64)
+        refs = [ref0, ref1]
+
+        h = [keep.tile([P, PACK, S], F32, name="h%d" % b) for b in range(PASSES)]
+
+        def by_slice(bank):
+            return bank[:].rearrange("j (p t) -> j t p", t=PACK)
+
+        def products(b, k):
+            lhsT = v_codes[k // 4][:, P * (k % 4) : P * (k % 4 + 1)].bitcast(FP8X4)
+            lhsT_scale = v_plane[:, P * k : P * (k + 1)]
+
+            def product(tag, codes, plane):
+                bank = psum.tile([P, PASS], F32, name=tag, tag=tag)
+                nc.tensor.matmul_mx(out=bank[:], lhsT=lhsT, lhsT_scale=lhsT_scale, rhs=codes, rhs_scale=plane, start=True, stop=True)
+                return bank
+
+            phase = product("phase", w1q[b][0][:].bitcast(FP8X4), w1q[b][1][:])
+            inph = product("inph", w2_codes[:, 2 * PASS * b : 2 * PASS * (b + 1)].bitcast(FP4X4), w2_plane[:, PASS * b : PASS * (b + 1)])
+            quad = product("quad", w3q[b][0][:].bitcast(FP8X4), w3q[b][1][:])
+            size = work.tile([P, PACK, P], F32, name="size", tag="short", bufs=2, align_bytes=64)
+            nc.scalar.activation(out=size[:], in_=by_slice(phase), func=ACT.Abs)
+            sin = work.tile([P, PACK, P], F32, name="sin")
+            nc.scalar.activation(out=sin[:], in_=by_slice(phase), func=ACT.Sin)
+            cos = work.tile([P, PACK, P], F32, name="cos")
+            nc.scalar.activation(out=cos[:], in_=size[:], func=ACT.Sin, scale=-1.0, bias=math.pi / 2)
+            sq = work.tile([P, PACK, P], F32, name="sq", bufs=2)
+            nc.vector.tensor_tensor(out=sq[:], in0=by_slice(quad), in1=sin[:], op=MULT)
+            ci = work.tile([P, PACK, P], F32, name="ci", bufs=2)
+            nc.vector.tensor_tensor(out=ci[:], in0=by_slice(inph), in1=cos[:], op=MULT)
+            if b == 0 and k == 0:
+                nc.gpsimd.tensor_copy(clock2[:, 8:9], ci[:, 0, 0:1])
+            hsum = psum.tile([P, PACK, P], F32, name="hsum", tag="hsum")
+            for t in range(PACK):
+                nc.tensor.matmul(out=hsum[:, t, :], lhsT=sq[:, t, :], rhs=ident[:], is_transpose=True, start=True, stop=False)
+                nc.tensor.matmul(out=hsum[:, t, :], lhsT=ci[:, t, :], rhs=ident[:], is_transpose=True, start=False, stop=True)
+            return hsum
+
+        def scatter(b, t, k0, k1):
+            js = slice(P * k0, P * k1)
+            nc.vector.tensor_tensor(pages[t][:].indirect(idx2[:, 8 * k0 : 8 * k1]), h[b][:, t, js], gains[:, t, js], MULT)
+
+        plan = {1: [(0, 0, 2)], 2: [(1, 0, 3)], 3: [(2, 0, 4)], 4: [(3, 0, 5)], 5: [(0, 2, 6), (1, 3, 6)],
+                7: [(2, 4, 8), (3, 5, 8), (0, 6, 8), (1, 6, 8)]}
+
+        def place(b, k, hsum):
+            nc.scalar.copy(out=h[b][:, :, P * k : P * (k + 1)], in_=hsum[:])
+            if b == 0 and k == 1:
+                nc.gpsimd.tensor_copy(clock2[:, k : k + 1], h[0][:, 0, P * k : P * k + 1])
+            for t, k0, k1 in plan.get(k, []):
+                scatter(b, t, k0, k1)
+
+        def fetch(b, m0, m1):
+            z = stage.tile([P, PACK, m1 - m0], F32, name="z", tag="stage", align_bytes=64)
+            for t in range(PACK):
+                nc.vector.tensor_tensor(z[:, t, :], pages[t][:].indirect(idx3[:, m0 // 16 : m1 // 16]), refs[b][:, t, m0:m1], ADD)
+            return z
+
+        pieces = [[(0, 512), (512, 1024)], [(0, 512), (512, 768), (768, 1024)]]
+        zq = [mx_tiles("z%d" % b, PICKS) for b in range(PASSES)]
+        z0 = []
+        sums = {}
+        for u in range(PASSES * BLOCKS + 1):
+            if u < PASSES * BLOCKS:
+                sums[u] = products(u // BLOCKS, u % BLOCKS)
+            if u == 1:
+                gather_words(1)
+                nc.sync.dma_start(out=ref1[:], in_=ref[PASS : 2 * PASS].rearrange("(p t) m -> p t m", t=PACK))
+            if u in (3, 4):
+                quantise_late(raw_w1b, w1q[1][0], w1q[1][1], 256 * (u - 3))
+            if u in (5, 6):
+                quantise_late(raw_w3b, w3q[1][0], w3q[1][1], 256 * (u - 5))
+            done = u - 1
+            if done % BLOCKS == 5 or done < 0:
+                continue
+            if done % BLOCKS == 6:
+                place(done // BLOCKS, 5, sums[done - 1])
+            place(done // BLOCKS, done % BLOCKS, sums[done])
+            if done == BLOCKS - 1:
+                z0 = [fetch(0, m0, m1) for m0, m1 in pieces[0]]
+
+        for (m0, m1), z in zip(pieces[0], z0):
+            for c0 in (0, 256):
+                quantise_late(z, zq[0][0][:, m0:m1], zq[0][1][:, m0:m1], c0)
+        z1 = [fetch(1, m0, m1) for m0, m1 in pieces[1]]
+        tags = ["phase", "inph", "quad", "hsum"]
+        for (m0, m1), z in zip(pieces[1], z1):
+            quantise(nc.scalar.copy, z, zq[1][0][:, m0:m1], zq[1][1][:, m0:m1])
+            result = stage.tile([P, N // P, m1 - m0], F32, name="result", tag="stage", align_bytes=64)
+            for n in range(N // P):
+                acc = psum.tile([P, m1 - m0], F32, name="acc", tag=tags[n])
+                for b in range(PASSES):
+                    nc.tensor.matmul_mx(
+                        out=acc[:],
+                        lhsT=w4_codes[:, b, P * n : P * (n + 1)].bitcast(FP8X4),
+                        lhsT_scale=w4_plane[:, b, P * n : P * (n + 1)],
+                        rhs=zq[b][0][:, m0:m1].bitcast(FP8X4),
+                        rhs_scale=zq[b][1][:, m0:m1],
+                        start=(b == 0),
+                        stop=(b == PASSES - 1),
+                    )
+                if m0 > 0 and n % 2 == 1:
+                    nc.vector.tensor_copy(out=result[:, n, :], in_=acc[:])
+                else:
+                    nc.scalar.copy(out=result[:, n, :], in_=acc[:])
+            nc.sync.dma_start(out=out.rearrange("(n p) m -> p n m", p=P)[:, :, m0:m1], in_=result[:])

@@ -23,16 +23,14 @@ P = 128
 PACK = 4
 PASS = P * PACK
 PASSES = H // PASS
-BLOCKS = S // P
+HALF = S // 2
+PIECE = 256
+PIECES = PICKS // PIECE
 
 
 def load_scale_rows(nc, plane, rows):
     for q in range(4):
         nc.sync.dma_start(out=plane[32 * q : 32 * q + 4].bitcast(I32), in_=rows[4 * q : 4 * q + 4].bitcast(I32))
-
-
-def interleave(copy, dst, src):
-    copy(out=dst.rearrange("p (c i) t -> p c t i", i=4), in_=src.rearrange("p t (c i) -> p c t i", i=4))
 
 
 def tile_list_burst_derotation_kernel(
@@ -42,192 +40,209 @@ def tile_list_burst_derotation_kernel(
     with ExitStack() as ctx:
         lists = ctx.enter_context(tc.tile_pool(name="lists", bufs=1))
         keep = ctx.enter_context(tc.tile_pool(name="keep", bufs=1))
-        stage = ctx.enter_context(tc.tile_pool(name="stage", bufs=3))
-        half = ctx.enter_context(tc.tile_pool(name="half", bufs=2))
-        work = ctx.enter_context(tc.tile_pool(name="work", bufs=3))
-        psum = ctx.enter_context(tc.psum_pool(name="psum", bufs=2))
+        work = ctx.enter_context(tc.tile_pool(name="work", bufs=2))
+        psum = ctx.enter_context(tc.psum_pool(name="psum", bufs=1))
 
-        tab_plane = keep.tile([P, T], U8, align_bytes=64)
+        tab_plane = keep.tile([P, T], U8, tag="page3", align_bytes=64)
         nc.vector.memset(tab_plane[:].bitcast(I32), 0)
         w2_plane = keep.tile([P, H], U8, align_bytes=64)
         nc.vector.memset(w2_plane[:].bitcast(I32), 0)
         w4_plane = keep.tile([P, PASSES, N], U8, align_bytes=64)
         nc.vector.memset(w4_plane[:].rearrange("p a n -> p (a n)").bitcast(I32), 0)
-        pages = [keep.tile([P, T2], F32, name="page%d" % t) for t in range(PACK)]
-        for page in pages:
-            nc.vector.memset(page[:], 0.0)
+        page0 = keep.tile([P, T2], F32, align_bytes=64)
+        nc.vector.memset(page0[:], 0.0)
         ident = keep.tile([P, P], F32)
         make_identity(nc, ident[:])
 
-        def load_weight(w, b, c0, c1):
-            if b == 0:
-                raw = keep.tile([P, PACK, c1 - c0], F32, name="first", tag="first", bufs=4, align_bytes=64)
-            else:
-                raw = stage.tile([P, PACK, c1 - c0], F32, name="raw", tag="stage", align_bytes=64)
-            nc.sync.dma_start(out=raw[:], in_=w[:, PASS * b + c0 : PASS * b + c1].rearrange("(p i) c -> p i c", i=PACK))
-            return raw
+        def load_weights(s0, s1, tag):
+            raw = keep.tile([P, 2, PACK, P * (s1 - s0)], F32, name="raw", tag=tag, align_bytes=64)
+            for n, w in enumerate((w1, w3)):
+                nc.sync.dma_start(out=raw[:, n], in_=w[:, P * s0 : P * s1].rearrange("(p i) c -> p i c", i=PACK))
+            return [raw[:, :, :, P * s : P * (s + 1)] for s in range(s1 - s0)]
 
-        def quantise(copy, raw, codes, plane):
-            width = raw.shape[2]
-            grouped = half.tile([P, width, PACK], BF16, name="grouped", tag="half", align_bytes=64)
-            interleave(copy, grouped[:], raw[:])
-            nc.vector.quantize_mx(out=codes.bitcast(FP8X4), scales=plane, in_=grouped[:].rearrange("p c t -> p (c t)"))
-
-        def quantise_late(raw, codes, plane, c0):
-            grouped = work.tile([P, 256, PACK], BF16, name="grouped", tag="short", bufs=2, align_bytes=64)
-            interleave(nc.scalar.copy, grouped[:], raw[:, :, c0 : c0 + 256])
-            nc.vector.quantize_mx(out=codes[:, c0 : c0 + 256].bitcast(FP8X4), scales=plane[:, c0 : c0 + 256], in_=grouped[:].rearrange("p c t -> p (c t)"))
-
-        def mx_tiles(name, width):
-            codes = keep.tile([P, width], U32, name=name + "_codes", align_bytes=64)
-            plane = keep.tile([P, width], U8, name=name + "_plane", align_bytes=64)
-            return codes, plane
+        def load_ref(b, tag):
+            rows = keep.tile([P, PACK, PICKS], F32, name="rows", tag=tag, align_bytes=64)
+            nc.sync.dma_start(out=rows[:], in_=ref[PASS * b : PASS * (b + 1)].rearrange("(s p) m -> p s m", p=P))
+            return rows
 
         idx = lists.tile([P, S // 16], U16)
         nc.sync.dma_start(idx[:], offs)
-        idx2 = lists.tile([P, S // 16], U16)
-        nc.sync.dma_start(idx2[:], offs2)
-        raw_w1 = [load_weight(w1, 0, c0, c0 + 256) for c0 in (0, 256)]
+        raws = load_weights(0, 1, "page1")
         w2_codes = keep.tile([P, 2 * H], U8, align_bytes=64)
         nc.sync.dma_start(out=w2_codes[:].bitcast(I32), in_=w2_words[0].bitcast(I32))
         load_scale_rows(nc, tab_plane, tab_scales[0])
         tab = keep.tile([P, T], I32, tag="wide", align_bytes=64)
-        words = tab_words[0].rearrange("p t i -> p (t i)").bitcast(I32)
-        for c in range(0, T, T // 4):
-            nc.sync.dma_start(out=tab[:, c : c + T // 4], in_=words[:, c : c + T // 4])
-        raw_w3 = [load_weight(w3, 0, c0, c0 + 256) for c0 in (0, 256)]
+        nc.sync.dma_start(out=tab[:], in_=tab_words[0].rearrange("p t i -> p (t i)").bitcast(I32))
         load_scale_rows(nc, w2_plane, w2_scales[0])
-        clock2 = keep.tile([P, 16], F32)
-        gains = keep.tile([P, PACK, S], F32)
-        for q in range(4):
-            nc.sync.dma_start(out=gains[32 * q : 32 * q + 32], in_=wgs.rearrange("(p t) j -> p t j", t=PACK))
-        raw_w1b = load_weight(w1, 1, 0, PASS)
-        raw_w3b = load_weight(w3, 1, 0, PASS)
+        idx2 = lists.tile([P, S // 16], U16)
+        nc.sync.dma_start(idx2[:], offs2)
+        gains = keep.tile([P, S], F32, tag="gains")
+        nc.sync.dma_start(out=gains[:], in_=wgs)
+        raws.extend(load_weights(1, 2, "page2"))
+        raws.extend(load_weights(2, 4, "raw2"))
         idx3 = lists.tile([P, PICKS // 16], U16)
         nc.sync.dma_start(idx3[:], offs3)
-        ref0 = keep.tile([P, PACK, PICKS], F32)
-        nc.sync.dma_start(out=ref0[:], in_=ref[0:PASS].rearrange("(p t) m -> p t m", t=PACK))
+        raws.extend(load_weights(4, 8, "raw4"))
+        refs = [load_ref(0, "ref0")]
         w4_codes = keep.tile([P, PASSES, N], I32, align_bytes=64)
         nc.sync.dma_start(out=w4_codes[:], in_=w4_words.rearrange("a p c i -> p a (c i)").bitcast(I32))
         load_scale_rows(nc, w4_plane, w4_scales.rearrange("a q n -> q a n"))
 
-        w1q = [mx_tiles("w1_%d" % b, PASS) for b in range(PASSES)]
-        w3q = [mx_tiles("w3_%d" % b, PASS) for b in range(PASSES)]
-        for c, raw in enumerate(raw_w1):
-            quantise(nc.vector.tensor_copy, raw, w1q[0][0][:, 256 * c : 256 * c + 256], w1q[0][1][:, 256 * c : 256 * c + 256])
+        def quantise(grouped, name):
+            width = grouped.shape[1] // PACK
+            codes = keep.tile([P, width], U32, name=name + "_codes", align_bytes=64)
+            plane = keep.tile([P, width], U8, name=name + "_plane", align_bytes=64)
+            nc.vector.quantize_mx(out=codes[:].bitcast(FP8X4), scales=plane[:], in_=grouped)
+            return codes, plane
+
+        def quantise_weights(s, copy):
+            grouped = work.tile([P, 2 * P * PACK], BF16, name="grouped", tag="short", bufs=3, align_bytes=64)
+            copy(
+                out=grouped[:].rearrange("p (n c e i) -> p n c i e", n=2, e=4, i=PACK),
+                in_=raws[s].rearrange("p n i (c e) -> p n c i e", e=4),
+            )
+            return quantise(grouped[:], "w13_%d" % s)
+
+        wq = [quantise_weights(0, nc.vector.tensor_copy)]
         v_plane = keep.tile([P, S], U8, align_bytes=64)
         nc.vector.tensor_copy(v_plane[:], tab_plane[:].indirect(idx[:]))
-        v_codes = [keep.tile([P, S // 2], U32, name="v_codes%d" % g, align_bytes=64) for g in range(2)]
+        v_codes = []
+        for g in range(2):
+            words = keep.tile([P, HALF], U32, name="v_codes%d" % g, align_bytes=64)
+            nc.vector.tensor_copy(words[:], tab[:].bitcast(U32).indirect(idx[:, 32 * g : 32 * g + 32]))
+            v_codes.append(words)
+        refs.append(load_ref(1, "wide"))
+        pages = [page0]
 
-        def gather_words(g):
-            nc.vector.tensor_copy(v_codes[g][:], tab[:].bitcast(U32).indirect(idx[:, 32 * g : 32 * g + 32]))
+        def clear_page(n):
+            page = keep.tile([P, T2], F32, name="page", tag="page%d" % n, align_bytes=64)
+            nc.gpsimd.memset(page[:], 0.0)
+            pages.append(page)
 
-        gather_words(0)
-        for c, raw in enumerate(raw_w3):
-            quantise(nc.vector.tensor_copy, raw, w3q[0][0][:, 256 * c : 256 * c + 256], w3q[0][1][:, 256 * c : 256 * c + 256])
-        ref1 = keep.tile([P, PACK, PICKS], F32, tag="wide", align_bytes=64)
-        refs = [ref0, ref1]
+        clear_page(1)
 
-        h = [keep.tile([P, PACK, S], F32, name="h%d" % b) for b in range(PASSES)]
+        def first_product(g, tag, codes, plane):
+            bank = psum.tile([P, 4, P], F32, name=tag, tag=tag)
+            for k in range(4):
+                nc.tensor.matmul_mx(
+                    out=bank[:, k, :],
+                    lhsT=v_codes[g][:, P * k : P * (k + 1)].bitcast(FP8X4),
+                    lhsT_scale=v_plane[:, HALF * g + P * k : HALF * g + P * (k + 1)],
+                    rhs=codes,
+                    rhs_scale=plane,
+                    start=True,
+                    stop=True,
+                )
+            return bank
 
-        def by_slice(bank):
-            return bank[:].rearrange("j (p t) -> j t p", t=PACK)
-
-        def products(b, k):
-            lhsT = v_codes[k // 4][:, P * (k % 4) : P * (k % 4 + 1)].bitcast(FP8X4)
-            lhsT_scale = v_plane[:, P * k : P * (k + 1)]
-
-            def product(tag, codes, plane):
-                bank = psum.tile([P, PASS], F32, name=tag, tag=tag)
-                nc.tensor.matmul_mx(out=bank[:], lhsT=lhsT, lhsT_scale=lhsT_scale, rhs=codes, rhs_scale=plane, start=True, stop=True)
-                return bank
-
-            phase = product("phase", w1q[b][0][:].bitcast(FP8X4), w1q[b][1][:])
-            inph = product("inph", w2_codes[:, 2 * PASS * b : 2 * PASS * (b + 1)].bitcast(FP4X4), w2_plane[:, PASS * b : PASS * (b + 1)])
-            quad = product("quad", w3q[b][0][:].bitcast(FP8X4), w3q[b][1][:])
-            size = work.tile([P, PACK, P], F32, name="size", tag="short", bufs=2, align_bytes=64)
-            nc.scalar.activation(out=size[:], in_=by_slice(phase), func=ACT.Abs)
-            sin = work.tile([P, PACK, P], F32, name="sin")
-            nc.scalar.activation(out=sin[:], in_=by_slice(phase), func=ACT.Sin)
-            cos = work.tile([P, PACK, P], F32, name="cos")
+        def derotate(s, g):
+            codes, plane = wq[s]
+            phase = first_product(g, "phase", codes[:, 0:P].bitcast(FP8X4), plane[:, 0:P])
+            quad = first_product(g, "quad", codes[:, P : 2 * P].bitcast(FP8X4), plane[:, P : 2 * P])
+            inph = first_product(
+                g, "inph", w2_codes[:, 2 * P * s : 2 * P * (s + 1)].bitcast(FP4X4), w2_plane[:, P * s : P * (s + 1)]
+            )
+            sin = work.tile([P, 4, P], F32, name="sin")
+            nc.scalar.activation(out=sin[:], in_=phase[:], func=ACT.Sin)
+            size = work.tile([P, 4, P], F32, name="size", tag="short", bufs=3, align_bytes=64)
+            nc.scalar.activation(out=size[:], in_=phase[:], func=ACT.Abs)
+            cos = work.tile([P, 4, P], F32, name="cos")
             nc.scalar.activation(out=cos[:], in_=size[:], func=ACT.Sin, scale=-1.0, bias=math.pi / 2)
-            sq = work.tile([P, PACK, P], F32, name="sq", bufs=2)
-            nc.vector.tensor_tensor(out=sq[:], in0=by_slice(quad), in1=sin[:], op=MULT)
-            ci = work.tile([P, PACK, P], F32, name="ci", bufs=2)
-            nc.vector.tensor_tensor(out=ci[:], in0=by_slice(inph), in1=cos[:], op=MULT)
-            if b == 0 and k == 0:
-                nc.gpsimd.tensor_copy(clock2[:, 8:9], ci[:, 0, 0:1])
-            hsum = psum.tile([P, PACK, P], F32, name="hsum", tag="hsum")
-            for t in range(PACK):
-                nc.tensor.matmul(out=hsum[:, t, :], lhsT=sq[:, t, :], rhs=ident[:], is_transpose=True, start=True, stop=False)
-                nc.tensor.matmul(out=hsum[:, t, :], lhsT=ci[:, t, :], rhs=ident[:], is_transpose=True, start=False, stop=True)
+            sq = work.tile([P, 4, P], F32, name="sq")
+            nc.vector.tensor_tensor(out=sq[:], in0=quad[:], in1=sin[:], op=MULT)
+            ci = work.tile([P, 4, P], F32, name="ci")
+            nc.vector.tensor_tensor(out=ci[:], in0=inph[:], in1=cos[:], op=MULT)
+            hsum = psum.tile([P, 4, P], F32, name="hsum", tag="hsum")
+            for k in range(4):
+                turn(hsum[:, k, :], sq[:, k, :], k == 0, False)
+            for k in range(4):
+                turn(hsum[:, k, :], ci[:, k, :], False, k == 3)
             return hsum
 
-        def scatter(b, t, k0, k1):
-            js = slice(P * k0, P * k1)
-            nc.vector.tensor_tensor(pages[t][:].indirect(idx2[:, 8 * k0 : 8 * k1]), h[b][:, t, js], gains[:, t, js], MULT)
+        def turn(dst, src, start, stop):
+            nc.tensor.matmul(out=dst, lhsT=src, rhs=ident[:], is_transpose=True, start=start, stop=stop)
 
-        plan = {1: [(0, 0, 2)], 2: [(1, 0, 3)], 3: [(2, 0, 4)], 4: [(3, 0, 5)], 5: [(0, 2, 6), (1, 3, 6)],
-                7: [(2, 4, 8), (3, 5, 8), (0, 6, 8), (1, 6, 8)]}
+        def place(s, g, hsum):
+            h = work.tile([P, HALF], F32, name="h", bufs=3)
+            nc.scalar.copy(out=h[:], in_=hsum[:].rearrange("p k j -> p (k j)"))
+            page = pages[s % PACK]
+            nc.vector.tensor_tensor(page[:].indirect(idx2[:, 32 * g : 32 * g + 32]), h[:], gains[:, HALF * g : HALF * (g + 1)], MULT)
 
-        def place(b, k, hsum):
-            nc.scalar.copy(out=h[b][:, :, P * k : P * (k + 1)], in_=hsum[:])
-            if b == 0 and k == 1:
-                nc.gpsimd.tensor_copy(clock2[:, k : k + 1], h[0][:, 0, P * k : P * k + 1])
-            for t, k0, k1 in plan.get(k, []):
-                scatter(b, t, k0, k1)
+        def fetch(dst, t, m0, m1):
+            nc.vector.tensor_copy(dst, pages[t][:].indirect(idx3[:, m0 // 16 : m1 // 16]))
 
-        def fetch(b, m0, m1):
-            z = stage.tile([P, PACK, m1 - m0], F32, name="z", tag="stage", align_bytes=64)
-            for t in range(PACK):
-                nc.vector.tensor_tensor(z[:, t, :], pages[t][:].indirect(idx3[:, m0 // 16 : m1 // 16]), refs[b][:, t, m0:m1], ADD)
-            return z
+        def quantise_z(b, c, picked, copies, banks):
+            words = psum.tile([P, 2, 2, P], F32, name="words", tag="words", bufs=2)
+            for k in range(2):
+                zsum = psum.tile([P, PACK, P], F32, name="zsum", tag=banks[k])
+                m0 = PIECE * c + P * k
+                for t in range(PACK):
+                    turn(zsum[:, t, :], refs[b][:, t, m0 : m0 + P], t == 0, False)
+                for t in range(PACK):
+                    turn(zsum[:, t, :], picked[:, t, P * k : P * (k + 1)], False, t == PACK - 1)
+                rounded = work.tile([P, 2, P, 2], BF16, name="rounded", tag="short", bufs=3, align_bytes=64)
+                copies[k](out=rounded[:], in_=zsum[:].rearrange("m t (q u e) -> m u (t q) e", u=2, e=2))
+                pairs = rounded[:].rearrange("m u q e -> m (u q e)").bitcast(F32)
+                for u in range(2):
+                    nc.tensor.transpose(words[:, k, u, :], pairs[:, P * u : P * (u + 1)], ident[:])
+            grouped = work.tile([P, PIECE * PACK], BF16, name="zgrouped", align_bytes=64)
+            nc.scalar.copy(
+                out=grouped[:].bitcast(F32).rearrange("q (k m u) -> q k m u", k=2, u=2),
+                in_=words[:].rearrange("q k u m -> q k m u"),
+            )
+            return quantise(grouped[:], "z%d_%d" % (b, c))
 
-        pieces = [[(0, 512), (512, 1024)], [(0, 512), (512, 768), (768, 1024)]]
-        zq = [mx_tiles("z%d" % b, PICKS) for b in range(PASSES)]
+        units = [(s, g) for s in range(H // P) for g in range(2)]
         z0 = []
-        sums = {}
-        for u in range(PASSES * BLOCKS + 1):
-            if u < PASSES * BLOCKS:
-                sums[u] = products(u // BLOCKS, u % BLOCKS)
-            if u == 1:
-                gather_words(1)
-                nc.sync.dma_start(out=ref1[:], in_=ref[PASS : 2 * PASS].rearrange("(p t) m -> p t m", t=PACK))
-            if u in (3, 4):
-                quantise_late(raw_w1b, w1q[1][0], w1q[1][1], 256 * (u - 3))
-            if u in (5, 6):
-                quantise_late(raw_w3b, w3q[1][0], w3q[1][1], 256 * (u - 5))
-            done = u - 1
-            if done % BLOCKS == 5 or done < 0:
-                continue
-            if done % BLOCKS == 6:
-                place(done // BLOCKS, 5, sums[done - 1])
-            place(done // BLOCKS, done % BLOCKS, sums[done])
-            if done == BLOCKS - 1:
-                z0 = [fetch(0, m0, m1) for m0, m1 in pieces[0]]
+        picked0 = keep.tile([P, PACK, PICKS], F32)
+        hsum = derotate(0, 0)
+        for u, (s, g) in enumerate(units):
+            following = derotate(*units[u + 1]) if u + 1 < len(units) else None
+            place(s, g, hsum)
+            hsum = following
+            if g == 0 and s + 1 < H // P:
+                wq.append(quantise_weights(s + 1, nc.scalar.copy))
+            if u in (0, 2):
+                clear_page(2 + u // 2)
+            if u == 2 * PACK - 1:
+                for t in range(PACK):
+                    fetch(picked0[:, t, :], t, 0, PICKS)
+            if u in (9, 11, 13, 14):
+                c = len(z0)
+                z0.append(quantise_z(0, c, picked0[:, :, PIECE * c : PIECE * (c + 1)], [nc.scalar.copy, nc.scalar.copy], ("zsum0", "zsum1")))
 
-        for (m0, m1), z in zip(pieces[0], z0):
-            for c0 in (0, 256):
-                quantise_late(z, zq[0][0][:, m0:m1], zq[0][1][:, m0:m1], c0)
-        z1 = [fetch(1, m0, m1) for m0, m1 in pieces[1]]
-        tags = ["phase", "inph", "quad", "hsum"]
-        for (m0, m1), z in zip(pieces[1], z1):
-            quantise(nc.scalar.copy, z, zq[1][0][:, m0:m1], zq[1][1][:, m0:m1])
-            result = stage.tile([P, N // P, m1 - m0], F32, name="result", tag="stage", align_bytes=64)
-            for n in range(N // P):
-                acc = psum.tile([P, m1 - m0], F32, name="acc", tag=tags[n])
-                for b in range(PASSES):
-                    nc.tensor.matmul_mx(
-                        out=acc[:],
-                        lhsT=w4_codes[:, b, P * n : P * (n + 1)].bitcast(FP8X4),
-                        lhsT_scale=w4_plane[:, b, P * n : P * (n + 1)],
-                        rhs=zq[b][0][:, m0:m1].bitcast(FP8X4),
-                        rhs_scale=zq[b][1][:, m0:m1],
-                        start=(b == 0),
-                        stop=(b == PASSES - 1),
-                    )
-                if m0 > 0 and n % 2 == 1:
-                    nc.vector.tensor_copy(out=result[:, n, :], in_=acc[:])
-                else:
-                    nc.scalar.copy(out=result[:, n, :], in_=acc[:])
-            nc.sync.dma_start(out=out.rearrange("(n p) m -> p n m", p=P)[:, :, m0:m1], in_=result[:])
+        picked1 = keep.tile([P, PIECES, PACK, PIECE], F32, tag="gains")
+        for c in range(PIECES):
+            for t in range(PACK):
+                fetch(picked1[:, c, t, :], t, PIECE * c, PIECE * (c + 1))
+        tags = [("phase", "quad"), ("inph", "hsum")]
+        sum_banks = [("zsum0", "zsum1")] + tags + [("zsum0", "zsum1")]
+
+        def second_pass(c):
+            other = nc.vector.tensor_copy if c == PIECES - 1 else nc.scalar.copy
+            return quantise_z(1, c, picked1[:, c], [nc.scalar.copy, other], sum_banks[c])
+
+        z1 = [second_pass(0)]
+        for c in range(PIECES):
+            last = c == PIECES - 1
+            if not last:
+                z1.append(second_pass(c + 1))
+            zq = [z0[c], z1[c]]
+            result = work.tile([P, N // P, PIECE], F32, name="result", bufs=3)
+            for pair in range(2):
+                acc = psum.tile([P, 2, PIECE], F32, name="acc", tag=tags[c % 2][pair])
+                for i in range(2):
+                    n = 2 * pair + i
+                    for b in range(PASSES):
+                        nc.tensor.matmul_mx(
+                            out=acc[:, i, :],
+                            lhsT=w4_codes[:, b, P * n : P * (n + 1)].bitcast(FP8X4),
+                            lhsT_scale=w4_plane[:, b, P * n : P * (n + 1)],
+                            rhs=zq[b][0][:].bitcast(FP8X4),
+                            rhs_scale=zq[b][1][:],
+                            start=(b == 0),
+                            stop=(b == PASSES - 1),
+                        )
+                copy = nc.vector.tensor_copy if c >= 2 and pair == 0 else nc.scalar.copy
+                copy(out=result[:, 2 * pair : 2 * pair + 2, :], in_=acc[:])
+            nc.sync.dma_start(out=out.rearrange("(n p) m -> p n m", p=P)[:, :, PIECE * c : PIECE * (c + 1)], in_=result[:])

@@ -185,7 +185,7 @@ def tile_list_burst_derotation_kernel(
                 pairs = rounded[:].rearrange("m u q e -> m (u q e)").bitcast(F32)
                 for u in range(2):
                     nc.tensor.transpose(words[:, k, u, :], pairs[:, P * u : P * (u + 1)], ident[:])
-            grouped = work.tile([P, PIECE * PACK], BF16, name="zgrouped", align_bytes=64)
+            grouped = work.tile([P, PIECE * PACK], BF16, name="zgrouped", bufs=PIECES, align_bytes=64)
             nc.scalar.copy(
                 out=grouped[:].bitcast(F32).rearrange("q (k m u) -> q k m u", k=2, u=2),
                 in_=words[:].rearrange("q k u m -> q k m u"),
@@ -196,12 +196,13 @@ def tile_list_burst_derotation_kernel(
         z0 = []
         picked0 = keep.tile([P, PACK, PICKS], F32)
         hsum = derotate(0, 0)
+        wq.append(quantise_weights(1, nc.vector.tensor_copy))
         for u, (s, g) in enumerate(units):
             following = derotate(*units[u + 1]) if u + 1 < len(units) else None
             place(s, g, hsum)
             hsum = following
-            if g == 0 and s + 1 < H // P:
-                wq.append(quantise_weights(s + 1, nc.scalar.copy))
+            if g == 0 and s + 2 < H // P:
+                wq.append(quantise_weights(s + 2, nc.scalar.copy))
             if u in (0, 2):
                 clear_page(2 + u // 2)
             if u == 2 * PACK - 1:
@@ -222,13 +223,10 @@ def tile_list_burst_derotation_kernel(
             other = nc.vector.tensor_copy if c == PIECES - 1 else nc.scalar.copy
             return quantise_z(1, c, picked1[:, c], [nc.scalar.copy, other], sum_banks[c])
 
-        z1 = [second_pass(0)]
+        z1 = [second_pass(c) for c in range(PIECES)]
         for c in range(PIECES):
-            last = c == PIECES - 1
-            if not last:
-                z1.append(second_pass(c + 1))
             zq = [z0[c], z1[c]]
-            result = work.tile([P, N // P, PIECE], F32, name="result", bufs=3)
+            result = work.tile([P, N // P, PIECE], F32, name="result", bufs=PIECES)
             for pair in range(2):
                 acc = psum.tile([P, 2, PIECE], F32, name="acc", tag=tags[c % 2][pair])
                 for i in range(2):
@@ -243,6 +241,6 @@ def tile_list_burst_derotation_kernel(
                             start=(b == 0),
                             stop=(b == PASSES - 1),
                         )
-                copy = nc.vector.tensor_copy if c >= 2 and pair == 0 else nc.scalar.copy
+                copy = nc.vector.tensor_copy if pair == 0 else nc.scalar.copy
                 copy(out=result[:, 2 * pair : 2 * pair + 2, :], in_=acc[:])
             nc.sync.dma_start(out=out.rearrange("(n p) m -> p n m", p=P)[:, :, PIECE * c : PIECE * (c + 1)], in_=result[:])

@@ -23,14 +23,16 @@ P = 128
 PACK = 4
 PASS = P * PACK
 PASSES = H // PASS
+SLICES = H // P
 HALF = S // 2
 PIECE = 256
 PIECES = PICKS // PIECE
+LAG = 3
 
 
-def load_scale_rows(nc, plane, rows):
+def load_scale_rows(queue, plane, rows):
     for q in range(4):
-        nc.sync.dma_start(out=plane[32 * q : 32 * q + 4].bitcast(I32), in_=rows[4 * q : 4 * q + 4].bitcast(I32))
+        queue.dma_start(out=plane[32 * q : 32 * q + 4].bitcast(I32), in_=rows[4 * q : 4 * q + 4].bitcast(I32))
 
 
 def tile_list_burst_derotation_kernel(
@@ -43,86 +45,114 @@ def tile_list_burst_derotation_kernel(
         work = ctx.enter_context(tc.tile_pool(name="work", bufs=2))
         psum = ctx.enter_context(tc.psum_pool(name="psum", bufs=1))
 
-        tab_plane = keep.tile([P, T], U8, tag="page3", align_bytes=64)
+        tab_plane = keep.tile([P, T], U8, align_bytes=64)
         nc.vector.memset(tab_plane[:].bitcast(I32), 0)
-        w2_plane = keep.tile([P, H], U8, align_bytes=64)
-        nc.vector.memset(w2_plane[:].bitcast(I32), 0)
+        w2_rows = keep.tile([P, H], U8, align_bytes=64)
+        nc.vector.memset(w2_rows[:].bitcast(I32), 0)
         w4_plane = keep.tile([P, PASSES, N], U8, align_bytes=64)
         nc.vector.memset(w4_plane[:].rearrange("p a n -> p (a n)").bitcast(I32), 0)
-        page0 = keep.tile([P, T2], F32, align_bytes=64)
-        nc.vector.memset(page0[:], 0.0)
+        pages = []
+
+        def clear_page(t):
+            page = keep.tile([P, T2], F32, name="page%d" % t, align_bytes=64)
+            nc.vector.memset(page[:], 0.0)
+            pages.append(page)
+
         ident = keep.tile([P, P], F32)
         make_identity(nc, ident[:])
 
-        def load_weights(s0, s1, tag):
-            raw = keep.tile([P, 2, PACK, P * (s1 - s0)], F32, name="raw", tag=tag, align_bytes=64)
-            for n, w in enumerate((w1, w3)):
-                nc.sync.dma_start(out=raw[:, n], in_=w[:, P * s0 : P * s1].rearrange("(p i) c -> p i c", i=PACK))
-            return [raw[:, :, :, P * s : P * (s + 1)] for s in range(s1 - s0)]
+        def load_weight(w, b, tag):
+            raw = keep.tile([P, PACK, PASS], F32, name="raw", tag=tag, align_bytes=64)
+            nc.sync.dma_start(out=raw[:], in_=w[:, PASS * b : PASS * (b + 1)].rearrange("(p i) c -> p i c", i=PACK))
+            return raw[:]
 
-        def load_ref(b, tag):
-            rows = keep.tile([P, PACK, PICKS], F32, name="rows", tag=tag, align_bytes=64)
-            nc.sync.dma_start(out=rows[:], in_=ref[PASS * b : PASS * (b + 1)].rearrange("(s p) m -> p s m", p=P))
-            return rows
+        def load_gains(t0, t1):
+            rows = keep.tile([P, t1 - t0, S], F32, name="gains%d" % t0)
+            for q in range(4):
+                nc.sync.dma_start(out=rows[32 * q : 32 * (q + 1)], in_=wgs.rearrange("(q t) j -> q t j", t=PACK)[:, t0:t1])
+            return [rows[:, t, :] for t in range(t1 - t0)]
+
+        def load_ref(b, t0, tag):
+            rows = keep.tile([P, 2, PICKS], F32, name="rows", tag=tag, align_bytes=64)
+            nc.sync.dma_start(
+                out=rows[:], in_=ref[PASS * b : PASS * (b + 1)].rearrange("(p t) m -> p t m", t=PACK)[:, t0 : t0 + 2]
+            )
+            return [rows[:, 0, :], rows[:, 1, :]]
 
         idx = lists.tile([P, S // 16], U16)
         nc.sync.dma_start(idx[:], offs)
-        raws = load_weights(0, 1, "page1")
-        w2_codes = keep.tile([P, 2 * H], U8, align_bytes=64)
-        nc.sync.dma_start(out=w2_codes[:].bitcast(I32), in_=w2_words[0].bitcast(I32))
-        load_scale_rows(nc, tab_plane, tab_scales[0])
+        raw1 = [load_weight(w1, 0, "raw1a")]
+        w2_raw = keep.tile([P, 2 * H], U8, align_bytes=64)
+        nc.sync.dma_start(out=w2_raw[:].bitcast(I32), in_=w2_words[0].bitcast(I32))
+        load_scale_rows(nc.sync, tab_plane, tab_scales[0])
         tab = keep.tile([P, T], I32, tag="wide", align_bytes=64)
         nc.sync.dma_start(out=tab[:], in_=tab_words[0].rearrange("p t i -> p (t i)").bitcast(I32))
-        load_scale_rows(nc, w2_plane, w2_scales[0])
+        load_scale_rows(nc.sync, w2_rows, w2_scales[0])
+        raw3 = [load_weight(w3, 0, "raw3a")]
         idx2 = lists.tile([P, S // 16], U16)
         nc.sync.dma_start(idx2[:], offs2)
-        gains = keep.tile([P, S], F32, tag="gains")
-        nc.sync.dma_start(out=gains[:], in_=wgs)
-        raws.extend(load_weights(1, 2, "page2"))
-        raws.extend(load_weights(2, 4, "raw2"))
+        gains = load_gains(0, 1)
         idx3 = lists.tile([P, PICKS // 16], U16)
         nc.sync.dma_start(idx3[:], offs3)
-        raws.extend(load_weights(4, 8, "raw4"))
-        refs = [load_ref(0, "ref0")]
+        gains.extend(load_gains(1, PACK))
+        refs = load_ref(0, 0, "ref0") + load_ref(0, 2, "ref1")
+        later = keep.tile([P, 2, PACK, PASS], F32, tag="later", align_bytes=64)
+        for n, (w, raw) in enumerate(((w1, raw1), (w3, raw3))):
+            nc.sync.dma_start(out=later[:, n], in_=w[:, PASS:H].rearrange("(p i) c -> p i c", i=PACK))
+            raw.append(later[:, n])
         w4_codes = keep.tile([P, PASSES, N], I32, align_bytes=64)
         nc.sync.dma_start(out=w4_codes[:], in_=w4_words.rearrange("a p c i -> p a (c i)").bitcast(I32))
-        load_scale_rows(nc, w4_plane, w4_scales.rearrange("a q n -> q a n"))
+        load_scale_rows(nc.sync, w4_plane, w4_scales.rearrange("a q n -> q a n"))
 
-        def quantise(grouped, name):
-            width = grouped.shape[1] // PACK
-            codes = keep.tile([P, width], U32, name=name + "_codes", align_bytes=64)
-            plane = keep.tile([P, width], U8, name=name + "_plane", align_bytes=64)
-            nc.vector.quantize_mx(out=codes[:].bitcast(FP8X4), scales=plane[:], in_=grouped)
+        def quantise(grouped, codes, plane):
+            nc.vector.quantize_mx(out=codes.bitcast(FP8X4), scales=plane, in_=grouped)
+
+        def quantised_weight(name):
+            codes = keep.tile([P, PASS], U32, name=name + "_codes", align_bytes=64)
+            plane = keep.tile([P, PASS], U8, name=name + "_plane", align_bytes=64)
             return codes, plane
 
-        def quantise_weights(s, copy):
-            grouped = work.tile([P, 2 * P * PACK], BF16, name="grouped", tag="short", bufs=3, align_bytes=64)
+        def quantise_weight(raw, q, t0, t1, copy):
+            grouped = work.tile([P, t1 - t0, P, PACK], BF16, name="grouped", align_bytes=64)
             copy(
-                out=grouped[:].rearrange("p (n c e i) -> p n c i e", n=2, e=4, i=PACK),
-                in_=raws[s].rearrange("p n i (c e) -> p n c i e", e=4),
+                out=grouped[:].rearrange("p t m i -> p m i t"),
+                in_=raw.rearrange("p i (m t) -> p m i t", t=PACK)[:, :, :, t0:t1],
             )
-            return quantise(grouped[:], "w13_%d" % s)
+            quantise(grouped[:].rearrange("p t m i -> p (t m i)"), q[0][:, P * t0 : P * t1], q[1][:, P * t0 : P * t1])
 
-        wq = [quantise_weights(0, nc.vector.tensor_copy)]
+        q1 = [quantised_weight("w1a"), quantised_weight("w1b")]
+        q3 = [quantised_weight("w3a"), quantised_weight("w3b")]
+        quantise_weight(raw1[0], q1[0], 0, PACK, nc.vector.tensor_copy)
         v_plane = keep.tile([P, S], U8, align_bytes=64)
         nc.vector.tensor_copy(v_plane[:], tab_plane[:].indirect(idx[:]))
+        w2_codes = keep.tile([P, 2 * H], U8, align_bytes=64)
+        nc.vector.tensor_copy(
+            out=w2_codes[:].bitcast(U16).rearrange("p (b t m) -> p b m t", b=PASSES, t=PACK),
+            in_=w2_raw[:].bitcast(U16).rearrange("p (b m t) -> p b m t", b=PASSES, t=PACK),
+        )
         v_codes = []
-        for g in range(2):
+
+        def gather_words(g):
             words = keep.tile([P, HALF], U32, name="v_codes%d" % g, align_bytes=64)
             nc.vector.tensor_copy(words[:], tab[:].bitcast(U32).indirect(idx[:, 32 * g : 32 * g + 32]))
             v_codes.append(words)
-        refs.append(load_ref(1, "wide"))
-        pages = [page0]
 
-        def clear_page(n):
-            page = keep.tile([P, T2], F32, name="page", tag="page%d" % n, align_bytes=64)
-            nc.gpsimd.memset(page[:], 0.0)
-            pages.append(page)
+        gather_words(0)
+        w2_plane = keep.tile([P, H], U8, align_bytes=64)
+        nc.vector.tensor_copy(
+            out=w2_plane[:].rearrange("p (b t m) -> p b m t", b=PASSES, t=PACK),
+            in_=w2_rows[:].rearrange("p (b m t) -> p b m t", b=PASSES, t=PACK),
+        )
+        quantise_weight(raw3[0], q3[0], 0, 2, nc.vector.tensor_copy)
+        gather_words(1)
+        for t in range(PACK):
+            clear_page(t)
+        refs.extend(load_ref(1, 0, "raw1a") + load_ref(1, 2, "raw3a"))
+        z0 = keep.tile([P, PACK, PICKS], F32, tag="wide", align_bytes=64)
+        zs = [z0]
 
-        clear_page(1)
-
-        def first_product(g, tag, codes, plane):
-            bank = psum.tile([P, 4, P], F32, name=tag, tag=tag)
+        def first_product(g, tag, bufs, codes, plane):
+            bank = psum.tile([P, 4, P], F32, name=tag, tag=tag, bufs=bufs)
             for k in range(4):
                 nc.tensor.matmul_mx(
                     out=bank[:, k, :],
@@ -133,114 +163,132 @@ def tile_list_burst_derotation_kernel(
                     start=True,
                     stop=True,
                 )
-            return bank
+            return bank[:].rearrange("p k r -> p (k r)")
+
+        def product_room(s, g):
+            if g == 1 and s >= 1:
+                return zs[(s - 1) // PACK][:, (s - 1) % PACK, :]
+            if g == 0 and s >= LAG:
+                return refs[s - LAG]
+            room = work.tile([P, S], F32, name="room")
+            return room[:]
 
         def derotate(s, g):
-            codes, plane = wq[s]
-            phase = first_product(g, "phase", codes[:, 0:P].bitcast(FP8X4), plane[:, 0:P])
-            quad = first_product(g, "quad", codes[:, P : 2 * P].bitcast(FP8X4), plane[:, P : 2 * P])
+            b, t = divmod(s, PACK)
+            cols = slice(P * t, P * (t + 1))
+            phase = first_product(g, "phase", 2, q1[b][0][:, cols].bitcast(FP8X4), q1[b][1][:, cols])
             inph = first_product(
-                g, "inph", w2_codes[:, 2 * P * s : 2 * P * (s + 1)].bitcast(FP4X4), w2_plane[:, P * s : P * (s + 1)]
+                g, "inph", 1, w2_codes[:, 2 * P * s : 2 * P * (s + 1)].bitcast(FP4X4), w2_plane[:, P * s : P * (s + 1)]
             )
-            sin = work.tile([P, 4, P], F32, name="sin")
-            nc.scalar.activation(out=sin[:], in_=phase[:], func=ACT.Sin)
-            size = work.tile([P, 4, P], F32, name="size", tag="short", bufs=3, align_bytes=64)
-            nc.scalar.activation(out=size[:], in_=phase[:], func=ACT.Abs)
-            cos = work.tile([P, 4, P], F32, name="cos")
-            nc.scalar.activation(out=cos[:], in_=size[:], func=ACT.Sin, scale=-1.0, bias=math.pi / 2)
-            sq = work.tile([P, 4, P], F32, name="sq")
-            nc.vector.tensor_tensor(out=sq[:], in0=quad[:], in1=sin[:], op=MULT)
-            ci = work.tile([P, 4, P], F32, name="ci")
-            nc.vector.tensor_tensor(out=ci[:], in0=inph[:], in1=cos[:], op=MULT)
-            hsum = psum.tile([P, 4, P], F32, name="hsum", tag="hsum")
-            for k in range(4):
-                turn(hsum[:, k, :], sq[:, k, :], k == 0, False)
-            for k in range(4):
-                turn(hsum[:, k, :], ci[:, k, :], False, k == 3)
-            return hsum
+            quad = first_product(g, "quad", 1, q3[b][0][:, cols].bitcast(FP8X4), q3[b][1][:, cols])
+            size = work.tile([P, HALF], F32, name="size")
+            trig = work.tile([P, S], F32, name="trig", bufs=3)
+            room = product_room(s, g)
+            if (s, g) == (0, 0):
+                nc.scalar.activation(out=trig[:, HALF:S], in_=phase, func=ACT.Sin)
+                nc.scalar.activation(out=size[:], in_=phase, func=ACT.Abs)
+                nc.scalar.activation(out=trig[:, 0:HALF], in_=size[:], func=ACT.Sin, scale=-1.0, bias=math.pi / 2)
+                nc.vector.tensor_tensor(out=room[:, 0:HALF], in0=inph, in1=trig[:, 0:HALF], op=MULT)
+                nc.vector.tensor_tensor(out=room[:, HALF:S], in0=quad, in1=trig[:, HALF:S], op=MULT)
+                return room
+            nc.scalar.activation(out=size[:], in_=phase, func=ACT.Abs)
+            nc.scalar.activation(out=trig[:, HALF:S], in_=phase, func=ACT.Sin)
+            pair = work.tile([P, S], F32, name="pair", bufs=3)
+            nc.scalar.copy(out=pair[:, 0:HALF], in_=inph)
+            nc.scalar.activation(out=trig[:, 0:HALF], in_=size[:], func=ACT.Sin, scale=-1.0, bias=math.pi / 2)
+            nc.scalar.copy(out=pair[:, HALF:S], in_=quad)
+            nc.gpsimd.tensor_tensor(out=room, in0=pair[:], in1=trig[:], op=MULT)
+            return room
 
-        def turn(dst, src, start, stop):
-            nc.tensor.matmul(out=dst, lhsT=src, rhs=ident[:], is_transpose=True, start=start, stop=stop)
+        def turn(room):
+            hsum = psum.tile([P, 4, P], F32, name="hsum", tag="hsum", bufs=4)
+            for n in range(8):
+                nc.tensor.matmul(
+                    out=hsum[:, n % 4, :], lhsT=room[:, P * n : P * (n + 1)], rhs=ident[:], is_transpose=True,
+                    start=(n == 0), stop=(n == 7),
+                )
+            return hsum[:].rearrange("p k j -> p (k j)")
 
-        def place(s, g, hsum):
-            h = work.tile([P, HALF], F32, name="h", bufs=3)
-            nc.scalar.copy(out=h[:], in_=hsum[:].rearrange("p k j -> p (k j)"))
-            page = pages[s % PACK]
-            nc.vector.tensor_tensor(page[:].indirect(idx2[:, 32 * g : 32 * g + 32]), h[:], gains[:, HALF * g : HALF * (g + 1)], MULT)
+        def place(s, j0, j1, gained):
+            nc.vector.tensor_copy(pages[s % PACK][:].indirect(idx2[:, j0 // 16 : j1 // 16]), gained[:, j0:j1])
 
-        def fetch(dst, t, m0, m1):
-            nc.vector.tensor_copy(dst, pages[t][:].indirect(idx3[:, m0 // 16 : m1 // 16]))
-
-        def quantise_z(b, c, picked, copies, banks):
-            words = psum.tile([P, 2, 2, P], F32, name="words", tag="words", bufs=2)
-            for k in range(2):
-                zsum = psum.tile([P, PACK, P], F32, name="zsum", tag=banks[k])
-                m0 = PIECE * c + P * k
-                for t in range(PACK):
-                    turn(zsum[:, t, :], refs[b][:, t, m0 : m0 + P], t == 0, False)
-                for t in range(PACK):
-                    turn(zsum[:, t, :], picked[:, t, P * k : P * (k + 1)], False, t == PACK - 1)
-                rounded = work.tile([P, 2, P, 2], BF16, name="rounded", tag="short", bufs=3, align_bytes=64)
-                copies[k](out=rounded[:], in_=zsum[:].rearrange("m t (q u e) -> m u (t q) e", u=2, e=2))
-                pairs = rounded[:].rearrange("m u q e -> m (u q e)").bitcast(F32)
-                for u in range(2):
-                    nc.tensor.transpose(words[:, k, u, :], pairs[:, P * u : P * (u + 1)], ident[:])
-            grouped = work.tile([P, PIECE * PACK], BF16, name="zgrouped", bufs=PIECES, align_bytes=64)
-            nc.scalar.copy(
-                out=grouped[:].bitcast(F32).rearrange("q (k m u) -> q k m u", k=2, u=2),
-                in_=words[:].rearrange("q k u m -> q k m u"),
+        def fetch(s, m0, m1):
+            nc.vector.tensor_tensor(
+                zs[s // PACK][:, s % PACK, m0:m1], pages[s % PACK][:].indirect(idx3[:, m0 // 16 : m1 // 16]), refs[s][:, m0:m1], ADD
             )
-            return quantise(grouped[:], "z%d_%d" % (b, c))
 
-        units = [(s, g) for s in range(H // P) for g in range(2)]
-        z0 = []
-        picked0 = keep.tile([P, PACK, PICKS], F32)
-        hsum = derotate(0, 0)
-        wq.append(quantise_weights(1, nc.vector.tensor_copy))
+        z_codes = keep.tile([P, PASSES, PICKS], U32, align_bytes=64)
+        z_plane = keep.tile([P, PASSES, PICKS], U8, align_bytes=64)
+
+        def round_z(b, m0, m1, copy):
+            grouped = work.tile([P, (m1 - m0) * PACK], BF16, name="zgrouped", bufs=PIECES, align_bytes=64)
+            copy(
+                out=grouped[:].rearrange("p (c e t) -> p c t e", e=4, t=PACK),
+                in_=zs[b][:, :, m0:m1].rearrange("p t (c e) -> p c t e", e=4),
+            )
+            return grouped
+
+        def quantise_z(b, m0, m1, grouped):
+            quantise(grouped[:], z_codes[:, b, m0:m1], z_plane[:, b, m0:m1])
+
+        units = [(s, g) for s in range(SLICES) for g in range(2)]
+        room = derotate(0, 0)
+        quantise_weight(raw3[0], q3[0], 2, PACK, nc.vector.tensor_copy)
         for u, (s, g) in enumerate(units):
             following = derotate(*units[u + 1]) if u + 1 < len(units) else None
-            place(s, g, hsum)
-            hsum = following
-            if g == 0 and s + 2 < H // P:
-                wq.append(quantise_weights(s + 2, nc.scalar.copy))
-            if u in (0, 2):
-                clear_page(2 + u // 2)
-            if u == 2 * PACK - 1:
-                for t in range(PACK):
-                    fetch(picked0[:, t, :], t, 0, PICKS)
-            if u in (9, 11, 13, 14):
-                c = len(z0)
-                z0.append(quantise_z(0, c, picked0[:, :, PIECE * c : PIECE * (c + 1)], [nc.scalar.copy, nc.scalar.copy], ("zsum0", "zsum1")))
+            hsum = turn(room)
+            room = following
+            if g == 0:
+                gained = work.tile([P, S], F32, name="gained")
+            nc.vector.tensor_tensor(
+                out=gained[:, HALF * g : HALF * (g + 1)], in0=hsum, in1=gains[s % PACK][:, HALF * g : HALF * (g + 1)], op=MULT
+            )
+            if s < 2:
+                if u == 3:
+                    fetch(0, 0, PICKS)
+                place(s, HALF * g, HALF * (g + 1), gained)
+            elif g == 1:
+                fetch(s - 1, 0, PICKS)
+                place(s, 0, S, gained)
+            if u == 3:
+                quantise_weight(raw1[1], q1[1], 0, PACK, nc.scalar.copy)
+            if u == 5:
+                quantise_weight(raw3[1], q3[1], 0, PACK, nc.scalar.copy)
+                z1 = keep.tile([P, PACK, PICKS], F32, tag="later", align_bytes=64)
+                zs.append(z1)
+            if 10 <= u < 10 + PIECES:
+                m0 = PIECE * (u - 10)
+                quantise_z(0, m0, m0 + PIECE, round_z(0, m0, m0 + PIECE, nc.scalar.copy))
 
-        picked1 = keep.tile([P, PIECES, PACK, PIECE], F32, tag="gains")
+        banks = [("phase", 2), ("phase", 2), ("inph", 1), ("quad", 1)] + [("hsum", 4)] * 4
+
+        def last_product(acc, c, b):
+            for n in range(N // P):
+                nc.tensor.matmul_mx(
+                    out=acc[:, n, :],
+                    lhsT=w4_codes[:, b, P * n : P * (n + 1)].bitcast(FP8X4),
+                    lhsT_scale=w4_plane[:, b, P * n : P * (n + 1)],
+                    rhs=z_codes[:, b, P * c : P * (c + 1)].bitcast(FP8X4),
+                    rhs_scale=z_plane[:, b, P * c : P * (c + 1)],
+                    start=(b == 0 and n == 0),
+                    stop=(b == PASSES - 1 and n == N // P - 1),
+                )
+
+        accs = []
+        for c, (tag, bufs) in enumerate(banks):
+            acc = psum.tile([P, N // P, P], F32, name="acc", tag=tag, bufs=bufs)
+            last_product(acc, c, 0)
+            accs.append(acc)
         for c in range(PIECES):
-            for t in range(PACK):
-                fetch(picked1[:, c, t, :], t, PIECE * c, PIECE * (c + 1))
-        tags = [("phase", "quad"), ("inph", "hsum")]
-        sum_banks = [("zsum0", "zsum1")] + tags + [("zsum0", "zsum1")]
-
-        def second_pass(c):
-            other = nc.vector.tensor_copy if c == PIECES - 1 else nc.scalar.copy
-            return quantise_z(1, c, picked1[:, c], [nc.scalar.copy, other], sum_banks[c])
-
-        z1 = [second_pass(c) for c in range(PIECES)]
+            fetch(SLICES - 1, PIECE * c, PIECE * (c + 1))
+        rounded = [
+            round_z(1, PIECE * c, PIECE * (c + 1), nc.scalar.copy if c < 2 else nc.vector.tensor_copy) for c in range(PIECES)
+        ]
         for c in range(PIECES):
-            zq = [z0[c], z1[c]]
+            quantise_z(1, PIECE * c, PIECE * (c + 1), rounded[c])
             result = work.tile([P, N // P, PIECE], F32, name="result", bufs=PIECES)
-            for pair in range(2):
-                acc = psum.tile([P, 2, PIECE], F32, name="acc", tag=tags[c % 2][pair])
-                for i in range(2):
-                    n = 2 * pair + i
-                    for b in range(PASSES):
-                        nc.tensor.matmul_mx(
-                            out=acc[:, i, :],
-                            lhsT=w4_codes[:, b, P * n : P * (n + 1)].bitcast(FP8X4),
-                            lhsT_scale=w4_plane[:, b, P * n : P * (n + 1)],
-                            rhs=zq[b][0][:].bitcast(FP8X4),
-                            rhs_scale=zq[b][1][:],
-                            start=(b == 0),
-                            stop=(b == PASSES - 1),
-                        )
-                copy = nc.vector.tensor_copy if pair == 0 else nc.scalar.copy
-                copy(out=result[:, 2 * pair : 2 * pair + 2, :], in_=acc[:])
+            for h in range(2):
+                last_product(accs[2 * c + h], 2 * c + h, 1)
+                copy = nc.scalar.copy if h == 0 else nc.vector.tensor_copy
+                copy(out=result[:, :, P * h : P * (h + 1)], in_=accs[2 * c + h][:])
             nc.sync.dma_start(out=out.rearrange("(n p) m -> p n m", p=P)[:, :, PIECE * c : PIECE * (c + 1)], in_=result[:])

@@ -27,7 +27,9 @@ SLICES = H // P
 HALF = S // 2
 PIECE = 256
 PIECES = PICKS // PIECE
+CUTS = (0, 256, 512, 768, 896, 1024)
 LAG = 3
+LAST = (SLICES - 1, 1)
 
 
 def load_scale_rows(queue, plane, rows):
@@ -68,7 +70,7 @@ def tile_list_burst_derotation_kernel(
 
         def load_gains(t0, t1):
             rows = keep.tile([P, t1 - t0, S], F32, name="gains%d" % t0)
-            for q in range(4):
+            for q in (0, 2, 1, 3):
                 nc.sync.dma_start(out=rows[32 * q : 32 * (q + 1)], in_=wgs.rearrange("(q t) j -> q t j", t=PACK)[:, t0:t1])
             return [rows[:, t, :] for t in range(t1 - t0)]
 
@@ -91,17 +93,16 @@ def tile_list_burst_derotation_kernel(
         raw3 = [load_weight(w3, 0, "raw3a")]
         idx2 = lists.tile([P, S // 16], U16)
         nc.sync.dma_start(idx2[:], offs2)
-        gains = load_gains(0, 1)
-        idx3 = lists.tile([P, PICKS // 16], U16)
-        nc.sync.dma_start(idx3[:], offs3)
-        gains.extend(load_gains(1, PACK))
-        refs = load_ref(0, 0, "ref0") + load_ref(0, 2, "ref1")
+        gains = load_gains(0, 2)
         later = keep.tile([P, 2, PACK, PASS], F32, tag="later", align_bytes=64)
         for n, (w, raw) in enumerate(((w1, raw1), (w3, raw3))):
             nc.sync.dma_start(out=later[:, n], in_=w[:, PASS:H].rearrange("(p i) c -> p i c", i=PACK))
             raw.append(later[:, n])
-        w4_codes = keep.tile([P, PASSES, N], I32, align_bytes=64)
-        nc.sync.dma_start(out=w4_codes[:], in_=w4_words.rearrange("a p c i -> p a (c i)").bitcast(I32))
+        idx3 = lists.tile([P, PICKS // 16], U16)
+        nc.sync.dma_start(idx3[:], offs3)
+        refs = load_ref(0, 0, "ref0")
+        gains.extend(load_gains(2, PACK))
+        refs.extend(load_ref(0, 2, "ref1"))
         load_scale_rows(nc.sync, w4_plane, w4_scales.rearrange("a q n -> q a n"))
 
         def quantise(grouped, codes, plane):
@@ -112,8 +113,8 @@ def tile_list_burst_derotation_kernel(
             plane = keep.tile([P, PASS], U8, name=name + "_plane", align_bytes=64)
             return codes, plane
 
-        def quantise_weight(raw, q, t0, t1, copy):
-            grouped = work.tile([P, t1 - t0, P, PACK], BF16, name="grouped", align_bytes=64)
+        def quantise_weight(raw, q, t0, t1, copy, tag):
+            grouped = work.tile([P, t1 - t0, P, PACK], BF16, name="grouped", tag=tag, align_bytes=64)
             copy(
                 out=grouped[:].rearrange("p t m i -> p m i t"),
                 in_=raw.rearrange("p i (m t) -> p m i t", t=PACK)[:, :, :, t0:t1],
@@ -122,7 +123,7 @@ def tile_list_burst_derotation_kernel(
 
         q1 = [quantised_weight("w1a"), quantised_weight("w1b")]
         q3 = [quantised_weight("w3a"), quantised_weight("w3b")]
-        quantise_weight(raw1[0], q1[0], 0, PACK, nc.vector.tensor_copy)
+        quantise_weight(raw1[0], q1[0], 0, PACK, nc.vector.tensor_copy, "grouped")
         v_plane = keep.tile([P, S], U8, align_bytes=64)
         nc.vector.tensor_copy(v_plane[:], tab_plane[:].indirect(idx[:]))
         w2_codes = keep.tile([P, 2 * H], U8, align_bytes=64)
@@ -143,11 +144,10 @@ def tile_list_burst_derotation_kernel(
             out=w2_plane[:].rearrange("p (b t m) -> p b m t", b=PASSES, t=PACK),
             in_=w2_rows[:].rearrange("p (b m t) -> p b m t", b=PASSES, t=PACK),
         )
-        quantise_weight(raw3[0], q3[0], 0, 2, nc.vector.tensor_copy)
+        quantise_weight(raw3[0], q3[0], 0, 2, nc.vector.tensor_copy, "grouped")
         gather_words(1)
         for t in range(PACK):
             clear_page(t)
-        refs.extend(load_ref(1, 0, "raw1a") + load_ref(1, 2, "raw3a"))
         z0 = keep.tile([P, PACK, PICKS], F32, tag="wide", align_bytes=64)
         zs = [z0]
 
@@ -166,11 +166,16 @@ def tile_list_burst_derotation_kernel(
             return bank[:].rearrange("p k r -> p (k r)")
 
         def product_room(s, g):
+            if (s, g) == LAST:
+                room = keep.tile([P, S], F32, name="room", tag="w4", align_bytes=64)
+                return room[:]
+            if (s, g) == (SLICES - 1, 0):
+                return zs[1][:, PACK - 1, :]
             if g == 1 and s >= 1:
                 return zs[(s - 1) // PACK][:, (s - 1) % PACK, :]
             if g == 0 and s >= LAG:
                 return refs[s - LAG]
-            room = work.tile([P, S], F32, name="room")
+            room = work.tile([P, S], F32, name="room", align_bytes=64)
             return room[:]
 
         def derotate(s, g):
@@ -182,7 +187,10 @@ def tile_list_burst_derotation_kernel(
             )
             quad = first_product(g, "quad", 1, q3[b][0][:, cols].bitcast(FP8X4), q3[b][1][:, cols])
             size = work.tile([P, HALF], F32, name="size")
-            trig = work.tile([P, S], F32, name="trig", bufs=3)
+            if (s, g) == LAST:
+                trig = keep.tile([P, S], F32, name="trig", tag="raw1a", align_bytes=64)
+            else:
+                trig = work.tile([P, S], F32, name="trig", bufs=3)
             room = product_room(s, g)
             if (s, g) == (0, 0):
                 nc.scalar.activation(out=trig[:, HALF:S], in_=phase, func=ACT.Sin)
@@ -193,11 +201,15 @@ def tile_list_burst_derotation_kernel(
                 return room
             nc.scalar.activation(out=size[:], in_=phase, func=ACT.Abs)
             nc.scalar.activation(out=trig[:, HALF:S], in_=phase, func=ACT.Sin)
-            pair = work.tile([P, S], F32, name="pair", bufs=3)
+            if (s, g) == LAST:
+                pair = keep.tile([P, S], F32, name="pair", tag="raw3a", align_bytes=64)
+            else:
+                pair = work.tile([P, S], F32, name="pair", bufs=3, align_bytes=64)
             nc.scalar.copy(out=pair[:, 0:HALF], in_=inph)
             nc.scalar.activation(out=trig[:, 0:HALF], in_=size[:], func=ACT.Sin, scale=-1.0, bias=math.pi / 2)
             nc.scalar.copy(out=pair[:, HALF:S], in_=quad)
-            nc.gpsimd.tensor_tensor(out=room, in0=pair[:], in1=trig[:], op=MULT)
+            for half in (slice(0, HALF), slice(HALF, S)):
+                nc.gpsimd.tensor_tensor(out=room[:, half], in0=pair[:, half], in1=trig[:, half], op=MULT)
             return room
 
         def turn(room):
@@ -212,19 +224,19 @@ def tile_list_burst_derotation_kernel(
         def place(s, j0, j1, gained):
             nc.vector.tensor_copy(pages[s % PACK][:].indirect(idx2[:, j0 // 16 : j1 // 16]), gained[:, j0:j1])
 
-        def fetch(s, m0, m1):
+        def fetch(dst, s, m0, m1):
             nc.vector.tensor_tensor(
-                zs[s // PACK][:, s % PACK, m0:m1], pages[s % PACK][:].indirect(idx3[:, m0 // 16 : m1 // 16]), refs[s][:, m0:m1], ADD
+                dst, pages[s % PACK][:].indirect(idx3[:, m0 // 16 : m1 // 16]), refs[s][:, m0:m1], ADD
             )
 
         z_codes = keep.tile([P, PASSES, PICKS], U32, align_bytes=64)
         z_plane = keep.tile([P, PASSES, PICKS], U8, align_bytes=64)
 
-        def round_z(b, m0, m1, copy):
-            grouped = work.tile([P, (m1 - m0) * PACK], BF16, name="zgrouped", bufs=PIECES, align_bytes=64)
+        def round_z(z, copy, tag, bufs):
+            grouped = work.tile([P, z.shape[2] * PACK], BF16, name="zgrouped", tag=tag, bufs=bufs, align_bytes=64)
             copy(
                 out=grouped[:].rearrange("p (c e t) -> p c t e", e=4, t=PACK),
-                in_=zs[b][:, :, m0:m1].rearrange("p t (c e) -> p c t e", e=4),
+                in_=z.rearrange("p t (c e) -> p c t e", e=4),
             )
             return grouped
 
@@ -233,7 +245,7 @@ def tile_list_burst_derotation_kernel(
 
         units = [(s, g) for s in range(SLICES) for g in range(2)]
         room = derotate(0, 0)
-        quantise_weight(raw3[0], q3[0], 2, PACK, nc.vector.tensor_copy)
+        quantise_weight(raw3[0], q3[0], 2, PACK, nc.vector.tensor_copy, "grouped")
         for u, (s, g) in enumerate(units):
             following = derotate(*units[u + 1]) if u + 1 < len(units) else None
             hsum = turn(room)
@@ -245,21 +257,25 @@ def tile_list_burst_derotation_kernel(
             )
             if s < 2:
                 if u == 3:
-                    fetch(0, 0, PICKS)
+                    fetch(zs[0][:, 0, :], 0, 0, PICKS)
                 place(s, HALF * g, HALF * (g + 1), gained)
             elif g == 1:
-                fetch(s - 1, 0, PICKS)
+                if s <= PACK:
+                    fetch(zs[0][:, s - 1, :], s - 1, 0, PICKS)
                 place(s, 0, S, gained)
+            if u == 2:
+                quantise_weight(raw1[1], q1[1], 0, PACK, nc.scalar.copy, "room")
             if u == 3:
-                quantise_weight(raw1[1], q1[1], 0, PACK, nc.scalar.copy)
-            if u == 5:
-                quantise_weight(raw3[1], q3[1], 0, PACK, nc.scalar.copy)
+                quantise_weight(raw3[1], q3[1], 0, PACK, nc.scalar.copy, "room")
                 z1 = keep.tile([P, PACK, PICKS], F32, tag="later", align_bytes=64)
                 zs.append(z1)
-            if 10 <= u < 10 + PIECES:
-                m0 = PIECE * (u - 10)
-                quantise_z(0, m0, m0 + PIECE, round_z(0, m0, m0 + PIECE, nc.scalar.copy))
+            if u == len(units) - 3:
+                for m0 in (0, HALF):
+                    quantise_z(0, m0, m0 + HALF, round_z(zs[0][:, :, m0 : m0 + HALF], nc.scalar.copy, "pair", 3))
 
+        refs.extend(load_ref(1, 0, "raw1a") + load_ref(1, 2, "raw3a"))
+        w4_codes = keep.tile([P, PASSES, N], I32, tag="w4", align_bytes=64)
+        nc.sync.dma_start(out=w4_codes[:], in_=w4_words.rearrange("a p c i -> p a (c i)").bitcast(I32))
         banks = [("phase", 2), ("phase", 2), ("inph", 1), ("quad", 1)] + [("hsum", 4)] * 4
 
         def last_product(acc, c, b):
@@ -279,16 +295,15 @@ def tile_list_burst_derotation_kernel(
             acc = psum.tile([P, N // P, P], F32, name="acc", tag=tag, bufs=bufs)
             last_product(acc, c, 0)
             accs.append(acc)
-        for c in range(PIECES):
-            fetch(SLICES - 1, PIECE * c, PIECE * (c + 1))
-        rounded = [
-            round_z(1, PIECE * c, PIECE * (c + 1), nc.scalar.copy if c < 2 else nc.vector.tensor_copy) for c in range(PIECES)
-        ]
-        for c in range(PIECES):
-            quantise_z(1, PIECE * c, PIECE * (c + 1), rounded[c])
-            result = work.tile([P, N // P, PIECE], F32, name="result", bufs=PIECES)
-            for h in range(2):
-                last_product(accs[2 * c + h], 2 * c + h, 1)
-                copy = nc.scalar.copy if h == 0 else nc.vector.tensor_copy
-                copy(out=result[:, :, P * h : P * (h + 1)], in_=accs[2 * c + h][:])
-            nc.sync.dma_start(out=out.rearrange("(n p) m -> p n m", p=P)[:, :, PIECE * c : PIECE * (c + 1)], in_=result[:])
+        for m0, m1 in zip(CUTS, CUTS[1:]):
+            picked = work.tile([P, PACK, m1 - m0], F32, name="picked")
+            for t in range(PACK):
+                fetch(picked[:, t, :], PACK + t, m0, m1)
+            copy = nc.scalar.copy if m1 < PICKS else nc.vector.tensor_copy
+            quantise_z(1, m0, m1, round_z(picked[:], copy, "zgrouped", 2))
+        for c in range(2 * PIECES):
+            result = work.tile([P, N // P, P], F32, name="result", bufs=2 * PIECES)
+            last_product(accs[c], c, 1)
+            copy = nc.vector.tensor_copy if c == 2 * PIECES - 1 else nc.scalar.copy
+            copy(out=result[:], in_=accs[c][:])
+            nc.sync.dma_start(out=out.rearrange("(n p) m -> p n m", p=P)[:, :, P * c : P * (c + 1)], in_=result[:])

@@ -29,7 +29,9 @@ PIECE = 256
 PIECES = PICKS // PIECE
 CUTS = (0, 256, 512, 768, 896, 1024)
 LAG = 3
-LAST = (SLICES - 1, 1)
+LAST = (SLICES - 1, HALF)
+FUSED = SLICES - 2
+PAIR_TAGS = {(1, HALF): "page2", (2, HALF): "page3", LAST: "raw3a"}
 
 
 def load_scale_rows(queue, plane, rows):
@@ -55,9 +57,9 @@ def tile_list_burst_derotation_kernel(
         nc.vector.memset(w4_plane[:].rearrange("p a n -> p (a n)").bitcast(I32), 0)
         pages = []
 
-        def clear_page(t):
-            page = keep.tile([P, T2], F32, name="page%d" % t, align_bytes=64)
-            nc.vector.memset(page[:], 0.0)
+        def clear_page(t, engine):
+            page = keep.tile([P, T2], F32, name="page", tag="page%d" % t, align_bytes=64)
+            engine.memset(page[:], 0.0)
             pages.append(page)
 
         ident = keep.tile([P, P], F32)
@@ -93,11 +95,12 @@ def tile_list_burst_derotation_kernel(
         raw3 = [load_weight(w3, 0, "raw3a")]
         idx2 = lists.tile([P, S // 16], U16)
         nc.sync.dma_start(idx2[:], offs2)
-        gains = load_gains(0, 2)
+        gains = load_gains(0, 1)
         later = keep.tile([P, 2, PACK, PASS], F32, tag="later", align_bytes=64)
         for n, (w, raw) in enumerate(((w1, raw1), (w3, raw3))):
             nc.sync.dma_start(out=later[:, n], in_=w[:, PASS:H].rearrange("(p i) c -> p i c", i=PACK))
             raw.append(later[:, n])
+        gains.extend(load_gains(1, 2))
         idx3 = lists.tile([P, PICKS // 16], U16)
         nc.sync.dma_start(idx3[:], offs3)
         refs = load_ref(0, 0, "ref0")
@@ -116,8 +119,8 @@ def tile_list_burst_derotation_kernel(
         def quantise_weight(raw, q, t0, t1, copy, tag):
             grouped = work.tile([P, t1 - t0, P, PACK], BF16, name="grouped", tag=tag, align_bytes=64)
             copy(
-                out=grouped[:].rearrange("p t m i -> p m i t"),
-                in_=raw.rearrange("p i (m t) -> p m i t", t=PACK)[:, :, :, t0:t1],
+                out=grouped[:].rearrange("p t m i -> p m t i"),
+                in_=raw.rearrange("p i (m t) -> p m t i", t=PACK)[:, :, t0:t1, :],
             )
             quantise(grouped[:].rearrange("p t m i -> p (t m i)"), q[0][:, P * t0 : P * t1], q[1][:, P * t0 : P * t1])
 
@@ -146,80 +149,82 @@ def tile_list_burst_derotation_kernel(
         )
         quantise_weight(raw3[0], q3[0], 0, 2, nc.vector.tensor_copy, "grouped")
         gather_words(1)
-        for t in range(PACK):
-            clear_page(t)
+        for t in range(2):
+            clear_page(t, nc.vector)
         z0 = keep.tile([P, PACK, PICKS], F32, tag="wide", align_bytes=64)
         zs = [z0]
 
-        def first_product(g, tag, bufs, codes, plane):
-            bank = psum.tile([P, 4, P], F32, name=tag, tag=tag, bufs=bufs)
-            for k in range(4):
+        def first_product(j0, j1, tag, bufs, codes, plane):
+            bank = psum.tile([P, j1 - j0], F32, name=tag, tag=tag, bufs=bufs)
+            for j in range(j0, j1, P):
                 nc.tensor.matmul_mx(
-                    out=bank[:, k, :],
-                    lhsT=v_codes[g][:, P * k : P * (k + 1)].bitcast(FP8X4),
-                    lhsT_scale=v_plane[:, HALF * g + P * k : HALF * g + P * (k + 1)],
+                    out=bank[:, j - j0 : j - j0 + P],
+                    lhsT=v_codes[j // HALF][:, j % HALF : j % HALF + P].bitcast(FP8X4),
+                    lhsT_scale=v_plane[:, j : j + P],
                     rhs=codes,
                     rhs_scale=plane,
                     start=True,
                     stop=True,
                 )
-            return bank[:].rearrange("p k r -> p (k r)")
+            return bank[:]
 
-        def product_room(s, g):
-            if (s, g) == LAST:
+        def product_room(s, j0):
+            if (s, j0) == LAST:
                 room = keep.tile([P, S], F32, name="room", tag="w4", align_bytes=64)
                 return room[:]
-            if (s, g) == (SLICES - 1, 0):
+            if (s, j0) == (SLICES - 1, 0):
                 return zs[1][:, PACK - 1, :]
-            if g == 1 and s >= 1:
+            if j0 == HALF and s >= 1:
                 return zs[(s - 1) // PACK][:, (s - 1) % PACK, :]
-            if g == 0 and s >= LAG:
+            if j0 == 0 and s >= LAG:
                 return refs[s - LAG]
             room = work.tile([P, S], F32, name="room", align_bytes=64)
             return room[:]
 
-        def derotate(s, g):
+        def derotate(s, j0, j1):
             b, t = divmod(s, PACK)
             cols = slice(P * t, P * (t + 1))
-            phase = first_product(g, "phase", 2, q1[b][0][:, cols].bitcast(FP8X4), q1[b][1][:, cols])
+            first, second = slice(0, j1 - j0), slice(j1 - j0, 2 * (j1 - j0))
+            phase = first_product(j0, j1, "phase", 2, q1[b][0][:, cols].bitcast(FP8X4), q1[b][1][:, cols])
+            spare = (s, j0) == (0, PIECE)
             inph = first_product(
-                g, "inph", 1, w2_codes[:, 2 * P * s : 2 * P * (s + 1)].bitcast(FP4X4), w2_plane[:, P * s : P * (s + 1)]
+                j0, j1, *(("hsum", 4) if spare else ("inph", 1)), w2_codes[:, 2 * P * s : 2 * P * (s + 1)].bitcast(FP4X4), w2_plane[:, P * s : P * (s + 1)]
             )
-            quad = first_product(g, "quad", 1, q3[b][0][:, cols].bitcast(FP8X4), q3[b][1][:, cols])
-            size = work.tile([P, HALF], F32, name="size")
-            if (s, g) == LAST:
+            quad = first_product(j0, j1, *(("hsum", 4) if spare else ("quad", 1)), q3[b][0][:, cols].bitcast(FP8X4), q3[b][1][:, cols])
+            size = work.tile([P, j1 - j0], F32, name="size", align_bytes=64)
+            if (s, j0) == LAST:
                 trig = keep.tile([P, S], F32, name="trig", tag="raw1a", align_bytes=64)
             else:
                 trig = work.tile([P, S], F32, name="trig", bufs=3)
-            room = product_room(s, g)
-            if (s, g) == (0, 0):
-                nc.scalar.activation(out=trig[:, HALF:S], in_=phase, func=ACT.Sin)
+            room = product_room(s, j0)
+            if j1 - j0 < HALF:
+                nc.scalar.activation(out=trig[:, second], in_=phase, func=ACT.Sin)
                 nc.scalar.activation(out=size[:], in_=phase, func=ACT.Abs)
-                nc.scalar.activation(out=trig[:, 0:HALF], in_=size[:], func=ACT.Sin, scale=-1.0, bias=math.pi / 2)
-                nc.vector.tensor_tensor(out=room[:, 0:HALF], in0=inph, in1=trig[:, 0:HALF], op=MULT)
-                nc.vector.tensor_tensor(out=room[:, HALF:S], in0=quad, in1=trig[:, HALF:S], op=MULT)
+                nc.scalar.activation(out=trig[:, first], in_=size[:], func=ACT.Sin, scale=-1.0, bias=math.pi / 2)
+                nc.vector.tensor_tensor(out=room[:, first], in0=inph, in1=trig[:, first], op=MULT)
+                nc.vector.tensor_tensor(out=room[:, second], in0=quad, in1=trig[:, second], op=MULT)
                 return room
             nc.scalar.activation(out=size[:], in_=phase, func=ACT.Abs)
-            nc.scalar.activation(out=trig[:, HALF:S], in_=phase, func=ACT.Sin)
-            if (s, g) == LAST:
-                pair = keep.tile([P, S], F32, name="pair", tag="raw3a", align_bytes=64)
+            nc.scalar.activation(out=trig[:, second], in_=phase, func=ACT.Sin)
+            if (s, j0) in PAIR_TAGS:
+                pair = keep.tile([P, S], F32, name="pair", tag=PAIR_TAGS[(s, j0)], align_bytes=64)
             else:
                 pair = work.tile([P, S], F32, name="pair", bufs=3, align_bytes=64)
-            nc.scalar.copy(out=pair[:, 0:HALF], in_=inph)
-            nc.scalar.activation(out=trig[:, 0:HALF], in_=size[:], func=ACT.Sin, scale=-1.0, bias=math.pi / 2)
-            nc.scalar.copy(out=pair[:, HALF:S], in_=quad)
-            for half in (slice(0, HALF), slice(HALF, S)):
+            nc.scalar.copy(out=pair[:, first], in_=inph)
+            nc.scalar.activation(out=trig[:, first], in_=size[:], func=ACT.Sin, scale=-1.0, bias=math.pi / 2)
+            nc.scalar.copy(out=pair[:, second], in_=quad)
+            for half in (first, second):
                 nc.gpsimd.tensor_tensor(out=room[:, half], in0=pair[:, half], in1=trig[:, half], op=MULT)
             return room
 
-        def turn(room):
-            hsum = psum.tile([P, 4, P], F32, name="hsum", tag="hsum", bufs=4)
-            for n in range(8):
+        def turn(room, width):
+            hsum = psum.tile([P, width], F32, name="hsum", tag="hsum", bufs=4)
+            for j in range(0, 2 * width, P):
                 nc.tensor.matmul(
-                    out=hsum[:, n % 4, :], lhsT=room[:, P * n : P * (n + 1)], rhs=ident[:], is_transpose=True,
-                    start=(n == 0), stop=(n == 7),
+                    out=hsum[:, j % width : j % width + P], lhsT=room[:, j : j + P], rhs=ident[:], is_transpose=True,
+                    start=(j == 0), stop=(j == 2 * width - P),
                 )
-            return hsum[:].rearrange("p k j -> p (k j)")
+            return hsum[:]
 
         def place(s, j0, j1, gained):
             nc.vector.tensor_copy(pages[s % PACK][:].indirect(idx2[:, j0 // 16 : j1 // 16]), gained[:, j0:j1])
@@ -243,35 +248,38 @@ def tile_list_burst_derotation_kernel(
         def quantise_z(b, m0, m1, grouped):
             quantise(grouped[:], z_codes[:, b, m0:m1], z_plane[:, b, m0:m1])
 
-        units = [(s, g) for s in range(SLICES) for g in range(2)]
-        room = derotate(0, 0)
-        quantise_weight(raw3[0], q3[0], 2, PACK, nc.vector.tensor_copy, "grouped")
-        for u, (s, g) in enumerate(units):
+        units = [(0, 0, PIECE), (0, PIECE, HALF)] + [(s, j0, j0 + HALF) for s in range(SLICES) for j0 in (0, HALF)][1:]
+        room = derotate(*units[0])
+        for u, (s, j0, j1) in enumerate(units):
             following = derotate(*units[u + 1]) if u + 1 < len(units) else None
-            hsum = turn(room)
+            if u == 0:
+                quantise_weight(raw3[0], q3[0], 2, PACK, nc.vector.tensor_copy, "grouped")
+            hsum = turn(room, j1 - j0)
             room = following
-            if g == 0:
-                gained = work.tile([P, S], F32, name="gained")
-            nc.vector.tensor_tensor(
-                out=gained[:, HALF * g : HALF * (g + 1)], in0=hsum, in1=gains[s % PACK][:, HALF * g : HALF * (g + 1)], op=MULT
-            )
+            if j0 == 0:
+                gained = work.tile([P, S], F32, name="gained", bufs=3)
+            if s < FUSED:
+                nc.vector.tensor_tensor(out=gained[:, j0:j1], in0=hsum, in1=gains[s % PACK][:, j0:j1], op=MULT)
+            else:
+                nc.scalar.copy(out=gained[:, j0:j1], in_=hsum)
+            if j1 == S and 1 <= s <= PACK:
+                fetch(zs[0][:, s - 1, :], s - 1, 0, PICKS)
             if s < 2:
-                if u == 3:
-                    fetch(zs[0][:, 0, :], 0, 0, PICKS)
-                place(s, HALF * g, HALF * (g + 1), gained)
-            elif g == 1:
-                if s <= PACK:
-                    fetch(zs[0][:, s - 1, :], s - 1, 0, PICKS)
+                place(s, j0, j1, gained)
+            elif j1 == S and s < FUSED:
                 place(s, 0, S, gained)
-            if u == 2:
+            elif j1 == S:
+                nc.vector.tensor_tensor(pages[s % PACK][:].indirect(idx2[:]), gained[:], gains[s % PACK], MULT)
+            if (s, j0) == (1, 0):
                 quantise_weight(raw1[1], q1[1], 0, PACK, nc.scalar.copy, "room")
-            if u == 3:
+                clear_page(2, nc.gpsimd)
+            if (s, j0) == (2, 0):
                 quantise_weight(raw3[1], q3[1], 0, PACK, nc.scalar.copy, "room")
+                clear_page(3, nc.gpsimd)
                 z1 = keep.tile([P, PACK, PICKS], F32, tag="later", align_bytes=64)
                 zs.append(z1)
-            if u == len(units) - 3:
-                for m0 in (0, HALF):
-                    quantise_z(0, m0, m0 + HALF, round_z(zs[0][:, :, m0 : m0 + HALF], nc.scalar.copy, "pair", 3))
+        for m0 in (0, HALF):
+            quantise_z(0, m0, m0 + HALF, round_z(zs[0][:, :, m0 : m0 + HALF], nc.scalar.copy, "size", 2))
 
         refs.extend(load_ref(1, 0, "raw1a") + load_ref(1, 2, "raw3a"))
         w4_codes = keep.tile([P, PASSES, N], I32, tag="w4", align_bytes=64)
@@ -301,9 +309,9 @@ def tile_list_burst_derotation_kernel(
                 fetch(picked[:, t, :], PACK + t, m0, m1)
             copy = nc.scalar.copy if m1 < PICKS else nc.vector.tensor_copy
             quantise_z(1, m0, m1, round_z(picked[:], copy, "zgrouped", 2))
+        result = keep.tile([P, 2 * PIECES, N // P, P], F32, tag="wide", align_bytes=64)
         for c in range(2 * PIECES):
-            result = work.tile([P, N // P, P], F32, name="result", bufs=2 * PIECES)
             last_product(accs[c], c, 1)
             copy = nc.vector.tensor_copy if c == 2 * PIECES - 1 else nc.scalar.copy
-            copy(out=result[:], in_=accs[c][:])
-            nc.sync.dma_start(out=out.rearrange("(n p) m -> p n m", p=P)[:, :, P * c : P * (c + 1)], in_=result[:])
+            copy(out=result[:, c], in_=accs[c][:])
+            nc.sync.dma_start(out=out.rearrange("(n p) m -> p n m", p=P)[:, :, P * c : P * (c + 1)], in_=result[:, c])

@@ -30,7 +30,6 @@ PIECES = PICKS // PIECE
 CUTS = (0, 256, 512, 768, 896, 1024)
 LAG = 3
 LAST = (SLICES - 1, HALF)
-FUSED = SLICES - 2
 PAIR_TAGS = {(1, HALF): "page2", (2, HALF): "page3", LAST: "raw3a"}
 
 
@@ -258,18 +257,13 @@ def tile_list_burst_derotation_kernel(
             room = following
             if j0 == 0:
                 gained = work.tile([P, S], F32, name="gained", bufs=3)
-            if s < FUSED:
-                nc.vector.tensor_tensor(out=gained[:, j0:j1], in0=hsum, in1=gains[s % PACK][:, j0:j1], op=MULT)
-            else:
-                nc.scalar.copy(out=gained[:, j0:j1], in_=hsum)
+            nc.vector.tensor_tensor(out=gained[:, j0:j1], in0=hsum, in1=gains[s % PACK][:, j0:j1], op=MULT)
             if j1 == S and 1 <= s <= PACK:
                 fetch(zs[0][:, s - 1, :], s - 1, 0, PICKS)
             if s < 2:
                 place(s, j0, j1, gained)
-            elif j1 == S and s < FUSED:
-                place(s, 0, S, gained)
             elif j1 == S:
-                nc.vector.tensor_tensor(pages[s % PACK][:].indirect(idx2[:]), gained[:], gains[s % PACK], MULT)
+                place(s, 0, S, gained)
             if (s, j0) == (1, 0):
                 quantise_weight(raw1[1], q1[1], 0, PACK, nc.scalar.copy, "room")
                 clear_page(2, nc.gpsimd)

@@ -30,7 +30,6 @@ PIECES = PICKS // PIECE
 CUTS = (0, 256, 512, 768, 896, 1024)
 LAG = 3
 LAST = (SLICES - 1, HALF)
-PAIR_TAGS = {(1, HALF): "page2", (2, HALF): "page3", LAST: "raw3a"}
 
 
 def load_scale_rows(queue, plane, rows):
@@ -56,9 +55,9 @@ def tile_list_burst_derotation_kernel(
         nc.vector.memset(w4_plane[:].rearrange("p a n -> p (a n)").bitcast(I32), 0)
         pages = []
 
-        def clear_page(t, engine):
-            page = keep.tile([P, T2], F32, name="page", tag="page%d" % t, align_bytes=64)
-            engine.memset(page[:], 0.0)
+        def clear_page(t):
+            page = keep.tile([P, T2], F32, name="page%d" % t, align_bytes=64)
+            nc.vector.memset(page[:], 0.0)
             pages.append(page)
 
         ident = keep.tile([P, P], F32)
@@ -118,8 +117,8 @@ def tile_list_burst_derotation_kernel(
         def quantise_weight(raw, q, t0, t1, copy, tag):
             grouped = work.tile([P, t1 - t0, P, PACK], BF16, name="grouped", tag=tag, align_bytes=64)
             copy(
-                out=grouped[:].rearrange("p t m i -> p m t i"),
-                in_=raw.rearrange("p i (m t) -> p m t i", t=PACK)[:, :, t0:t1, :],
+                out=grouped[:].rearrange("p t m i -> p m i t"),
+                in_=raw.rearrange("p i (m t) -> p m i t", t=PACK)[:, :, :, t0:t1],
             )
             quantise(grouped[:].rearrange("p t m i -> p (t m i)"), q[0][:, P * t0 : P * t1], q[1][:, P * t0 : P * t1])
 
@@ -148,8 +147,8 @@ def tile_list_burst_derotation_kernel(
         )
         quantise_weight(raw3[0], q3[0], 0, 2, nc.vector.tensor_copy, "grouped")
         gather_words(1)
-        for t in range(2):
-            clear_page(t, nc.vector)
+        for t in range(PACK):
+            clear_page(t)
         z0 = keep.tile([P, PACK, PICKS], F32, tag="wide", align_bytes=64)
         zs = [z0]
 
@@ -205,8 +204,8 @@ def tile_list_burst_derotation_kernel(
                 return room
             nc.scalar.activation(out=size[:], in_=phase, func=ACT.Abs)
             nc.scalar.activation(out=trig[:, second], in_=phase, func=ACT.Sin)
-            if (s, j0) in PAIR_TAGS:
-                pair = keep.tile([P, S], F32, name="pair", tag=PAIR_TAGS[(s, j0)], align_bytes=64)
+            if (s, j0) == LAST:
+                pair = keep.tile([P, S], F32, name="pair", tag="raw3a", align_bytes=64)
             else:
                 pair = work.tile([P, S], F32, name="pair", bufs=3, align_bytes=64)
             nc.scalar.copy(out=pair[:, first], in_=inph)
@@ -266,10 +265,8 @@ def tile_list_burst_derotation_kernel(
                 place(s, 0, S, gained)
             if (s, j0) == (1, 0):
                 quantise_weight(raw1[1], q1[1], 0, PACK, nc.scalar.copy, "room")
-                clear_page(2, nc.gpsimd)
             if (s, j0) == (2, 0):
                 quantise_weight(raw3[1], q3[1], 0, PACK, nc.scalar.copy, "room")
-                clear_page(3, nc.gpsimd)
                 z1 = keep.tile([P, PACK, PICKS], F32, tag="later", align_bytes=64)
                 zs.append(z1)
         for m0 in (0, HALF):

@@ -29,6 +29,7 @@ PIECE = 256
 PIECES = PICKS // PIECE
 CUTS = (0, 256, 512, 768, 896, 1024)
 LAG = 3
+PAGES = 2
 LAST = (SLICES - 1, HALF)
 
 
@@ -147,8 +148,9 @@ def tile_list_burst_derotation_kernel(
         )
         quantise_weight(raw3[0], q3[0], 0, 2, nc.vector.tensor_copy, "grouped")
         gather_words(1)
-        for t in range(PACK):
-            clear_page(t)
+        for n in range(PAGES):
+            clear_page(n)
+        refs.extend(load_ref(1, 0, "raw1a"))
         z0 = keep.tile([P, PACK, PICKS], F32, tag="wide", align_bytes=64)
         zs = [z0]
 
@@ -170,8 +172,6 @@ def tile_list_burst_derotation_kernel(
             if (s, j0) == LAST:
                 room = keep.tile([P, S], F32, name="room", tag="w4", align_bytes=64)
                 return room[:]
-            if (s, j0) == (SLICES - 1, 0):
-                return zs[1][:, PACK - 1, :]
             if j0 == HALF and s >= 1:
                 return zs[(s - 1) // PACK][:, (s - 1) % PACK, :]
             if j0 == 0 and s >= LAG:
@@ -190,10 +190,7 @@ def tile_list_burst_derotation_kernel(
             )
             quad = first_product(j0, j1, *(("hsum", 4) if spare else ("quad", 1)), q3[b][0][:, cols].bitcast(FP8X4), q3[b][1][:, cols])
             size = work.tile([P, j1 - j0], F32, name="size", align_bytes=64)
-            if (s, j0) == LAST:
-                trig = keep.tile([P, S], F32, name="trig", tag="raw1a", align_bytes=64)
-            else:
-                trig = work.tile([P, S], F32, name="trig", bufs=3)
+            trig = work.tile([P, S], F32, name="trig", bufs=3)
             room = product_room(s, j0)
             if j1 - j0 < HALF:
                 nc.scalar.activation(out=trig[:, second], in_=phase, func=ACT.Sin)
@@ -225,11 +222,11 @@ def tile_list_burst_derotation_kernel(
             return hsum[:]
 
         def place(s, j0, j1, gained):
-            nc.vector.tensor_copy(pages[s % PACK][:].indirect(idx2[:, j0 // 16 : j1 // 16]), gained[:, j0:j1])
+            nc.vector.tensor_copy(pages[s % PAGES][:].indirect(idx2[:, j0 // 16 : j1 // 16]), gained[:, j0:j1])
 
         def fetch(dst, s, m0, m1):
             nc.vector.tensor_tensor(
-                dst, pages[s % PACK][:].indirect(idx3[:, m0 // 16 : m1 // 16]), refs[s][:, m0:m1], ADD
+                dst, pages[s % PAGES][:].indirect(idx3[:, m0 // 16 : m1 // 16]), refs[s][:, m0:m1], ADD
             )
 
         z_codes = keep.tile([P, PASSES, PICKS], U32, align_bytes=64)
@@ -256,23 +253,29 @@ def tile_list_burst_derotation_kernel(
             room = following
             if j0 == 0:
                 gained = work.tile([P, S], F32, name="gained", bufs=3)
-            nc.vector.tensor_tensor(out=gained[:, j0:j1], in0=hsum, in1=gains[s % PACK][:, j0:j1], op=MULT)
-            if j1 == S and 1 <= s <= PACK:
-                fetch(zs[0][:, s - 1, :], s - 1, 0, PICKS)
+            if s < SLICES - 1:
+                nc.vector.tensor_tensor(out=gained[:, j0:j1], in0=hsum, in1=gains[s % PACK][:, j0:j1], op=MULT)
+            else:
+                nc.scalar.copy(out=gained[:, j0:j1], in_=hsum)
+            if j1 == S and 1 <= s < SLICES - 1:
+                fetch(zs[(s - 1) // PACK][:, (s - 1) % PACK, :], s - 1, 0, PICKS)
             if s < 2:
                 place(s, j0, j1, gained)
-            elif j1 == S:
+            elif j1 == S and s < SLICES - 1:
                 place(s, 0, S, gained)
+            elif j1 == S:
+                nc.vector.tensor_tensor(pages[s % PAGES][:].indirect(idx2[:]), gained[:], gains[s % PACK], MULT)
+            if (s, j0) == (SLICES - 2, HALF):
+                for m0 in (0, HALF):
+                    quantise_z(0, m0, m0 + HALF, round_z(zs[0][:, :, m0 : m0 + HALF], nc.scalar.copy, "pair", 3))
             if (s, j0) == (1, 0):
                 quantise_weight(raw1[1], q1[1], 0, PACK, nc.scalar.copy, "room")
             if (s, j0) == (2, 0):
                 quantise_weight(raw3[1], q3[1], 0, PACK, nc.scalar.copy, "room")
                 z1 = keep.tile([P, PACK, PICKS], F32, tag="later", align_bytes=64)
                 zs.append(z1)
-        for m0 in (0, HALF):
-            quantise_z(0, m0, m0 + HALF, round_z(zs[0][:, :, m0 : m0 + HALF], nc.scalar.copy, "size", 2))
 
-        refs.extend(load_ref(1, 0, "raw1a") + load_ref(1, 2, "raw3a"))
+        refs.extend(load_ref(1, 2, "raw3a"))
         w4_codes = keep.tile([P, PASSES, N], I32, tag="w4", align_bytes=64)
         nc.sync.dma_start(out=w4_codes[:], in_=w4_words.rearrange("a p c i -> p a (c i)").bitcast(I32))
         banks = [("phase", 2), ("phase", 2), ("inph", 1), ("quad", 1)] + [("hsum", 4)] * 4
@@ -294,15 +297,24 @@ def tile_list_burst_derotation_kernel(
             acc = psum.tile([P, N // P, P], F32, name="acc", tag=tag, bufs=bufs)
             last_product(acc, c, 0)
             accs.append(acc)
+        grouped = keep.tile([P, PICKS, PACK], BF16, align_bytes=64)
+
+        def round_pair(t0, m0, m1, z, copy):
+            copy(
+                out=grouped[:, m0:m1, t0 : t0 + 2].rearrange("p (c e) t -> p c t e", e=4),
+                in_=z.rearrange("p t (c e) -> p c t e", e=4),
+            )
+
+        round_pair(0, 0, PICKS, zs[1][:, 0:2, :], nc.scalar.copy)
         for m0, m1 in zip(CUTS, CUTS[1:]):
-            picked = work.tile([P, PACK, m1 - m0], F32, name="picked")
-            for t in range(PACK):
-                fetch(picked[:, t, :], PACK + t, m0, m1)
-            copy = nc.scalar.copy if m1 < PICKS else nc.vector.tensor_copy
-            quantise_z(1, m0, m1, round_z(picked[:], copy, "zgrouped", 2))
+            picked = work.tile([P, 2, m1 - m0], F32, name="picked")
+            for t in range(2):
+                fetch(picked[:, t, :], SLICES - 2 + t, m0, m1)
+            round_pair(2, m0, m1, picked[:], nc.scalar.copy if m1 - m0 == PIECE else nc.vector.tensor_copy)
+            quantise(grouped[:, m0:m1, :].rearrange("p m t -> p (m t)"), z_codes[:, 1, m0:m1], z_plane[:, 1, m0:m1])
         result = keep.tile([P, 2 * PIECES, N // P, P], F32, tag="wide", align_bytes=64)
         for c in range(2 * PIECES):
             last_product(accs[c], c, 1)
-            copy = nc.vector.tensor_copy if c == 2 * PIECES - 1 else nc.scalar.copy
+            copy = nc.vector.tensor_copy if c >= 6 else nc.scalar.copy
             copy(out=result[:, c], in_=accs[c][:])
             nc.sync.dma_start(out=out.rearrange("(n p) m -> p n m", p=P)[:, :, P * c : P * (c + 1)], in_=result[:, c])

@@ -30,6 +30,7 @@ PIECES = PICKS // PIECE
 CUTS = (0, 256, 512, 768, 896, 1024)
 LAG = 3
 PAGES = 2
+FUSED = SLICES - 2
 LAST = (SLICES - 1, HALF)
 
 
@@ -130,8 +131,8 @@ def tile_list_burst_derotation_kernel(
         nc.vector.tensor_copy(v_plane[:], tab_plane[:].indirect(idx[:]))
         w2_codes = keep.tile([P, 2 * H], U8, align_bytes=64)
         nc.vector.tensor_copy(
-            out=w2_codes[:].bitcast(U16).rearrange("p (b t m) -> p b m t", b=PASSES, t=PACK),
-            in_=w2_raw[:].bitcast(U16).rearrange("p (b m t) -> p b m t", b=PASSES, t=PACK),
+            out=w2_codes[:].bitcast(U16).rearrange("p (b t m) -> p b t m", b=PASSES, t=PACK),
+            in_=w2_raw[:].bitcast(U16).rearrange("p (b m t) -> p b t m", b=PASSES, t=PACK),
         )
         v_codes = []
 
@@ -143,10 +144,10 @@ def tile_list_burst_derotation_kernel(
         gather_words(0)
         w2_plane = keep.tile([P, H], U8, align_bytes=64)
         nc.vector.tensor_copy(
-            out=w2_plane[:].rearrange("p (b t m) -> p b m t", b=PASSES, t=PACK),
-            in_=w2_rows[:].rearrange("p (b m t) -> p b m t", b=PASSES, t=PACK),
+            out=w2_plane[:].rearrange("p (b t m) -> p b t m", b=PASSES, t=PACK),
+            in_=w2_rows[:].rearrange("p (b m t) -> p b t m", b=PASSES, t=PACK),
         )
-        quantise_weight(raw3[0], q3[0], 0, 2, nc.vector.tensor_copy, "grouped")
+        quantise_weight(raw3[0], q3[0], 0, 1, nc.vector.tensor_copy, "grouped")
         gather_words(1)
         for n in range(PAGES):
             clear_page(n)
@@ -248,12 +249,14 @@ def tile_list_burst_derotation_kernel(
         for u, (s, j0, j1) in enumerate(units):
             following = derotate(*units[u + 1]) if u + 1 < len(units) else None
             if u == 0:
+                quantise_weight(raw3[0], q3[0], 1, 2, nc.vector.tensor_copy, "grouped")
+            if u == 1:
                 quantise_weight(raw3[0], q3[0], 2, PACK, nc.vector.tensor_copy, "grouped")
             hsum = turn(room, j1 - j0)
             room = following
             if j0 == 0:
                 gained = work.tile([P, S], F32, name="gained", bufs=3)
-            if s < SLICES - 1:
+            if s < FUSED:
                 nc.vector.tensor_tensor(out=gained[:, j0:j1], in0=hsum, in1=gains[s % PACK][:, j0:j1], op=MULT)
             else:
                 nc.scalar.copy(out=gained[:, j0:j1], in_=hsum)
@@ -261,7 +264,7 @@ def tile_list_burst_derotation_kernel(
                 fetch(zs[(s - 1) // PACK][:, (s - 1) % PACK, :], s - 1, 0, PICKS)
             if s < 2:
                 place(s, j0, j1, gained)
-            elif j1 == S and s < SLICES - 1:
+            elif j1 == S and s < FUSED:
                 place(s, 0, S, gained)
             elif j1 == S:
                 nc.vector.tensor_tensor(pages[s % PAGES][:].indirect(idx2[:]), gained[:], gains[s % PACK], MULT)

@@ -28,8 +28,9 @@ HALF = S // 2
 PIECE = 256
 PIECES = PICKS // PIECE
 CUTS = (0, 256, 512, 768, 896, 1024)
-LAG = 3
 PAGES = 2
+HALVED = 4
+CASTS = ((1, 0), (2, 0))
 FUSED = SLICES - 2
 LAST = (SLICES - 1, HALF)
 
@@ -116,8 +117,8 @@ def tile_list_burst_derotation_kernel(
             plane = keep.tile([P, PASS], U8, name=name + "_plane", align_bytes=64)
             return codes, plane
 
-        def quantise_weight(raw, q, t0, t1, copy, tag):
-            grouped = work.tile([P, t1 - t0, P, PACK], BF16, name="grouped", tag=tag, align_bytes=64)
+        def quantise_weight(raw, q, t0, t1, copy, pool, tag):
+            grouped = pool.tile([P, t1 - t0, P, PACK], BF16, name="grouped", tag=tag, align_bytes=64)
             copy(
                 out=grouped[:].rearrange("p t m i -> p m i t"),
                 in_=raw.rearrange("p i (m t) -> p m i t", t=PACK)[:, :, :, t0:t1],
@@ -126,7 +127,7 @@ def tile_list_burst_derotation_kernel(
 
         q1 = [quantised_weight("w1a"), quantised_weight("w1b")]
         q3 = [quantised_weight("w3a"), quantised_weight("w3b")]
-        quantise_weight(raw1[0], q1[0], 0, PACK, nc.vector.tensor_copy, "grouped")
+        quantise_weight(raw1[0], q1[0], 0, PACK, nc.vector.tensor_copy, work, "grouped")
         v_plane = keep.tile([P, S], U8, align_bytes=64)
         nc.vector.tensor_copy(v_plane[:], tab_plane[:].indirect(idx[:]))
         w2_codes = keep.tile([P, 2 * H], U8, align_bytes=64)
@@ -147,7 +148,7 @@ def tile_list_burst_derotation_kernel(
             out=w2_plane[:].rearrange("p (b t m) -> p b t m", b=PASSES, t=PACK),
             in_=w2_rows[:].rearrange("p (b m t) -> p b t m", b=PASSES, t=PACK),
         )
-        quantise_weight(raw3[0], q3[0], 0, 1, nc.vector.tensor_copy, "grouped")
+        quantise_weight(raw3[0], q3[0], 0, 1, nc.vector.tensor_copy, work, "grouped")
         gather_words(1)
         for n in range(PAGES):
             clear_page(n)
@@ -175,9 +176,10 @@ def tile_list_burst_derotation_kernel(
                 return room[:]
             if j0 == HALF and s >= 1:
                 return zs[(s - 1) // PACK][:, (s - 1) % PACK, :]
-            if j0 == 0 and s >= LAG:
-                return refs[s - LAG]
-            room = work.tile([P, S], F32, name="room", align_bytes=64)
+            if (s, j0) in CASTS:
+                room = keep.tile([P, S], F32, name="room", tag="cast%d" % s, align_bytes=64)
+                return room[:]
+            room = work.tile([P, S], F32, name="room", bufs=3, align_bytes=64)
             return room[:]
 
         def derotate(s, j0, j1):
@@ -249,9 +251,9 @@ def tile_list_burst_derotation_kernel(
         for u, (s, j0, j1) in enumerate(units):
             following = derotate(*units[u + 1]) if u + 1 < len(units) else None
             if u == 0:
-                quantise_weight(raw3[0], q3[0], 1, 2, nc.vector.tensor_copy, "grouped")
+                quantise_weight(raw3[0], q3[0], 1, 2, nc.vector.tensor_copy, work, "grouped")
             if u == 1:
-                quantise_weight(raw3[0], q3[0], 2, PACK, nc.vector.tensor_copy, "grouped")
+                quantise_weight(raw3[0], q3[0], 2, PACK, nc.vector.tensor_copy, work, "grouped")
             hsum = turn(room, j1 - j0)
             room = following
             if j0 == 0:
@@ -262,7 +264,7 @@ def tile_list_burst_derotation_kernel(
                 nc.scalar.copy(out=gained[:, j0:j1], in_=hsum)
             if j1 == S and 1 <= s < SLICES - 1:
                 fetch(zs[(s - 1) // PACK][:, (s - 1) % PACK, :], s - 1, 0, PICKS)
-            if s < 2:
+            if s < HALVED:
                 place(s, j0, j1, gained)
             elif j1 == S and s < FUSED:
                 place(s, 0, S, gained)
@@ -272,9 +274,9 @@ def tile_list_burst_derotation_kernel(
                 for m0 in (0, HALF):
                     quantise_z(0, m0, m0 + HALF, round_z(zs[0][:, :, m0 : m0 + HALF], nc.scalar.copy, "pair", 3))
             if (s, j0) == (1, 0):
-                quantise_weight(raw1[1], q1[1], 0, PACK, nc.scalar.copy, "room")
+                quantise_weight(raw1[1], q1[1], 0, PACK, nc.scalar.copy, keep, "cast1")
             if (s, j0) == (2, 0):
-                quantise_weight(raw3[1], q3[1], 0, PACK, nc.scalar.copy, "room")
+                quantise_weight(raw3[1], q3[1], 0, PACK, nc.scalar.copy, keep, "cast2")
                 z1 = keep.tile([P, PACK, PICKS], F32, tag="later", align_bytes=64)
                 zs.append(z1)
 

@@ -29,6 +29,7 @@ PIECE = 256
 PIECES = PICKS // PIECE
 CUTS = (0, 256, 512, 768, 896, 1024)
 PAGES = 2
+SPLIT = 2
 HALVED = 4
 CASTS = ((1, 0), (2, 0))
 FUSED = SLICES - 2
@@ -211,8 +212,8 @@ def tile_list_burst_derotation_kernel(
             nc.scalar.copy(out=pair[:, first], in_=inph)
             nc.scalar.activation(out=trig[:, first], in_=size[:], func=ACT.Sin, scale=-1.0, bias=math.pi / 2)
             nc.scalar.copy(out=pair[:, second], in_=quad)
-            for half in (first, second):
-                nc.gpsimd.tensor_tensor(out=room[:, half], in0=pair[:, half], in1=trig[:, half], op=MULT)
+            for part in (first, second) if s < SPLIT else (slice(0, S),):
+                nc.gpsimd.tensor_tensor(out=room[:, part], in0=pair[:, part], in1=trig[:, part], op=MULT)
             return room
 
         def turn(room, width):
@@ -270,9 +271,6 @@ def tile_list_burst_derotation_kernel(
                 place(s, 0, S, gained)
             elif j1 == S:
                 nc.vector.tensor_tensor(pages[s % PAGES][:].indirect(idx2[:]), gained[:], gains[s % PACK], MULT)
-            if (s, j0) == (SLICES - 2, HALF):
-                for m0 in (0, HALF):
-                    quantise_z(0, m0, m0 + HALF, round_z(zs[0][:, :, m0 : m0 + HALF], nc.scalar.copy, "pair", 3))
             if (s, j0) == (1, 0):
                 quantise_weight(raw1[1], q1[1], 0, PACK, nc.scalar.copy, keep, "cast1")
             if (s, j0) == (2, 0):
@@ -280,6 +278,8 @@ def tile_list_burst_derotation_kernel(
                 z1 = keep.tile([P, PACK, PICKS], F32, tag="later", align_bytes=64)
                 zs.append(z1)
 
+        for m0 in (0, HALF):
+            quantise_z(0, m0, m0 + HALF, round_z(zs[0][:, :, m0 : m0 + HALF], nc.scalar.copy, "size", 2))
         refs.extend(load_ref(1, 2, "raw3a"))
         w4_codes = keep.tile([P, PASSES, N], I32, tag="w4", align_bytes=64)
         nc.sync.dma_start(out=w4_codes[:], in_=w4_words.rearrange("a p c i -> p a (c i)").bitcast(I32))

@@ -52,7 +52,7 @@ def tile_list_burst_derotation_kernel(
         psum = ctx.enter_context(tc.psum_pool(name="psum", bufs=1))
 
         tab_plane = keep.tile([P, T], U8, align_bytes=64)
-        nc.vector.memset(tab_plane[:].bitcast(I32), 0)
+        nc.gpsimd.memset(tab_plane[:].bitcast(I32), 0)
         w2_rows = keep.tile([P, H], U8, align_bytes=64)
         nc.vector.memset(w2_rows[:].bitcast(I32), 0)
         w4_plane = keep.tile([P, PASSES, N], U8, align_bytes=64)
@@ -67,47 +67,53 @@ def tile_list_burst_derotation_kernel(
         ident = keep.tile([P, P], F32)
         make_identity(nc, ident[:])
 
-        def load_weight(w, b, tag):
-            raw = keep.tile([P, PACK, PASS], F32, name="raw", tag=tag, align_bytes=64)
-            nc.sync.dma_start(out=raw[:], in_=w[:, PASS * b : PASS * (b + 1)].rearrange("(p i) c -> p i c", i=PACK))
+        def load_weight(w, c0, c1, tag):
+            raw = keep.tile([P, PACK, c1 - c0], F32, name="raw", tag=tag, align_bytes=64)
+            nc.sync.dma_start(out=raw[:], in_=w[:, c0:c1].rearrange("(p i) c -> p i c", i=PACK))
             return raw[:]
 
-        def load_gains(t0, t1):
+        def load_dealt_gains(t0, t1):
             rows = keep.tile([P, t1 - t0, S], F32, name="gains%d" % t0)
             for q in (0, 2, 1, 3):
                 nc.sync.dma_start(out=rows[32 * q : 32 * (q + 1)], in_=wgs.rearrange("(q t) j -> q t j", t=PACK)[:, t0:t1])
             return [rows[:, t, :] for t in range(t1 - t0)]
 
-        def load_ref(b, t0, tag):
+        def load_ref(view, t0, tag):
             rows = keep.tile([P, 2, PICKS], F32, name="rows", tag=tag, align_bytes=64)
-            nc.sync.dma_start(
-                out=rows[:], in_=ref[PASS * b : PASS * (b + 1)].rearrange("(p t) m -> p t m", t=PACK)[:, t0 : t0 + 2]
-            )
+            nc.sync.dma_start(out=rows[:], in_=view[:, t0 : t0 + 2])
             return [rows[:, 0, :], rows[:, 1, :]]
+
+        plain_ref = ref[0:PASS].rearrange("(t p) m -> p t m", p=P)
+        dealt_ref = ref[PASS:H].rearrange("(p t) m -> p t m", t=PACK)
 
         idx = lists.tile([P, S // 16], U16)
         nc.sync.dma_start(idx[:], offs)
-        raw1 = [load_weight(w1, 0, "raw1a")]
         w2_raw = keep.tile([P, 2 * H], U8, align_bytes=64)
         nc.sync.dma_start(out=w2_raw[:].bitcast(I32), in_=w2_words[0].bitcast(I32))
         load_scale_rows(nc.sync, tab_plane, tab_scales[0])
         tab = keep.tile([P, T], I32, tag="wide", align_bytes=64)
         nc.sync.dma_start(out=tab[:], in_=tab_words[0].rearrange("p t i -> p (t i)").bitcast(I32))
+        raw1 = [load_weight(w1, 0, P, "raw1a")]
+        raw3 = [load_weight(w3, 0, P, "raw3a")]
         load_scale_rows(nc.sync, w2_rows, w2_scales[0])
-        raw3 = [load_weight(w3, 0, "raw3a")]
         idx2 = lists.tile([P, S // 16], U16)
         nc.sync.dma_start(idx2[:], offs2)
-        gains = load_gains(0, 1)
+        plain_gains = keep.tile([P, S], F32)
+        nc.sync.dma_start(out=plain_gains[:, 0:HALF], in_=wgs[:, 0:HALF])
+        raw1.append(load_weight(w1, P, 2 * P, "raw1b"))
+        raw3.append(load_weight(w3, P, 2 * P, "raw3b"))
+        nc.sync.dma_start(out=plain_gains[:, HALF:S], in_=wgs[:, HALF:S])
+        raw1.append(load_weight(w1, 2 * P, PASS, "raw1c"))
+        raw3.append(load_weight(w3, 2 * P, PASS, "raw3c"))
+        idx3 = lists.tile([P, PICKS // 16], U16)
+        nc.sync.dma_start(idx3[:], offs3)
+        refs = load_ref(plain_ref, 0, "ref0")
         later = keep.tile([P, 2, PACK, PASS], F32, tag="later", align_bytes=64)
         for n, (w, raw) in enumerate(((w1, raw1), (w3, raw3))):
             nc.sync.dma_start(out=later[:, n], in_=w[:, PASS:H].rearrange("(p i) c -> p i c", i=PACK))
             raw.append(later[:, n])
-        gains.extend(load_gains(1, 2))
-        idx3 = lists.tile([P, PICKS // 16], U16)
-        nc.sync.dma_start(idx3[:], offs3)
-        refs = load_ref(0, 0, "ref0")
-        gains.extend(load_gains(2, PACK))
-        refs.extend(load_ref(0, 2, "ref1"))
+        refs.extend(load_ref(plain_ref, 2, "ref1"))
+        gains = [plain_gains[:]] * PACK + load_dealt_gains(0, 2) + load_dealt_gains(2, PACK)
         load_scale_rows(nc.sync, w4_plane, w4_scales.rearrange("a q n -> q a n"))
 
         def quantise(grouped, codes, plane):
@@ -118,23 +124,30 @@ def tile_list_burst_derotation_kernel(
             plane = keep.tile([P, PASS], U8, name=name + "_plane", align_bytes=64)
             return codes, plane
 
-        def quantise_weight(raw, q, t0, t1, copy, pool, tag):
-            grouped = pool.tile([P, t1 - t0, P, PACK], BF16, name="grouped", tag=tag, align_bytes=64)
-            copy(
-                out=grouped[:].rearrange("p t m i -> p m i t"),
-                in_=raw.rearrange("p i (m t) -> p m i t", t=PACK)[:, :, :, t0:t1],
+        def quantise_dealt(raw, q, tag):
+            grouped = keep.tile([P, PACK, P, PACK], BF16, name="grouped", tag=tag, align_bytes=64)
+            nc.scalar.copy(
+                out=grouped[:].rearrange("p t m i -> p m i t"), in_=raw.rearrange("p i (m t) -> p m i t", t=PACK)
             )
-            quantise(grouped[:].rearrange("p t m i -> p (t m i)"), q[0][:, P * t0 : P * t1], q[1][:, P * t0 : P * t1])
+            quantise(grouped[:].rearrange("p t m i -> p (t m i)"), q[0][:], q[1][:])
+
+        def gpsimd_copy(out, in_):
+            nc.gpsimd.tensor_scalar(out=out, in0=in_, scalar1=1.0, scalar2=0.0, op0=MULT, op1=ADD)
+
+        def quantise_plain(raw, q, c0, copy):
+            width = raw.shape[2]
+            grouped = work.tile([P, width, PACK], BF16, name="grouped", bufs=4, align_bytes=64)
+            copy(out=grouped[:], in_=raw.rearrange("p i c -> p c i"))
+            quantise(grouped[:].rearrange("p c i -> p (c i)"), q[0][:, c0 : c0 + width], q[1][:, c0 : c0 + width])
 
         q1 = [quantised_weight("w1a"), quantised_weight("w1b")]
         q3 = [quantised_weight("w3a"), quantised_weight("w3b")]
-        quantise_weight(raw1[0], q1[0], 0, PACK, nc.vector.tensor_copy, work, "grouped")
         v_plane = keep.tile([P, S], U8, align_bytes=64)
         nc.vector.tensor_copy(v_plane[:], tab_plane[:].indirect(idx[:]))
-        w2_codes = keep.tile([P, 2 * H], U8, align_bytes=64)
+        w2_dealt = keep.tile([P, 2 * PASS], U8, align_bytes=64)
         nc.vector.tensor_copy(
-            out=w2_codes[:].bitcast(U16).rearrange("p (b t m) -> p b t m", b=PASSES, t=PACK),
-            in_=w2_raw[:].bitcast(U16).rearrange("p (b m t) -> p b t m", b=PASSES, t=PACK),
+            out=w2_dealt[:].bitcast(U16).rearrange("p (t m) -> p t m", t=PACK),
+            in_=w2_raw[:, 2 * PASS : 2 * H].bitcast(U16).rearrange("p (m t) -> p t m", t=PACK),
         )
         v_codes = []
 
@@ -144,16 +157,17 @@ def tile_list_burst_derotation_kernel(
             v_codes.append(words)
 
         gather_words(0)
-        w2_plane = keep.tile([P, H], U8, align_bytes=64)
-        nc.vector.tensor_copy(
-            out=w2_plane[:].rearrange("p (b t m) -> p b t m", b=PASSES, t=PACK),
-            in_=w2_rows[:].rearrange("p (b m t) -> p b t m", b=PASSES, t=PACK),
-        )
-        quantise_weight(raw3[0], q3[0], 0, 1, nc.vector.tensor_copy, work, "grouped")
+        quantise_plain(raw1[0], q1[0], 0, nc.vector.tensor_copy)
+        quantise_plain(raw3[0], q3[0], 0, nc.vector.tensor_copy)
         gather_words(1)
+        w2_plane = keep.tile([P, PASS], U8, align_bytes=64)
+        nc.vector.tensor_copy(
+            out=w2_plane[:].rearrange("p (t m) -> p t m", t=PACK),
+            in_=w2_rows[:, PASS:H].rearrange("p (m t) -> p t m", t=PACK),
+        )
+        q2 = [(w2_raw, w2_rows), (w2_dealt, w2_plane)]
         for n in range(PAGES):
             clear_page(n)
-        refs.extend(load_ref(1, 0, "raw1a"))
         z0 = keep.tile([P, PACK, PICKS], F32, tag="wide", align_bytes=64)
         zs = [z0]
 
@@ -190,7 +204,7 @@ def tile_list_burst_derotation_kernel(
             phase = first_product(j0, j1, "phase", 2, q1[b][0][:, cols].bitcast(FP8X4), q1[b][1][:, cols])
             spare = (s, j0) == (0, PIECE)
             inph = first_product(
-                j0, j1, *(("hsum", 4) if spare else ("inph", 1)), w2_codes[:, 2 * P * s : 2 * P * (s + 1)].bitcast(FP4X4), w2_plane[:, P * s : P * (s + 1)]
+                j0, j1, *(("hsum", 4) if spare else ("inph", 1)), q2[b][0][:, 2 * P * t : 2 * P * (t + 1)].bitcast(FP4X4), q2[b][1][:, cols]
             )
             quad = first_product(j0, j1, *(("hsum", 4) if spare else ("quad", 1)), q3[b][0][:, cols].bitcast(FP8X4), q3[b][1][:, cols])
             size = work.tile([P, j1 - j0], F32, name="size", align_bytes=64)
@@ -206,7 +220,7 @@ def tile_list_burst_derotation_kernel(
             nc.scalar.activation(out=size[:], in_=phase, func=ACT.Abs)
             nc.scalar.activation(out=trig[:, second], in_=phase, func=ACT.Sin)
             if (s, j0) == LAST:
-                pair = keep.tile([P, S], F32, name="pair", tag="raw3a", align_bytes=64)
+                pair = keep.tile([P, S], F32, name="pair", tag="ref3", align_bytes=64)
             else:
                 pair = work.tile([P, S], F32, name="pair", bufs=3, align_bytes=64)
             nc.scalar.copy(out=pair[:, first], in_=inph)
@@ -252,35 +266,43 @@ def tile_list_burst_derotation_kernel(
         for u, (s, j0, j1) in enumerate(units):
             following = derotate(*units[u + 1]) if u + 1 < len(units) else None
             if u == 0:
-                quantise_weight(raw3[0], q3[0], 1, 2, nc.vector.tensor_copy, work, "grouped")
-            if u == 1:
-                quantise_weight(raw3[0], q3[0], 2, PACK, nc.vector.tensor_copy, work, "grouped")
+                quantise_plain(raw1[1], q1[0], P, gpsimd_copy)
+                quantise_plain(raw3[1], q3[0], P, gpsimd_copy)
+            if u == 2:
+                quantise_plain(raw1[2], q1[0], 2 * P, gpsimd_copy)
+                quantise_plain(raw3[2], q3[0], 2 * P, gpsimd_copy)
             hsum = turn(room, j1 - j0)
             room = following
             if j0 == 0:
                 gained = work.tile([P, S], F32, name="gained", bufs=3)
             if s < FUSED:
-                nc.vector.tensor_tensor(out=gained[:, j0:j1], in0=hsum, in1=gains[s % PACK][:, j0:j1], op=MULT)
+                nc.vector.tensor_tensor(out=gained[:, j0:j1], in0=hsum, in1=gains[s][:, j0:j1], op=MULT)
             else:
                 nc.scalar.copy(out=gained[:, j0:j1], in_=hsum)
             if j1 == S and 1 <= s < SLICES - 1:
                 fetch(zs[(s - 1) // PACK][:, (s - 1) % PACK, :], s - 1, 0, PICKS)
+                if s <= PACK:
+                    nc.sync.dma_start(out=out[P * (s - 1) : P * s, :], in_=z0[:, s - 1, :])
             if s < HALVED:
                 place(s, j0, j1, gained)
             elif j1 == S and s < FUSED:
                 place(s, 0, S, gained)
             elif j1 == S:
-                nc.vector.tensor_tensor(pages[s % PAGES][:].indirect(idx2[:]), gained[:], gains[s % PACK], MULT)
+                nc.vector.tensor_tensor(pages[s % PAGES][:].indirect(idx2[:]), gained[:], gains[s], MULT)
+            if (s, j1) == (2, S):
+                refs.extend(load_ref(dealt_ref, 0, "ref0"))
             if (s, j0) == (1, 0):
-                quantise_weight(raw1[1], q1[1], 0, PACK, nc.scalar.copy, keep, "cast1")
+                quantise_dealt(raw1[3], q1[1], "cast1")
             if (s, j0) == (2, 0):
-                quantise_weight(raw3[1], q3[1], 0, PACK, nc.scalar.copy, keep, "cast2")
+                quantise_dealt(raw3[3], q3[1], "cast2")
                 z1 = keep.tile([P, PACK, PICKS], F32, tag="later", align_bytes=64)
                 zs.append(z1)
 
+        z_back = keep.tile([P, PACK, PICKS], F32, tag="wide", align_bytes=64)
+        nc.sync.dma_start(out=z_back[:], in_=out.rearrange("(p t) m -> p t m", t=PACK))
         for m0 in (0, HALF):
-            quantise_z(0, m0, m0 + HALF, round_z(zs[0][:, :, m0 : m0 + HALF], nc.scalar.copy, "size", 2))
-        refs.extend(load_ref(1, 2, "raw3a"))
+            quantise_z(0, m0, m0 + HALF, round_z(z_back[:, :, m0 : m0 + HALF], nc.scalar.copy, "size", 2))
+        refs.extend(load_ref(dealt_ref, 2, "ref3"))
         w4_codes = keep.tile([P, PASSES, N], I32, tag="w4", align_bytes=64)
         nc.sync.dma_start(out=w4_codes[:], in_=w4_words.rearrange("a p c i -> p a (c i)").bitcast(I32))
         banks = [("phase", 2), ("phase", 2), ("inph", 1), ("quad", 1)] + [("hsum", 4)] * 4

@@ -52,7 +52,7 @@ def tile_list_burst_derotation_kernel(
         psum = ctx.enter_context(tc.psum_pool(name="psum", bufs=1))
 
         tab_plane = keep.tile([P, T], U8, align_bytes=64)
-        nc.gpsimd.memset(tab_plane[:].bitcast(I32), 0)
+        nc.vector.memset(tab_plane[:].bitcast(I32), 0)
         w2_rows = keep.tile([P, H], U8, align_bytes=64)
         nc.vector.memset(w2_rows[:].bitcast(I32), 0)
         w4_plane = keep.tile([P, PASSES, N], U8, align_bytes=64)
@@ -90,14 +90,14 @@ def tile_list_burst_derotation_kernel(
         nc.sync.dma_start(idx[:], offs)
         w2_raw = keep.tile([P, 2 * H], U8, align_bytes=64)
         nc.sync.dma_start(out=w2_raw[:].bitcast(I32), in_=w2_words[0].bitcast(I32))
+        idx2 = lists.tile([P, S // 16], U16)
+        nc.sync.dma_start(idx2[:], offs2)
         load_scale_rows(nc.sync, tab_plane, tab_scales[0])
         tab = keep.tile([P, T], I32, tag="wide", align_bytes=64)
         nc.sync.dma_start(out=tab[:], in_=tab_words[0].rearrange("p t i -> p (t i)").bitcast(I32))
         raw1 = [load_weight(w1, 0, P, "raw1a")]
         raw3 = [load_weight(w3, 0, P, "raw3a")]
         load_scale_rows(nc.sync, w2_rows, w2_scales[0])
-        idx2 = lists.tile([P, S // 16], U16)
-        nc.sync.dma_start(idx2[:], offs2)
         plain_gains = keep.tile([P, S], F32)
         nc.sync.dma_start(out=plain_gains[:, 0:HALF], in_=wgs[:, 0:HALF])
         raw1.append(load_weight(w1, P, 2 * P, "raw1b"))
@@ -130,9 +130,6 @@ def tile_list_burst_derotation_kernel(
                 out=grouped[:].rearrange("p t m i -> p m i t"), in_=raw.rearrange("p i (m t) -> p m i t", t=PACK)
             )
             quantise(grouped[:].rearrange("p t m i -> p (t m i)"), q[0][:], q[1][:])
-
-        def gpsimd_copy(out, in_):
-            nc.gpsimd.tensor_scalar(out=out, in0=in_, scalar1=1.0, scalar2=0.0, op0=MULT, op1=ADD)
 
         def quantise_plain(raw, q, c0, copy):
             width = raw.shape[2]
@@ -266,11 +263,11 @@ def tile_list_burst_derotation_kernel(
         for u, (s, j0, j1) in enumerate(units):
             following = derotate(*units[u + 1]) if u + 1 < len(units) else None
             if u == 0:
-                quantise_plain(raw1[1], q1[0], P, gpsimd_copy)
-                quantise_plain(raw3[1], q3[0], P, gpsimd_copy)
+                quantise_plain(raw1[1], q1[0], P, nc.scalar.copy)
+                quantise_plain(raw3[1], q3[0], P, nc.scalar.copy)
             if u == 2:
-                quantise_plain(raw1[2], q1[0], 2 * P, gpsimd_copy)
-                quantise_plain(raw3[2], q3[0], 2 * P, gpsimd_copy)
+                quantise_plain(raw1[2], q1[0], 2 * P, nc.scalar.copy)
+                quantise_plain(raw3[2], q3[0], 2 * P, nc.scalar.copy)
             hsum = turn(room, j1 - j0)
             room = following
             if j0 == 0:

@@ -26,14 +26,15 @@ PASSES = H // PASS
 SLICES = H // P
 HALF = S // 2
 PIECE = 256
-PIECES = PICKS // PIECE
 CUTS = (0, 256, 512, 768, 896, 1024)
 PAGES = 2
 SPLIT = 2
-HALVED = 4
-CASTS = ((1, 0), (2, 0))
-FUSED = SLICES - 2
-LAST = (SLICES - 1, HALF)
+HALVED = 2
+CASTS = ((2, 0), (3, 0))
+FINAL = SLICES - 1
+ROUNDS = ((6, HALF), (7, 0))
+SCALAR_ROUNDS = 512
+VECTOR_BANKS = (6, 7)
 
 
 def load_scale_rows(queue, plane, rows):
@@ -113,7 +114,9 @@ def tile_list_burst_derotation_kernel(
             nc.sync.dma_start(out=later[:, n], in_=w[:, PASS:H].rearrange("(p i) c -> p i c", i=PACK))
             raw.append(later[:, n])
         refs.extend(load_ref(plain_ref, 2, "ref1"))
-        gains = [plain_gains[:]] * PACK + load_dealt_gains(0, 2) + load_dealt_gains(2, PACK)
+        gains = [plain_gains[:]] * PACK + load_dealt_gains(0, 2)
+        refs.extend(load_ref(dealt_ref, 0, "ref2"))
+        gains.extend(load_dealt_gains(2, PACK))
         load_scale_rows(nc.sync, w4_plane, w4_scales.rearrange("a q n -> q a n"))
 
         def quantise(grouped, codes, plane):
@@ -131,9 +134,9 @@ def tile_list_burst_derotation_kernel(
             )
             quantise(grouped[:].rearrange("p t m i -> p (t m i)"), q[0][:], q[1][:])
 
-        def quantise_plain(raw, q, c0, copy):
+        def quantise_plain(raw, q, c0, copy, tag="grouped"):
             width = raw.shape[2]
-            grouped = work.tile([P, width, PACK], BF16, name="grouped", bufs=4, align_bytes=64)
+            grouped = work.tile([P, width, PACK], BF16, name="grouped", tag=tag, bufs=4 if tag == "grouped" else 1, align_bytes=64)
             copy(out=grouped[:], in_=raw.rearrange("p i c -> p c i"))
             quantise(grouped[:].rearrange("p c i -> p (c i)"), q[0][:, c0 : c0 + width], q[1][:, c0 : c0 + width])
 
@@ -149,13 +152,13 @@ def tile_list_burst_derotation_kernel(
         v_codes = []
 
         def gather_words(g):
-            words = keep.tile([P, HALF], U32, name="v_codes%d" % g, align_bytes=64)
+            words = work.tile([P, HALF], U32, name="v_codes%d" % g, bufs=1, align_bytes=64)
             nc.vector.tensor_copy(words[:], tab[:].bitcast(U32).indirect(idx[:, 32 * g : 32 * g + 32]))
             v_codes.append(words)
 
         gather_words(0)
         quantise_plain(raw1[0], q1[0], 0, nc.vector.tensor_copy)
-        quantise_plain(raw3[0], q3[0], 0, nc.vector.tensor_copy)
+        quantise_plain(raw3[0], q3[0], 0, nc.vector.tensor_copy, "v_codes1")
         gather_words(1)
         w2_plane = keep.tile([P, PASS], U8, align_bytes=64)
         nc.vector.tensor_copy(
@@ -182,17 +185,27 @@ def tile_list_burst_derotation_kernel(
                 )
             return bank[:]
 
+        pairs = []
+
         def product_room(s, j0):
-            if (s, j0) == LAST:
-                room = keep.tile([P, S], F32, name="room", tag="w4", align_bytes=64)
-                return room[:]
+            if j0 == 0 and s >= PAGES:
+                return refs[s - PAGES]
             if j0 == HALF and s >= 1:
-                return zs[(s - 1) // PACK][:, (s - 1) % PACK, :]
-            if (s, j0) in CASTS:
-                room = keep.tile([P, S], F32, name="room", tag="cast%d" % s, align_bytes=64)
-                return room[:]
-            room = work.tile([P, S], F32, name="room", bufs=3, align_bytes=64)
+                return pairs[-1]
+            room = work.tile([P, S], F32, name="room", align_bytes=64)
             return room[:]
+
+        def pair_room(s, j0):
+            if j0 == HALF and 1 <= s < FINAL:
+                return zs[(s - 1) // PACK][:, (s - 1) % PACK, :]
+            if (s, j0) == (FINAL, HALF):
+                pair = keep.tile([P, S], F32, name="pair", tag="ref3", align_bytes=64)
+                return pair[:]
+            if (s, j0) == (FINAL, 0):
+                pair = keep.tile([P, S], F32, name="pair", tag="z0_codes", align_bytes=64)
+                return pair[:]
+            pair = work.tile([P, S], F32, name="pair", align_bytes=64)
+            return pair[:]
 
         def derotate(s, j0, j1):
             b, t = divmod(s, PACK)
@@ -201,25 +214,26 @@ def tile_list_burst_derotation_kernel(
             phase = first_product(j0, j1, "phase", 2, q1[b][0][:, cols].bitcast(FP8X4), q1[b][1][:, cols])
             spare = (s, j0) == (0, PIECE)
             inph = first_product(
-                j0, j1, *(("hsum", 4) if spare else ("inph", 1)), q2[b][0][:, 2 * P * t : 2 * P * (t + 1)].bitcast(FP4X4), q2[b][1][:, cols]
+                j0, j1, *(("hsum", 4) if spare else ("inph", 1)),
+                q2[b][0][:, 2 * P * t : 2 * P * (t + 1)].bitcast(FP4X4), q2[b][1][:, cols],
             )
-            quad = first_product(j0, j1, *(("hsum", 4) if spare else ("quad", 1)), q3[b][0][:, cols].bitcast(FP8X4), q3[b][1][:, cols])
+            quad = first_product(
+                j0, j1, *(("hsum", 4) if spare else ("quad", 1)), q3[b][0][:, cols].bitcast(FP8X4), q3[b][1][:, cols]
+            )
             size = work.tile([P, j1 - j0], F32, name="size", align_bytes=64)
             trig = work.tile([P, S], F32, name="trig", bufs=3)
             room = product_room(s, j0)
-            if j1 - j0 < HALF:
+            if (s, j0) in ((0, 0), (0, PIECE), (0, HALF)):
                 nc.scalar.activation(out=trig[:, second], in_=phase, func=ACT.Sin)
                 nc.scalar.activation(out=size[:], in_=phase, func=ACT.Abs)
                 nc.scalar.activation(out=trig[:, first], in_=size[:], func=ACT.Sin, scale=-1.0, bias=math.pi / 2)
                 nc.vector.tensor_tensor(out=room[:, first], in0=inph, in1=trig[:, first], op=MULT)
                 nc.vector.tensor_tensor(out=room[:, second], in0=quad, in1=trig[:, second], op=MULT)
                 return room
+            pair = pair_room(s, j0)
+            pairs.append(pair)
             nc.scalar.activation(out=size[:], in_=phase, func=ACT.Abs)
             nc.scalar.activation(out=trig[:, second], in_=phase, func=ACT.Sin)
-            if (s, j0) == LAST:
-                pair = keep.tile([P, S], F32, name="pair", tag="ref3", align_bytes=64)
-            else:
-                pair = work.tile([P, S], F32, name="pair", bufs=3, align_bytes=64)
             nc.scalar.copy(out=pair[:, first], in_=inph)
             nc.scalar.activation(out=trig[:, first], in_=size[:], func=ACT.Sin, scale=-1.0, bias=math.pi / 2)
             nc.scalar.copy(out=pair[:, second], in_=quad)
@@ -244,101 +258,111 @@ def tile_list_burst_derotation_kernel(
                 dst, pages[s % PAGES][:].indirect(idx3[:, m0 // 16 : m1 // 16]), refs[s][:, m0:m1], ADD
             )
 
-        z_codes = keep.tile([P, PASSES, PICKS], U32, align_bytes=64)
-        z_plane = keep.tile([P, PASSES, PICKS], U8, align_bytes=64)
-
-        def round_z(z, copy, tag, bufs):
-            grouped = work.tile([P, z.shape[2] * PACK], BF16, name="zgrouped", tag=tag, bufs=bufs, align_bytes=64)
-            copy(
+        def round_z(z, tag):
+            grouped = keep.tile([P, z.shape[2] * PACK], BF16, name="zgrouped", tag=tag, align_bytes=64)
+            nc.scalar.copy(
                 out=grouped[:].rearrange("p (c e t) -> p c t e", e=4, t=PACK),
                 in_=z.rearrange("p t (c e) -> p c t e", e=4),
             )
             return grouped
 
-        def quantise_z(b, m0, m1, grouped):
-            quantise(grouped[:], z_codes[:, b, m0:m1], z_plane[:, b, m0:m1])
+        pieces = list(zip(CUTS, CUTS[1:]))
+        grouped = [keep.tile([P, m1 - m0, PACK], BF16, name="grouped%d" % m0, align_bytes=64) for m0, m1 in pieces]
 
+        def round_pair(n, t0, z, copy):
+            copy(
+                out=grouped[n][:, :, t0 : t0 + 2].rearrange("p (c e) t -> p c t e", e=4),
+                in_=z.rearrange("p t (c e) -> p c t e", e=4),
+            )
+
+        z0_rounded = []
         units = [(0, 0, PIECE), (0, PIECE, HALF)] + [(s, j0, j0 + HALF) for s in range(SLICES) for j0 in (0, HALF)][1:]
+        last_h = keep.tile([P, S], F32)
         room = derotate(*units[0])
         for u, (s, j0, j1) in enumerate(units):
+            if (s, j0) in ROUNDS:
+                m0 = HALF * len(z0_rounded)
+                z0_rounded.append(round_z(z_back[:, :, m0 : m0 + HALF], "cast%d" % (1 + len(z0_rounded))))
             following = derotate(*units[u + 1]) if u + 1 < len(units) else None
             if u == 0:
-                quantise_plain(raw1[1], q1[0], P, nc.scalar.copy)
-                quantise_plain(raw3[1], q3[0], P, nc.scalar.copy)
-            if u == 2:
+                quantise_plain(raw1[1], q1[0], P, nc.vector.tensor_copy)
+                quantise_plain(raw3[1], q3[0], P, nc.vector.tensor_copy)
+            if u == 3:
                 quantise_plain(raw1[2], q1[0], 2 * P, nc.scalar.copy)
                 quantise_plain(raw3[2], q3[0], 2 * P, nc.scalar.copy)
+            if (s, j0) == (FINAL, 0):
+                for n, (m0, m1) in enumerate(pieces):
+                    round_pair(n, 0, z1[:, :, m0:m1], nc.scalar.copy)
             hsum = turn(room, j1 - j0)
             room = following
-            if j0 == 0:
-                gained = work.tile([P, S], F32, name="gained", bufs=3)
-            if s < FUSED:
-                nc.vector.tensor_tensor(out=gained[:, j0:j1], in0=hsum, in1=gains[s][:, j0:j1], op=MULT)
+            if s == FINAL:
+                nc.scalar.copy(out=last_h[:, j0:j1], in_=hsum)
             else:
-                nc.scalar.copy(out=gained[:, j0:j1], in_=hsum)
-            if j1 == S and 1 <= s < SLICES - 1:
+                if j0 == 0:
+                    gained = work.tile([P, S], F32, name="gained")
+                nc.vector.tensor_tensor(out=gained[:, j0:j1], in0=hsum, in1=gains[s][:, j0:j1], op=MULT)
+            if j0 == 0 and 1 <= s < FINAL:
                 fetch(zs[(s - 1) // PACK][:, (s - 1) % PACK, :], s - 1, 0, PICKS)
                 if s <= PACK:
                     nc.sync.dma_start(out=out[P * (s - 1) : P * s, :], in_=z0[:, s - 1, :])
+            if (s, j0) == (PACK, 0):
+                z_back = keep.tile([P, PACK, PICKS], F32, tag="wide", align_bytes=64)
+                nc.sync.dma_start(out=z_back[:], in_=out.rearrange("(p t) m -> p t m", t=PACK))
             if s < HALVED:
                 place(s, j0, j1, gained)
-            elif j1 == S and s < FUSED:
+            elif j1 == S and s < FINAL:
                 place(s, 0, S, gained)
-            elif j1 == S:
-                nc.vector.tensor_tensor(pages[s % PAGES][:].indirect(idx2[:]), gained[:], gains[s], MULT)
-            if (s, j1) == (2, S):
-                refs.extend(load_ref(dealt_ref, 0, "ref0"))
-            if (s, j0) == (1, 0):
+            if (s, j0) == CASTS[0]:
                 quantise_dealt(raw1[3], q1[1], "cast1")
-            if (s, j0) == (2, 0):
+            if (s, j0) == CASTS[1]:
                 quantise_dealt(raw3[3], q3[1], "cast2")
-                z1 = keep.tile([P, PACK, PICKS], F32, tag="later", align_bytes=64)
+                z1 = keep.tile([P, 2, PICKS], F32, tag="later", align_bytes=64)
                 zs.append(z1)
 
-        z_back = keep.tile([P, PACK, PICKS], F32, tag="wide", align_bytes=64)
-        nc.sync.dma_start(out=z_back[:], in_=out.rearrange("(p t) m -> p t m", t=PACK))
-        for m0 in (0, HALF):
-            quantise_z(0, m0, m0 + HALF, round_z(z_back[:, :, m0 : m0 + HALF], nc.scalar.copy, "size", 2))
         refs.extend(load_ref(dealt_ref, 2, "ref3"))
-        w4_codes = keep.tile([P, PASSES, N], I32, tag="w4", align_bytes=64)
+        z0_codes = keep.tile([P, PICKS], U32, align_bytes=64)
+        z1_codes = keep.tile([P, PICKS], U32, align_bytes=64)
+        z_codes = [z0_codes, z1_codes]
+        z_plane = keep.tile([P, PASSES, PICKS], U8, align_bytes=64)
+        for m0, rounded in zip((0, HALF), z0_rounded):
+            quantise(rounded[:], z0_codes[:, m0 : m0 + HALF], z_plane[:, 0, m0 : m0 + HALF])
+        nc.vector.tensor_tensor(pages[FINAL % PAGES][:].indirect(idx2[:]), last_h[:], gains[FINAL], MULT)
+        w4_codes = keep.tile([P, PASSES, N], I32, align_bytes=64)
         nc.sync.dma_start(out=w4_codes[:], in_=w4_words.rearrange("a p c i -> p a (c i)").bitcast(I32))
         banks = [("phase", 2), ("phase", 2), ("inph", 1), ("quad", 1)] + [("hsum", 4)] * 4
 
-        def last_product(acc, c, b):
-            for n in range(N // P):
+        def last_product(c, b, m0, m1):
+            base = PIECE * (c // 2)
+            for n in range(2):
+                rows = slice(P * (2 * (c % 2) + n), P * (2 * (c % 2) + n + 1))
                 nc.tensor.matmul_mx(
-                    out=acc[:, n, :],
-                    lhsT=w4_codes[:, b, P * n : P * (n + 1)].bitcast(FP8X4),
-                    lhsT_scale=w4_plane[:, b, P * n : P * (n + 1)],
-                    rhs=z_codes[:, b, P * c : P * (c + 1)].bitcast(FP8X4),
-                    rhs_scale=z_plane[:, b, P * c : P * (c + 1)],
+                    out=accs[c][:, n, m0 - base : m1 - base],
+                    lhsT=w4_codes[:, b, rows].bitcast(FP8X4),
+                    lhsT_scale=w4_plane[:, b, rows],
+                    rhs=z_codes[b][:, m0:m1].bitcast(FP8X4),
+                    rhs_scale=z_plane[:, b, m0:m1],
                     start=(b == 0 and n == 0),
-                    stop=(b == PASSES - 1 and n == N // P - 1),
+                    stop=(b == PASSES - 1 and n == 1 and m1 == base + PIECE),
                 )
 
         accs = []
         for c, (tag, bufs) in enumerate(banks):
-            acc = psum.tile([P, N // P, P], F32, name="acc", tag=tag, bufs=bufs)
-            last_product(acc, c, 0)
+            acc = psum.tile([P, 2, PIECE], F32, name="acc", tag=tag, bufs=bufs)
             accs.append(acc)
-        grouped = keep.tile([P, PICKS, PACK], BF16, align_bytes=64)
-
-        def round_pair(t0, m0, m1, z, copy):
-            copy(
-                out=grouped[:, m0:m1, t0 : t0 + 2].rearrange("p (c e) t -> p c t e", e=4),
-                in_=z.rearrange("p t (c e) -> p c t e", e=4),
-            )
-
-        round_pair(0, 0, PICKS, zs[1][:, 0:2, :], nc.scalar.copy)
-        for m0, m1 in zip(CUTS, CUTS[1:]):
+            last_product(c, 0, PIECE * (c // 2), PIECE * (c // 2 + 1))
+        result = keep.tile([P, len(banks), 2, PIECE], F32, tag="wide", align_bytes=64)
+        for n, (m0, m1) in enumerate(pieces):
             picked = work.tile([P, 2, m1 - m0], F32, name="picked")
             for t in range(2):
-                fetch(picked[:, t, :], SLICES - 2 + t, m0, m1)
-            round_pair(2, m0, m1, picked[:], nc.scalar.copy if m1 - m0 == PIECE else nc.vector.tensor_copy)
-            quantise(grouped[:, m0:m1, :].rearrange("p m t -> p (m t)"), z_codes[:, 1, m0:m1], z_plane[:, 1, m0:m1])
-        result = keep.tile([P, 2 * PIECES, N // P, P], F32, tag="wide", align_bytes=64)
-        for c in range(2 * PIECES):
-            last_product(accs[c], c, 1)
-            copy = nc.vector.tensor_copy if c >= 6 else nc.scalar.copy
-            copy(out=result[:, c], in_=accs[c][:])
-            nc.sync.dma_start(out=out.rearrange("(n p) m -> p n m", p=P)[:, :, P * c : P * (c + 1)], in_=result[:, c])
+                fetch(picked[:, t, :], FINAL - 1 + t, m0, m1)
+            round_pair(n, 2, picked[:], nc.scalar.copy if m0 < SCALAR_ROUNDS else nc.vector.tensor_copy)
+            quantise(grouped[n][:].rearrange("p m t -> p (m t)"), z1_codes[:, m0:m1], z_plane[:, 1, m0:m1])
+            for c in (2 * (m0 // PIECE), 2 * (m0 // PIECE) + 1):
+                last_product(c, 1, m0, m1)
+                if m1 % PIECE == 0:
+                    copy = nc.vector.tensor_copy if c in VECTOR_BANKS else nc.scalar.copy
+                    copy(out=result[:, c], in_=accs[c][:])
+                    nc.sync.dma_start(
+                        out=out.rearrange("(n p) m -> p n m", p=P)[:, 2 * (c % 2) : 2 * (c % 2) + 2, PIECE * (c // 2) : PIECE * (c // 2 + 1)],
+                        in_=result[:, c],
+                    )

@@ -37,6 +37,10 @@ SCALAR_ROUNDS = 512
 VECTOR_BANKS = (6, 7)
 
 
+def page_of(s):
+    return 1 if s in (0, FINAL) else 0
+
+
 def load_scale_rows(queue, plane, rows):
     for q in range(4):
         queue.dma_start(out=plane[32 * q : 32 * q + 4].bitcast(I32), in_=rows[4 * q : 4 * q + 4].bitcast(I32))
@@ -251,11 +255,11 @@ def tile_list_burst_derotation_kernel(
             return hsum[:]
 
         def place(s, j0, j1, gained):
-            nc.vector.tensor_copy(pages[s % PAGES][:].indirect(idx2[:, j0 // 16 : j1 // 16]), gained[:, j0:j1])
+            nc.vector.tensor_copy(pages[page_of(s)][:].indirect(idx2[:, j0 // 16 : j1 // 16]), gained[:, j0:j1])
 
         def fetch(dst, s, m0, m1):
             nc.vector.tensor_tensor(
-                dst, pages[s % PAGES][:].indirect(idx3[:, m0 // 16 : m1 // 16]), refs[s][:, m0:m1], ADD
+                dst, pages[page_of(s)][:].indirect(idx3[:, m0 // 16 : m1 // 16]), refs[s][:, m0:m1], ADD
             )
 
         def round_z(z, tag):
@@ -287,9 +291,9 @@ def tile_list_burst_derotation_kernel(
             if u == 0:
                 quantise_plain(raw1[1], q1[0], P, nc.vector.tensor_copy)
                 quantise_plain(raw3[1], q3[0], P, nc.vector.tensor_copy)
-            if u == 3:
+            if u == 1:
                 quantise_plain(raw1[2], q1[0], 2 * P, nc.scalar.copy)
-                quantise_plain(raw3[2], q3[0], 2 * P, nc.scalar.copy)
+                quantise_plain(raw3[2], q3[0], 2 * P, nc.scalar.copy, "early")
             if (s, j0) == (FINAL, 0):
                 for n, (m0, m1) in enumerate(pieces):
                     round_pair(n, 0, z1[:, :, m0:m1], nc.scalar.copy)
@@ -298,7 +302,9 @@ def tile_list_burst_derotation_kernel(
             if s == FINAL:
                 nc.scalar.copy(out=last_h[:, j0:j1], in_=hsum)
             else:
-                if j0 == 0:
+                if (s, j0) == (1, 0):
+                    gained = work.tile([P, S], F32, name="gained", tag="early", bufs=1, align_bytes=64)
+                elif j0 == 0:
                     gained = work.tile([P, S], F32, name="gained")
                 nc.vector.tensor_tensor(out=gained[:, j0:j1], in0=hsum, in1=gains[s][:, j0:j1], op=MULT)
             if j0 == 0 and 1 <= s < FINAL:
@@ -326,7 +332,7 @@ def tile_list_burst_derotation_kernel(
         z_plane = keep.tile([P, PASSES, PICKS], U8, align_bytes=64)
         for m0, rounded in zip((0, HALF), z0_rounded):
             quantise(rounded[:], z0_codes[:, m0 : m0 + HALF], z_plane[:, 0, m0 : m0 + HALF])
-        nc.vector.tensor_tensor(pages[FINAL % PAGES][:].indirect(idx2[:]), last_h[:], gains[FINAL], MULT)
+        nc.vector.tensor_tensor(pages[page_of(FINAL)][:].indirect(idx2[:]), last_h[:], gains[FINAL], MULT)
         w4_codes = keep.tile([P, PASSES, N], I32, align_bytes=64)
         nc.sync.dma_start(out=w4_codes[:], in_=w4_words.rearrange("a p c i -> p a (c i)").bitcast(I32))
         banks = [("phase", 2), ("phase", 2), ("inph", 1), ("quad", 1)] + [("hsum", 4)] * 4

@@ -28,17 +28,12 @@ HALF = S // 2
 PIECE = 256
 CUTS = (0, 256, 512, 768, 896, 1024)
 PAGES = 2
-SPLIT = 2
-HALVED = 2
-CASTS = ((2, 0), (3, 0))
 FINAL = SLICES - 1
-ROUNDS = ((6, HALF), (7, 0))
+SHARE = 512
+DEALT_CASTS = {2: 0, 3: 2}
+ROUNDS = {5: 0, 6: HALF}
 SCALAR_ROUNDS = 512
 VECTOR_BANKS = (6, 7)
-
-
-def page_of(s):
-    return 1 if s in (0, FINAL) else 0
 
 
 def load_scale_rows(queue, plane, rows):
@@ -53,8 +48,11 @@ def tile_list_burst_derotation_kernel(
     with ExitStack() as ctx:
         lists = ctx.enter_context(tc.tile_pool(name="lists", bufs=1))
         keep = ctx.enter_context(tc.tile_pool(name="keep", bufs=1))
-        work = ctx.enter_context(tc.tile_pool(name="work", bufs=2))
         psum = ctx.enter_context(tc.psum_pool(name="psum", bufs=1))
+
+        def sbuf(shape, dtype, tag, bufs=1):
+            tile = keep.tile(shape, dtype, name=tag, tag=tag, bufs=bufs, align_bytes=64)
+            return tile[:]
 
         tab_plane = keep.tile([P, T], U8, align_bytes=64)
         nc.vector.memset(tab_plane[:].bitcast(I32), 0)
@@ -107,16 +105,17 @@ def tile_list_burst_derotation_kernel(
         nc.sync.dma_start(out=plain_gains[:, 0:HALF], in_=wgs[:, 0:HALF])
         raw1.append(load_weight(w1, P, 2 * P, "raw1b"))
         raw3.append(load_weight(w3, P, 2 * P, "raw3b"))
+        raw1.append(load_weight(w1, 2 * P, 3 * P, "raw1c"))
+        raw3.append(load_weight(w3, 2 * P, 3 * P, "raw3c"))
         nc.sync.dma_start(out=plain_gains[:, HALF:S], in_=wgs[:, HALF:S])
-        raw1.append(load_weight(w1, 2 * P, PASS, "raw1c"))
-        raw3.append(load_weight(w3, 2 * P, PASS, "raw3c"))
+        raw1.append(load_weight(w1, 3 * P, PASS, "raw1d"))
+        raw3.append(load_weight(w3, 3 * P, PASS, "raw3d"))
         idx3 = lists.tile([P, PICKS // 16], U16)
         nc.sync.dma_start(idx3[:], offs3)
         refs = load_ref(plain_ref, 0, "ref0")
         later = keep.tile([P, 2, PACK, PASS], F32, tag="later", align_bytes=64)
-        for n, (w, raw) in enumerate(((w1, raw1), (w3, raw3))):
+        for n, w in enumerate((w1, w3)):
             nc.sync.dma_start(out=later[:, n], in_=w[:, PASS:H].rearrange("(p i) c -> p i c", i=PACK))
-            raw.append(later[:, n])
         refs.extend(load_ref(plain_ref, 2, "ref1"))
         gains = [plain_gains[:]] * PACK + load_dealt_gains(0, 2)
         refs.extend(load_ref(dealt_ref, 0, "ref2"))
@@ -126,57 +125,60 @@ def tile_list_burst_derotation_kernel(
         def quantise(grouped, codes, plane):
             nc.vector.quantize_mx(out=codes.bitcast(FP8X4), scales=plane, in_=grouped)
 
+        def gpsimd_round(out, in_):
+            nc.gpsimd.tensor_scalar(out=out, in0=in_, scalar1=1.0, scalar2=0.0, op0=MULT, op1=ADD)
+
         def quantised_weight(name):
-            codes = keep.tile([P, PASS], U32, name=name + "_codes", align_bytes=64)
-            plane = keep.tile([P, PASS], U8, name=name + "_plane", align_bytes=64)
-            return codes, plane
+            return sbuf([P, PASS], U32, name + "_codes"), sbuf([P, PASS], U8, name + "_plane")
 
-        def quantise_dealt(raw, q, tag):
-            grouped = keep.tile([P, PACK, P, PACK], BF16, name="grouped", tag=tag, align_bytes=64)
+        def quantise_dealt(raw, q, t0, room):
+            grouped = room.bitcast(BF16).rearrange("p (t m i) -> p t m i", t=2, i=PACK)
             nc.scalar.copy(
-                out=grouped[:].rearrange("p t m i -> p m i t"), in_=raw.rearrange("p i (m t) -> p m i t", t=PACK)
+                out=grouped.rearrange("p t m i -> p m i t"),
+                in_=raw.rearrange("p i (m t) -> p m i t", t=PACK)[:, :, :, t0 : t0 + 2],
             )
-            quantise(grouped[:].rearrange("p t m i -> p (t m i)"), q[0][:], q[1][:])
+            cols = slice(P * t0, P * (t0 + 2))
+            quantise(grouped.rearrange("p t m i -> p (t m i)"), q[0][:, cols], q[1][:, cols])
 
-        def quantise_plain(raw, q, c0, copy, tag="grouped"):
+        def quantise_plain(raw, q, c0, copy, tag):
             width = raw.shape[2]
-            grouped = work.tile([P, width, PACK], BF16, name="grouped", tag=tag, bufs=4 if tag == "grouped" else 1, align_bytes=64)
-            copy(out=grouped[:], in_=raw.rearrange("p i c -> p c i"))
-            quantise(grouped[:].rearrange("p c i -> p (c i)"), q[0][:, c0 : c0 + width], q[1][:, c0 : c0 + width])
+            grouped = sbuf([P, width, PACK], BF16, tag)
+            copy(out=grouped, in_=raw.rearrange("p i c -> p c i"))
+            quantise(grouped.rearrange("p c i -> p (c i)"), q[0][:, c0 : c0 + width], q[1][:, c0 : c0 + width])
 
         q1 = [quantised_weight("w1a"), quantised_weight("w1b")]
         q3 = [quantised_weight("w3a"), quantised_weight("w3b")]
-        v_plane = keep.tile([P, S], U8, align_bytes=64)
-        nc.vector.tensor_copy(v_plane[:], tab_plane[:].indirect(idx[:]))
-        w2_dealt = keep.tile([P, 2 * PASS], U8, align_bytes=64)
+        v_plane = sbuf([P, S], U8, "v_plane")
+        nc.vector.tensor_copy(v_plane, tab_plane[:].indirect(idx[:]))
+        w2_dealt = sbuf([P, 2 * PASS], U8, "w2_dealt")
         nc.vector.tensor_copy(
-            out=w2_dealt[:].bitcast(U16).rearrange("p (t m) -> p t m", t=PACK),
+            out=w2_dealt.bitcast(U16).rearrange("p (t m) -> p t m", t=PACK),
             in_=w2_raw[:, 2 * PASS : 2 * H].bitcast(U16).rearrange("p (m t) -> p t m", t=PACK),
         )
         v_codes = []
 
         def gather_words(g):
-            words = work.tile([P, HALF], U32, name="v_codes%d" % g, bufs=1, align_bytes=64)
-            nc.vector.tensor_copy(words[:], tab[:].bitcast(U32).indirect(idx[:, 32 * g : 32 * g + 32]))
+            words = sbuf([P, HALF], U32, "v_codes%d" % g)
+            nc.vector.tensor_copy(words, tab[:].bitcast(U32).indirect(idx[:, 32 * g : 32 * g + 32]))
             v_codes.append(words)
 
         gather_words(0)
-        quantise_plain(raw1[0], q1[0], 0, nc.vector.tensor_copy)
+        quantise_plain(raw1[0], q1[0], 0, nc.vector.tensor_copy, "cast0")
         quantise_plain(raw3[0], q3[0], 0, nc.vector.tensor_copy, "v_codes1")
         gather_words(1)
-        w2_plane = keep.tile([P, PASS], U8, align_bytes=64)
+        w2_plane = sbuf([P, PASS], U8, "w2_plane")
         nc.vector.tensor_copy(
-            out=w2_plane[:].rearrange("p (t m) -> p t m", t=PACK),
+            out=w2_plane.rearrange("p (t m) -> p t m", t=PACK),
             in_=w2_rows[:, PASS:H].rearrange("p (m t) -> p t m", t=PACK),
         )
         q2 = [(w2_raw, w2_rows), (w2_dealt, w2_plane)]
         for n in range(PAGES):
             clear_page(n)
-        z0 = keep.tile([P, PACK, PICKS], F32, tag="wide", align_bytes=64)
-        zs = [z0]
+        z0 = sbuf([P, PACK, PICKS], F32, "wide")
+        slots = [z0[:, t, :] for t in range(PACK)]
 
-        def first_product(j0, j1, tag, bufs, codes, plane):
-            bank = psum.tile([P, j1 - j0], F32, name=tag, tag=tag, bufs=bufs)
+        def first_product(j0, j1, tag, codes, plane):
+            bank = psum.tile([P, j1 - j0], F32, name=tag, tag=tag, bufs=2)
             for j in range(j0, j1, P):
                 nc.tensor.matmul_mx(
                     out=bank[:, j - j0 : j - j0 + P],
@@ -189,64 +191,39 @@ def tile_list_burst_derotation_kernel(
                 )
             return bank[:]
 
-        pairs = []
-
-        def product_room(s, j0):
-            if j0 == 0 and s >= PAGES:
-                return refs[s - PAGES]
-            if j0 == HALF and s >= 1:
-                return pairs[-1]
-            room = work.tile([P, S], F32, name="room", align_bytes=64)
-            return room[:]
-
-        def pair_room(s, j0):
-            if j0 == HALF and 1 <= s < FINAL:
-                return zs[(s - 1) // PACK][:, (s - 1) % PACK, :]
-            if (s, j0) == (FINAL, HALF):
-                pair = keep.tile([P, S], F32, name="pair", tag="ref3", align_bytes=64)
-                return pair[:]
-            if (s, j0) == (FINAL, 0):
-                pair = keep.tile([P, S], F32, name="pair", tag="z0_codes", align_bytes=64)
-                return pair[:]
-            pair = work.tile([P, S], F32, name="pair", align_bytes=64)
-            return pair[:]
-
-        def derotate(s, j0, j1):
+        def features(s, j0, j1):
             b, t = divmod(s, PACK)
             cols = slice(P * t, P * (t + 1))
-            first, second = slice(0, j1 - j0), slice(j1 - j0, 2 * (j1 - j0))
-            phase = first_product(j0, j1, "phase", 2, q1[b][0][:, cols].bitcast(FP8X4), q1[b][1][:, cols])
-            spare = (s, j0) == (0, PIECE)
-            inph = first_product(
-                j0, j1, *(("hsum", 4) if spare else ("inph", 1)),
-                q2[b][0][:, 2 * P * t : 2 * P * (t + 1)].bitcast(FP4X4), q2[b][1][:, cols],
-            )
-            quad = first_product(
-                j0, j1, *(("hsum", 4) if spare else ("quad", 1)), q3[b][0][:, cols].bitcast(FP8X4), q3[b][1][:, cols]
-            )
-            size = work.tile([P, j1 - j0], F32, name="size", align_bytes=64)
-            trig = work.tile([P, S], F32, name="trig", bufs=3)
-            room = product_room(s, j0)
-            if (s, j0) in ((0, 0), (0, PIECE), (0, HALF)):
-                nc.scalar.activation(out=trig[:, second], in_=phase, func=ACT.Sin)
-                nc.scalar.activation(out=size[:], in_=phase, func=ACT.Abs)
-                nc.scalar.activation(out=trig[:, first], in_=size[:], func=ACT.Sin, scale=-1.0, bias=math.pi / 2)
-                nc.vector.tensor_tensor(out=room[:, first], in0=inph, in1=trig[:, first], op=MULT)
-                nc.vector.tensor_tensor(out=room[:, second], in0=quad, in1=trig[:, second], op=MULT)
-                return room
-            pair = pair_room(s, j0)
-            pairs.append(pair)
-            nc.scalar.activation(out=size[:], in_=phase, func=ACT.Abs)
-            nc.scalar.activation(out=trig[:, second], in_=phase, func=ACT.Sin)
-            nc.scalar.copy(out=pair[:, first], in_=inph)
-            nc.scalar.activation(out=trig[:, first], in_=size[:], func=ACT.Sin, scale=-1.0, bias=math.pi / 2)
-            nc.scalar.copy(out=pair[:, second], in_=quad)
-            for part in (first, second) if s < SPLIT else (slice(0, S),):
-                nc.gpsimd.tensor_tensor(out=room[:, part], in0=pair[:, part], in1=trig[:, part], op=MULT)
-            return room
+            phase = first_product(j0, j1, "phase", q1[b][0][:, cols].bitcast(FP8X4), q1[b][1][:, cols])
+            inph = first_product(j0, j1, "inph", q2[b][0][:, 2 * P * t : 2 * P * (t + 1)].bitcast(FP4X4), q2[b][1][:, cols])
+            quad = first_product(j0, j1, "quad", q3[b][0][:, cols].bitcast(FP8X4), q3[b][1][:, cols])
+            return phase, inph, quad
+
+        def cosine(out, size):
+            nc.scalar.activation(out=out, in_=size, func=ACT.Sin, scale=-1.0, bias=math.pi / 2)
+
+        def derotate_on_vector(j0, j1, trig, room):
+            width = j1 - j0
+            phase, inph, quad = features(0, j0, j1)
+            size = sbuf([P, width], F32, "size", 2)
+            nc.scalar.activation(out=trig[:, width : 2 * width], in_=phase, func=ACT.Sin)
+            nc.scalar.activation(out=size, in_=phase, func=ACT.Abs)
+            cosine(trig[:, 0:width], size)
+            nc.vector.tensor_tensor(out=room[:, 0:width], in0=inph, in1=trig[:, 0:width], op=MULT)
+            nc.vector.tensor_tensor(out=room[:, width : 2 * width], in0=quad, in1=trig[:, width : 2 * width], op=MULT)
+
+        def derotate(s, j0, trig, pair, room):
+            phase, inph, quad = features(s, j0, j0 + HALF)
+            size = sbuf([P, HALF], F32, "size", 2)
+            nc.scalar.activation(out=size, in_=phase, func=ACT.Abs)
+            nc.scalar.activation(out=trig[:, HALF:S], in_=phase, func=ACT.Sin)
+            nc.scalar.copy(out=pair[:, 0:HALF], in_=inph)
+            cosine(trig[:, 0:HALF], size)
+            nc.scalar.copy(out=pair[:, HALF:S], in_=quad)
+            nc.gpsimd.tensor_tensor(out=room, in0=pair, in1=trig, op=MULT)
 
         def turn(room, width):
-            hsum = psum.tile([P, width], F32, name="hsum", tag="hsum", bufs=4)
+            hsum = psum.tile([P, width], F32, name="hsum", tag="hsum", bufs=2)
             for j in range(0, 2 * width, P):
                 nc.tensor.matmul(
                     out=hsum[:, j % width : j % width + P], lhsT=room[:, j : j + P], rhs=ident[:], is_transpose=True,
@@ -255,87 +232,95 @@ def tile_list_burst_derotation_kernel(
             return hsum[:]
 
         def place(s, j0, j1, gained):
-            nc.vector.tensor_copy(pages[page_of(s)][:].indirect(idx2[:, j0 // 16 : j1 // 16]), gained[:, j0:j1])
+            nc.vector.tensor_copy(pages[s // FINAL][:].indirect(idx2[:, j0 // 16 : j1 // 16]), gained)
 
         def fetch(dst, s, m0, m1):
-            nc.vector.tensor_tensor(
-                dst, pages[page_of(s)][:].indirect(idx3[:, m0 // 16 : m1 // 16]), refs[s][:, m0:m1], ADD
-            )
+            nc.vector.tensor_tensor(dst, pages[s // FINAL][:].indirect(idx3[:, m0 // 16 : m1 // 16]), refs[s][:, m0:m1], ADD)
 
-        def round_z(z, tag):
-            grouped = keep.tile([P, z.shape[2] * PACK], BF16, name="zgrouped", tag=tag, align_bytes=64)
-            nc.scalar.copy(
-                out=grouped[:].rearrange("p (c e t) -> p c t e", e=4, t=PACK),
-                in_=z.rearrange("p t (c e) -> p c t e", e=4),
-            )
-            return grouped
+        def round_planes(out, z, copy):
+            copy(out=out.rearrange("p (c e) t -> p c t e", e=4), in_=z.rearrange("p t (c e) -> p c t e", e=4))
 
         pieces = list(zip(CUTS, CUTS[1:]))
-        grouped = [keep.tile([P, m1 - m0, PACK], BF16, name="grouped%d" % m0, align_bytes=64) for m0, m1 in pieces]
+        grouped = [sbuf([P, m1 - m0, PACK], BF16, "grouped%d" % m0) for m0, m1 in pieces]
 
-        def round_pair(n, t0, z, copy):
-            copy(
-                out=grouped[n][:, :, t0 : t0 + 2].rearrange("p (c e) t -> p c t e", e=4),
-                in_=z.rearrange("p t (c e) -> p c t e", e=4),
-            )
-
-        z0_rounded = []
-        units = [(0, 0, PIECE), (0, PIECE, HALF)] + [(s, j0, j0 + HALF) for s in range(SLICES) for j0 in (0, HALF)][1:]
-        last_h = keep.tile([P, S], F32)
-        room = derotate(*units[0])
-        for u, (s, j0, j1) in enumerate(units):
-            if (s, j0) in ROUNDS:
-                m0 = HALF * len(z0_rounded)
-                z0_rounded.append(round_z(z_back[:, :, m0 : m0 + HALF], "cast%d" % (1 + len(z0_rounded))))
-            following = derotate(*units[u + 1]) if u + 1 < len(units) else None
+        opening = ((0, PIECE), (PIECE, HALF), (HALF, S))
+        rooms = [sbuf([P, S], F32, tag) for tag in ("z0_codes", "z1_codes", "last_h")]
+        derotate_on_vector(*opening[0], sbuf([P, S], F32, "trig_a", 3), rooms[0])
+        derotate_on_vector(*opening[1], sbuf([P, S], F32, "trig_a", 3), rooms[1])
+        quantise_plain(raw1[1], q1[0], P, nc.vector.tensor_copy, "cast0")
+        quantise_plain(raw3[1], q3[0], P, nc.vector.tensor_copy, "cast1")
+        for u, (j0, j1) in enumerate(opening):
             if u == 0:
-                quantise_plain(raw1[1], q1[0], P, nc.vector.tensor_copy)
-                quantise_plain(raw3[1], q3[0], P, nc.vector.tensor_copy)
-            if u == 1:
-                quantise_plain(raw1[2], q1[0], 2 * P, nc.scalar.copy)
-                quantise_plain(raw3[2], q3[0], 2 * P, nc.scalar.copy, "early")
-            if (s, j0) == (FINAL, 0):
-                for n, (m0, m1) in enumerate(pieces):
-                    round_pair(n, 0, z1[:, :, m0:m1], nc.scalar.copy)
-            hsum = turn(room, j1 - j0)
-            room = following
+                derotate_on_vector(*opening[2], sbuf([P, S], F32, "trig_b"), rooms[2])
+                quantise_plain(raw1[2], q1[0], 2 * P, gpsimd_round, "cast2")
+                quantise_plain(raw3[2], q3[0], 2 * P, gpsimd_round, "cast3")
+                quantise_plain(raw1[3], q1[0], 3 * P, gpsimd_round, "cast4")
+                quantise_plain(raw3[3], q3[0], 3 * P, gpsimd_round, "rounded0")
+            if u == 2:
+                room_a = sbuf([P, S], F32, "pair_b", 2)
+                derotate(1, 0, sbuf([P, S], F32, "trig_a", 3), sbuf([P, S], F32, "pair_a"), room_a)
+            hsum = turn(rooms[u], j1 - j0)
+            gained = sbuf([P, j1 - j0], F32, ("gained_a", "cast3", "gained_c")[u])
+            nc.vector.tensor_tensor(out=gained, in0=hsum, in1=gains[0][:, j0:j1], op=MULT)
+            place(0, j0, j1, gained)
+
+        hsum_a = turn(room_a, HALF)
+        z0_rounded = []
+        for s in range(1, SLICES):
+            trig_b = sbuf([P, S], F32, "z0_codes" if s == FINAL else "trig_b")
+            pair_b = sbuf([P, S], F32, "ref3") if s == FINAL else sbuf([P, S], F32, "pair_b", 2)
+            room_b = refs[s - 2] if s >= 2 else sbuf([P, S], F32, "w4_codes")
+            derotate(s, HALF, trig_b, pair_b, room_b)
             if s == FINAL:
-                nc.scalar.copy(out=last_h[:, j0:j1], in_=hsum)
+                nc.scalar.copy(out=last_h[:, HALF:S], in_=turn(room_b, HALF))
+                break
+            trig_a = sbuf([P, S], F32, "trig_a", 3)
+            derotate(s + 1, 0, trig_a, slots[0] if s == 1 else sbuf([P, S], F32, "pair_a"), pair_b)
+            if s in DEALT_CASTS:
+                quantise_dealt(later[:, 0], q1[1], DEALT_CASTS[s], sbuf([P, HALF], F32, "cast2"))
+                quantise_dealt(later[:, 1], q3[1], DEALT_CASTS[s], slots[s - 1][:, HALF:S])
+            if s == PACK - 1:
+                z1 = sbuf([P, 2, PICKS], F32, "later")
+                slots.extend([z1[:, 0, :], z1[:, 1, :]])
+            if s in ROUNDS:
+                rounded = sbuf([P, HALF, PACK], BF16, "rounded%d" % ROUNDS[s])
+                round_planes(rounded, z_back[:, :, ROUNDS[s] : ROUNDS[s] + HALF], nc.scalar.copy)
+                z0_rounded.append(rounded)
+            hsum_b = turn(room_b, HALF)
+            if s == 1:
+                gained = sbuf([P, S], F32, "rounded0")
+                nc.vector.tensor_tensor(out=gained[:, 0:HALF], in0=hsum_a, in1=gains[s][:, 0:HALF], op=MULT)
+                nc.vector.tensor_tensor(out=gained[:, HALF:S], in0=hsum_b, in1=gains[s][:, HALF:S], op=MULT)
             else:
-                if (s, j0) == (1, 0):
-                    gained = work.tile([P, S], F32, name="gained", tag="early", bufs=1, align_bytes=64)
-                elif j0 == 0:
-                    gained = work.tile([P, S], F32, name="gained")
-                nc.vector.tensor_tensor(out=gained[:, j0:j1], in0=hsum, in1=gains[s][:, j0:j1], op=MULT)
-            if j0 == 0 and 1 <= s < FINAL:
-                fetch(zs[(s - 1) // PACK][:, (s - 1) % PACK, :], s - 1, 0, PICKS)
-                if s <= PACK:
-                    nc.sync.dma_start(out=out[P * (s - 1) : P * s, :], in_=z0[:, s - 1, :])
-            if (s, j0) == (PACK, 0):
-                z_back = keep.tile([P, PACK, PICKS], F32, tag="wide", align_bytes=64)
-                nc.sync.dma_start(out=z_back[:], in_=out.rearrange("(p t) m -> p t m", t=PACK))
-            if s < HALVED:
-                place(s, j0, j1, gained)
-            elif j1 == S and s < FINAL:
-                place(s, 0, S, gained)
-            if (s, j0) == CASTS[0]:
-                quantise_dealt(raw1[3], q1[1], "cast1")
-            if (s, j0) == CASTS[1]:
-                quantise_dealt(raw3[3], q3[1], "cast2")
-                z1 = keep.tile([P, 2, PICKS], F32, tag="later", align_bytes=64)
-                zs.append(z1)
+                gained = trig_a
+                nc.vector.tensor_tensor(out=gained[:, SHARE:S], in0=hsum_b, in1=gains[s][:, SHARE:S], op=MULT)
+                nc.gpsimd.tensor_tensor(out=gained[:, 0:SHARE], in0=slots[s - 1][:, 0:SHARE], in1=gains[s][:, 0:SHARE], op=MULT)
+            hsum_a = turn(pair_b, HALF)
+            if s + 1 == FINAL:
+                last_h = sbuf([P, S], F32, "last_h")
+                nc.scalar.copy(out=last_h[:, 0:HALF], in_=hsum_a)
+            else:
+                nc.scalar.copy(out=slots[s][:, 0:HALF], in_=hsum_a)
+            fetch(slots[s - 1], s - 1, 0, PICKS)
+            if s <= PACK:
+                nc.sync.dma_start(out=out[P * (s - 1) : P * s, :], in_=slots[s - 1])
+            if s == PACK:
+                z_back = sbuf([P, PACK, PICKS], F32, "wide")
+                nc.sync.dma_start(out=z_back, in_=out.rearrange("(p t) m -> p t m", t=PACK))
+            place(s, 0, S, gained)
+            if s + 1 == FINAL:
+                for n, (m0, m1) in enumerate(pieces):
+                    round_planes(grouped[n][:, :, 0:2], z1[:, :, m0:m1], nc.scalar.copy)
 
         refs.extend(load_ref(dealt_ref, 2, "ref3"))
-        z0_codes = keep.tile([P, PICKS], U32, align_bytes=64)
-        z1_codes = keep.tile([P, PICKS], U32, align_bytes=64)
-        z_codes = [z0_codes, z1_codes]
-        z_plane = keep.tile([P, PASSES, PICKS], U8, align_bytes=64)
+        z_codes = [sbuf([P, PICKS], U32, "z0_codes"), sbuf([P, PICKS], U32, "z1_codes")]
+        z_plane = sbuf([P, PASSES, PICKS], U8, "z_plane")
         for m0, rounded in zip((0, HALF), z0_rounded):
-            quantise(rounded[:], z0_codes[:, m0 : m0 + HALF], z_plane[:, 0, m0 : m0 + HALF])
-        nc.vector.tensor_tensor(pages[page_of(FINAL)][:].indirect(idx2[:]), last_h[:], gains[FINAL], MULT)
-        w4_codes = keep.tile([P, PASSES, N], I32, align_bytes=64)
-        nc.sync.dma_start(out=w4_codes[:], in_=w4_words.rearrange("a p c i -> p a (c i)").bitcast(I32))
-        banks = [("phase", 2), ("phase", 2), ("inph", 1), ("quad", 1)] + [("hsum", 4)] * 4
+            quantise(rounded.rearrange("p m t -> p (m t)"), z_codes[0][:, m0 : m0 + HALF], z_plane[:, 0, m0 : m0 + HALF])
+        nc.vector.tensor_tensor(pages[1][:].indirect(idx2[:]), last_h, gains[FINAL], MULT)
+        w4_codes = sbuf([P, PASSES, N], I32, "w4_codes")
+        nc.sync.dma_start(out=w4_codes, in_=w4_words.rearrange("a p c i -> p a (c i)").bitcast(I32))
+        banks = ["phase", "phase", "inph", "inph", "quad", "quad", "hsum", "hsum"]
 
         def last_product(c, b, m0, m1):
             base = PIECE * (c // 2)
@@ -352,17 +337,17 @@ def tile_list_burst_derotation_kernel(
                 )
 
         accs = []
-        for c, (tag, bufs) in enumerate(banks):
-            acc = psum.tile([P, 2, PIECE], F32, name="acc", tag=tag, bufs=bufs)
+        for c, tag in enumerate(banks):
+            acc = psum.tile([P, 2, PIECE], F32, name="acc", tag=tag, bufs=2)
             accs.append(acc)
             last_product(c, 0, PIECE * (c // 2), PIECE * (c // 2 + 1))
-        result = keep.tile([P, len(banks), 2, PIECE], F32, tag="wide", align_bytes=64)
+        result = sbuf([P, len(banks), 2, PIECE], F32, "wide")
         for n, (m0, m1) in enumerate(pieces):
-            picked = work.tile([P, 2, m1 - m0], F32, name="picked")
+            picked = sbuf([P, 2, m1 - m0], F32, "picked", 2)
             for t in range(2):
                 fetch(picked[:, t, :], FINAL - 1 + t, m0, m1)
-            round_pair(n, 2, picked[:], nc.scalar.copy if m0 < SCALAR_ROUNDS else nc.vector.tensor_copy)
-            quantise(grouped[n][:].rearrange("p m t -> p (m t)"), z1_codes[:, m0:m1], z_plane[:, 1, m0:m1])
+            round_planes(grouped[n][:, :, 2:4], picked, nc.scalar.copy if m0 < SCALAR_ROUNDS else nc.vector.tensor_copy)
+            quantise(grouped[n].rearrange("p m t -> p (m t)"), z_codes[1][:, m0:m1], z_plane[:, 1, m0:m1])
             for c in (2 * (m0 // PIECE), 2 * (m0 // PIECE) + 1):
                 last_product(c, 1, m0, m1)
                 if m1 % PIECE == 0:

@@ -125,9 +125,6 @@ def tile_list_burst_derotation_kernel(
         def quantise(grouped, codes, plane):
             nc.vector.quantize_mx(out=codes.bitcast(FP8X4), scales=plane, in_=grouped)
 
-        def gpsimd_round(out, in_):
-            nc.gpsimd.tensor_scalar(out=out, in0=in_, scalar1=1.0, scalar2=0.0, op0=MULT, op1=ADD)
-
         def quantised_weight(name):
             return sbuf([P, PASS], U32, name + "_codes"), sbuf([P, PASS], U8, name + "_plane")
 
@@ -247,15 +244,13 @@ def tile_list_burst_derotation_kernel(
         rooms = [sbuf([P, S], F32, tag) for tag in ("z0_codes", "z1_codes", "last_h")]
         derotate_on_vector(*opening[0], sbuf([P, S], F32, "trig_a", 3), rooms[0])
         derotate_on_vector(*opening[1], sbuf([P, S], F32, "trig_a", 3), rooms[1])
-        quantise_plain(raw1[1], q1[0], P, nc.vector.tensor_copy, "cast0")
-        quantise_plain(raw3[1], q3[0], P, nc.vector.tensor_copy, "cast1")
+        quantise_plain(raw1[1], q1[0], P, nc.scalar.copy, "cast0")
+        quantise_plain(raw3[1], q3[0], P, nc.scalar.copy, "cast1")
         for u, (j0, j1) in enumerate(opening):
             if u == 0:
                 derotate_on_vector(*opening[2], sbuf([P, S], F32, "trig_b"), rooms[2])
-                quantise_plain(raw1[2], q1[0], 2 * P, gpsimd_round, "cast2")
-                quantise_plain(raw3[2], q3[0], 2 * P, gpsimd_round, "cast3")
-                quantise_plain(raw1[3], q1[0], 3 * P, gpsimd_round, "cast4")
-                quantise_plain(raw3[3], q3[0], 3 * P, gpsimd_round, "rounded0")
+                quantise_plain(raw1[2], q1[0], 2 * P, nc.vector.tensor_copy, "cast2")
+                quantise_plain(raw3[2], q3[0], 2 * P, nc.vector.tensor_copy, "cast3")
             if u == 2:
                 room_a = sbuf([P, S], F32, "pair_b", 2)
                 derotate(1, 0, sbuf([P, S], F32, "trig_a", 3), sbuf([P, S], F32, "pair_a"), room_a)
@@ -276,6 +271,9 @@ def tile_list_burst_derotation_kernel(
                 break
             trig_a = sbuf([P, S], F32, "trig_a", 3)
             derotate(s + 1, 0, trig_a, slots[0] if s == 1 else sbuf([P, S], F32, "pair_a"), pair_b)
+            if s == 1:
+                quantise_plain(raw1[3], q1[0], 3 * P, nc.scalar.copy, "cast4")
+                quantise_plain(raw3[3], q3[0], 3 * P, nc.scalar.copy, "cast5")
             if s in DEALT_CASTS:
                 quantise_dealt(later[:, 0], q1[1], DEALT_CASTS[s], sbuf([P, HALF], F32, "cast2"))
                 quantise_dealt(later[:, 1], q3[1], DEALT_CASTS[s], slots[s - 1][:, HALF:S])

@@ -29,7 +29,7 @@ PIECE = 256
 CUTS = (0, 256, 512, 768, 896, 1024)
 PAGES = 2
 FINAL = SLICES - 1
-SHARE = 512
+LEAD = 3 * HALF
 DEALT_CASTS = {2: 0, 3: 2}
 ROUNDS = {5: 0, 6: HALF}
 SCALAR_ROUNDS = 512
@@ -75,12 +75,6 @@ def tile_list_burst_derotation_kernel(
             nc.sync.dma_start(out=raw[:], in_=w[:, c0:c1].rearrange("(p i) c -> p i c", i=PACK))
             return raw[:]
 
-        def load_dealt_gains(t0, t1):
-            rows = keep.tile([P, t1 - t0, S], F32, name="gains%d" % t0)
-            for q in (0, 2, 1, 3):
-                nc.sync.dma_start(out=rows[32 * q : 32 * (q + 1)], in_=wgs.rearrange("(q t) j -> q t j", t=PACK)[:, t0:t1])
-            return [rows[:, t, :] for t in range(t1 - t0)]
-
         def load_ref(view, t0, tag):
             rows = keep.tile([P, 2, PICKS], F32, name="rows", tag=tag, align_bytes=64)
             nc.sync.dma_start(out=rows[:], in_=view[:, t0 : t0 + 2])
@@ -112,14 +106,41 @@ def tile_list_burst_derotation_kernel(
         raw3.append(load_weight(w3, 3 * P, PASS, "raw3d"))
         idx3 = lists.tile([P, PICKS // 16], U16)
         nc.sync.dma_start(idx3[:], offs3)
-        refs = load_ref(plain_ref, 0, "ref0")
+        arena = sbuf([P, LEAD + FINAL * PICKS - HALF], F32, "arena")
+        halves = arena.rearrange("p (n c) -> p n c", c=HALF)
+        refs = []
+
+        def load_ref_pair(view, t0):
+            rows = arena[:, LEAD + PICKS * len(refs) : LEAD + PICKS * (len(refs) + 2)].rearrange("p (t m) -> p t m", t=2)
+            nc.sync.dma_start(out=rows, in_=view[:, t0 : t0 + 2])
+            refs.extend([rows[:, 0, :], rows[:, 1, :]])
+
+        def load_dealt(dst, t, j0, j1):
+            for q in (0, 2, 1, 3):
+                nc.sync.dma_start(out=dst[32 * q : 32 * (q + 1)], in_=wgs.rearrange("(q t) j -> q t j", t=PACK)[:, t, j0:j1])
+
+        def load_factors(s):
+            factors[s] = sbuf([P, HALF + S], F32, "factors", 3)
+            if s < PACK:
+                nc.sync.dma_start(out=factors[s][:, 0:HALF], in_=wgs[:, HALF:S])
+            else:
+                load_dealt(factors[s][:, 0:HALF], s - PACK, HALF, S)
+
+        factors = {}
+        load_ref_pair(plain_ref, 0)
+        load_factors(2)
         later = keep.tile([P, 2, PACK, PASS], F32, tag="later", align_bytes=64)
         for n, w in enumerate((w1, w3)):
             nc.sync.dma_start(out=later[:, n], in_=w[:, PASS:H].rearrange("(p i) c -> p i c", i=PACK))
-        refs.extend(load_ref(plain_ref, 2, "ref1"))
-        gains = [plain_gains[:]] * PACK + load_dealt_gains(0, 2)
-        refs.extend(load_ref(dealt_ref, 0, "ref2"))
-        gains.extend(load_dealt_gains(2, PACK))
+        load_factors(3)
+        load_ref_pair(plain_ref, 2)
+        load_factors(4)
+        dealt_gains = sbuf([P, PACK - 1, HALF], F32, "dealt_gains")
+        load_dealt(dealt_gains, slice(0, PACK - 1), 0, HALF)
+        load_ref_pair(dealt_ref, 0)
+        last_gains = sbuf([P, S], F32, "last_gains")
+        load_dealt(last_gains, PACK - 1, 0, S)
+        gains = [plain_gains[:]] * PACK + [dealt_gains[:, t, :] for t in range(PACK - 1)]
         load_scale_rows(nc.sync, w4_plane, w4_scales.rearrange("a q n -> q a n"))
 
         def quantise(grouped, codes, plane):
@@ -171,8 +192,8 @@ def tile_list_burst_derotation_kernel(
         q2 = [(w2_raw, w2_rows), (w2_dealt, w2_plane)]
         for n in range(PAGES):
             clear_page(n)
-        z0 = sbuf([P, PACK, PICKS], F32, "wide")
-        slots = [z0[:, t, :] for t in range(PACK)]
+        z0 = sbuf([P, PACK * PICKS + HALF], F32, "wide")
+        spans = [z0[:, PICKS * t : PICKS * t + HALF + S] for t in range(PACK)]
 
         def first_product(j0, j1, tag, codes, plane):
             bank = psum.tile([P, j1 - j0], F32, name=tag, tag=tag, bufs=2)
@@ -209,7 +230,7 @@ def tile_list_burst_derotation_kernel(
             nc.vector.tensor_tensor(out=room[:, 0:width], in0=inph, in1=trig[:, 0:width], op=MULT)
             nc.vector.tensor_tensor(out=room[:, width : 2 * width], in0=quad, in1=trig[:, width : 2 * width], op=MULT)
 
-        def derotate(s, j0, trig, pair, room):
+        def unload(s, j0, trig, pair):
             phase, inph, quad = features(s, j0, j0 + HALF)
             size = sbuf([P, HALF], F32, "size", 2)
             nc.scalar.activation(out=size, in_=phase, func=ACT.Abs)
@@ -217,13 +238,18 @@ def tile_list_burst_derotation_kernel(
             nc.scalar.copy(out=pair[:, 0:HALF], in_=inph)
             cosine(trig[:, 0:HALF], size)
             nc.scalar.copy(out=pair[:, HALF:S], in_=quad)
-            nc.gpsimd.tensor_tensor(out=room, in0=pair, in1=trig, op=MULT)
+
+        def multiply(out, in0, in1):
+            nc.gpsimd.tensor_tensor(out=out, in0=in0, in1=in1, op=MULT)
+
+        def parts(ap, width=HALF):
+            return ap[:, 0 : 2 * width].rearrange("p (n c) -> p n c", n=2)
 
         def turn(room, width):
             hsum = psum.tile([P, width], F32, name="hsum", tag="hsum", bufs=2)
             for j in range(0, 2 * width, P):
                 nc.tensor.matmul(
-                    out=hsum[:, j % width : j % width + P], lhsT=room[:, j : j + P], rhs=ident[:], is_transpose=True,
+                    out=hsum[:, j % width : j % width + P], lhsT=room[:, j // width, j % width : j % width + P], rhs=ident[:], is_transpose=True,
                     start=(j == 0), stop=(j == 2 * width - P),
                 )
             return hsum[:]
@@ -238,12 +264,11 @@ def tile_list_burst_derotation_kernel(
             copy(out=out.rearrange("p (c e) t -> p c t e", e=4), in_=z.rearrange("p t (c e) -> p c t e", e=4))
 
         pieces = list(zip(CUTS, CUTS[1:]))
-        grouped = [sbuf([P, m1 - m0, PACK], BF16, "grouped%d" % m0) for m0, m1 in pieces]
 
         opening = ((0, PIECE), (PIECE, HALF), (HALF, S))
         rooms = [sbuf([P, S], F32, tag) for tag in ("z0_codes", "z1_codes", "last_h")]
-        derotate_on_vector(*opening[0], sbuf([P, S], F32, "trig_a", 3), rooms[0])
-        derotate_on_vector(*opening[1], sbuf([P, S], F32, "trig_a", 3), rooms[1])
+        derotate_on_vector(*opening[0], sbuf([P, HALF], F32, "grouped0"), rooms[0])
+        derotate_on_vector(*opening[1], sbuf([P, HALF], F32, "grouped%d" % PIECE), rooms[1])
         quantise_plain(raw1[1], q1[0], P, nc.scalar.copy, "cast0")
         quantise_plain(raw3[1], q3[0], P, nc.scalar.copy, "cast1")
         for u, (j0, j1) in enumerate(opening):
@@ -252,34 +277,46 @@ def tile_list_burst_derotation_kernel(
                 quantise_plain(raw1[2], q1[0], 2 * P, nc.vector.tensor_copy, "cast2")
                 quantise_plain(raw3[2], q3[0], 2 * P, nc.vector.tensor_copy, "cast3")
             if u == 2:
-                room_a = sbuf([P, S], F32, "pair_b", 2)
-                derotate(1, 0, sbuf([P, S], F32, "trig_a", 3), sbuf([P, S], F32, "pair_a"), room_a)
-            hsum = turn(rooms[u], j1 - j0)
+                room_a = sbuf([P, S], F32, "w4_codes")
+                pair_a = sbuf([P, S], F32, "z_plane")
+                trig_a = sbuf([P, S], F32, "trig_a")
+                unload(1, HALF, trig_a, pair_a)
+                multiply(room_a, pair_a, trig_a)
+            hsum = turn(parts(rooms[u], j1 - j0), j1 - j0)
             gained = sbuf([P, j1 - j0], F32, ("gained_a", "cast3", "gained_c")[u])
             nc.vector.tensor_tensor(out=gained, in0=hsum, in1=gains[0][:, j0:j1], op=MULT)
             place(0, j0, j1, gained)
 
-        hsum_a = turn(room_a, HALF)
+        hsum_a = turn(parts(room_a), HALF)
         z0_rounded = []
         for s in range(1, SLICES):
             trig_b = sbuf([P, S], F32, "z0_codes" if s == FINAL else "trig_b")
-            pair_b = sbuf([P, S], F32, "ref3") if s == FINAL else sbuf([P, S], F32, "pair_b", 2)
-            room_b = refs[s - 2] if s >= 2 else sbuf([P, S], F32, "w4_codes")
-            derotate(s, HALF, trig_b, pair_b, room_b)
+            pair_b = sbuf([P, S], F32, "ref3" if s == FINAL else "pair_b")
+            spare = 2 * FINAL + 1
+            room_b = halves[:, 2 * s : spare + 1 : spare - 2 * s, :]
+            unload(s, 0, trig_b, pair_b)
+            multiply(room_b, parts(pair_b), parts(trig_b))
             if s == FINAL:
-                nc.scalar.copy(out=last_h[:, HALF:S], in_=turn(room_b, HALF))
+                nc.scalar.copy(out=last_h[:, 0:HALF], in_=turn(room_b, HALF))
                 break
-            trig_a = sbuf([P, S], F32, "trig_a", 3)
-            derotate(s + 1, 0, trig_a, slots[0] if s == 1 else sbuf([P, S], F32, "pair_a"), pair_b)
+            room_a = arena[:, PICKS * (s - 1) : PICKS * s]
             if s == 1:
+                trig_a = sbuf([P, S], F32, "rounded%d" % HALF)
+                unload(s + 1, HALF, trig_a, spans[0][:, HALF:])
+                multiply(room_a, spans[0][:, HALF:], trig_a)
                 quantise_plain(raw1[3], q1[0], 3 * P, nc.scalar.copy, "cast4")
                 quantise_plain(raw3[3], q3[0], 3 * P, nc.scalar.copy, "cast5")
+            else:
+                unload(s + 1, HALF, factors[s][:, HALF:], spans[s - 1][:, HALF:])
+                multiply(arena[:, PICKS * (s - 1) - HALF : PICKS * s], spans[s - 1], factors[s])
+            if PACK < s + 3 < FINAL:
+                load_factors(s + 3)
             if s in DEALT_CASTS:
                 quantise_dealt(later[:, 0], q1[1], DEALT_CASTS[s], sbuf([P, HALF], F32, "cast2"))
-                quantise_dealt(later[:, 1], q3[1], DEALT_CASTS[s], slots[s - 1][:, HALF:S])
+                quantise_dealt(later[:, 1], q3[1], DEALT_CASTS[s], sbuf([P, HALF], F32, "cast3"))
             if s == PACK - 1:
-                z1 = sbuf([P, 2, PICKS], F32, "later")
-                slots.extend([z1[:, 0, :], z1[:, 1, :]])
+                z1 = sbuf([P, 2 * PICKS + HALF], F32, "later")
+                spans.extend([z1[:, PICKS * t : PICKS * t + HALF + S] for t in range(2)])
             if s in ROUNDS:
                 rounded = sbuf([P, HALF, PACK], BF16, "rounded%d" % ROUNDS[s])
                 round_planes(rounded, z_back[:, :, ROUNDS[s] : ROUNDS[s] + HALF], nc.scalar.copy)
@@ -287,35 +324,35 @@ def tile_list_burst_derotation_kernel(
             hsum_b = turn(room_b, HALF)
             if s == 1:
                 gained = sbuf([P, S], F32, "rounded0")
-                nc.vector.tensor_tensor(out=gained[:, 0:HALF], in0=hsum_a, in1=gains[s][:, 0:HALF], op=MULT)
-                nc.vector.tensor_tensor(out=gained[:, HALF:S], in0=hsum_b, in1=gains[s][:, HALF:S], op=MULT)
+                nc.vector.tensor_tensor(out=gained[:, HALF:S], in0=hsum_a, in1=gains[s][:, HALF:S], op=MULT)
             else:
-                gained = trig_a
-                nc.vector.tensor_tensor(out=gained[:, SHARE:S], in0=hsum_b, in1=gains[s][:, SHARE:S], op=MULT)
-                nc.gpsimd.tensor_tensor(out=gained[:, 0:SHARE], in0=slots[s - 1][:, 0:SHARE], in1=gains[s][:, 0:SHARE], op=MULT)
-            hsum_a = turn(pair_b, HALF)
+                gained = arena[:, PICKS * (s - 2) : PICKS * (s - 1)]
+            nc.vector.tensor_tensor(out=gained[:, 0:HALF], in0=hsum_b, in1=gains[s][:, 0:HALF], op=MULT)
+            hsum_a = turn(parts(room_a), HALF)
             if s + 1 == FINAL:
                 last_h = sbuf([P, S], F32, "last_h")
-                nc.scalar.copy(out=last_h[:, 0:HALF], in_=hsum_a)
-            else:
-                nc.scalar.copy(out=slots[s][:, 0:HALF], in_=hsum_a)
-            fetch(slots[s - 1], s - 1, 0, PICKS)
+                nc.scalar.copy(out=last_h[:, HALF:S], in_=hsum_a)
+            fetch(spans[s - 1][:, 0:PICKS], s - 1, 0, PICKS)
+            if s + 1 < FINAL:
+                nc.scalar.copy(out=spans[s][:, 0:HALF], in_=hsum_a)
             if s <= PACK:
-                nc.sync.dma_start(out=out[P * (s - 1) : P * s, :], in_=slots[s - 1])
+                nc.sync.dma_start(out=out[P * (s - 1) : P * s, :], in_=spans[s - 1][:, 0:PICKS])
             if s == PACK:
                 z_back = sbuf([P, PACK, PICKS], F32, "wide")
                 nc.sync.dma_start(out=z_back, in_=out.rearrange("(p t) m -> p t m", t=PACK))
             place(s, 0, S, gained)
             if s + 1 == FINAL:
+                grouped = [sbuf([P, m1 - m0, PACK], BF16, "grouped%d" % m0) for m0, m1 in pieces]
+                planes = z1[:, 0 : 2 * PICKS].rearrange("p (t m) -> p t m", t=2)
                 for n, (m0, m1) in enumerate(pieces):
-                    round_planes(grouped[n][:, :, 0:2], z1[:, :, m0:m1], nc.scalar.copy)
+                    round_planes(grouped[n][:, :, 0:2], planes[:, :, m0:m1], nc.scalar.copy)
 
         refs.extend(load_ref(dealt_ref, 2, "ref3"))
         z_codes = [sbuf([P, PICKS], U32, "z0_codes"), sbuf([P, PICKS], U32, "z1_codes")]
         z_plane = sbuf([P, PASSES, PICKS], U8, "z_plane")
         for m0, rounded in zip((0, HALF), z0_rounded):
             quantise(rounded.rearrange("p m t -> p (m t)"), z_codes[0][:, m0 : m0 + HALF], z_plane[:, 0, m0 : m0 + HALF])
-        nc.vector.tensor_tensor(pages[1][:].indirect(idx2[:]), last_h, gains[FINAL], MULT)
+        nc.vector.tensor_tensor(pages[1][:].indirect(idx2[:]), last_h, last_gains, MULT)
         w4_codes = sbuf([P, PASSES, N], I32, "w4_codes")
         nc.sync.dma_start(out=w4_codes, in_=w4_words.rearrange("a p c i -> p a (c i)").bitcast(I32))
         banks = ["phase", "phase", "inph", "inph", "quad", "quad", "hsum", "hsum"]

@@ -106,7 +106,7 @@ def tile_list_burst_derotation_kernel(
         raw3.append(load_weight(w3, 3 * P, PASS, "raw3d"))
         idx3 = lists.tile([P, PICKS // 16], U16)
         nc.sync.dma_start(idx3[:], offs3)
-        arena = sbuf([P, LEAD + FINAL * PICKS - HALF], F32, "arena")
+        arena = sbuf([P, LEAD + FINAL * PICKS], F32, "arena")
         halves = arena.rearrange("p (n c) -> p n c", c=HALF)
         refs = []
 
@@ -146,26 +146,35 @@ def tile_list_burst_derotation_kernel(
         def quantise(grouped, codes, plane):
             nc.vector.quantize_mx(out=codes.bitcast(FP8X4), scales=plane, in_=grouped)
 
-        def quantised_weight(name):
-            return sbuf([P, PASS], U32, name + "_codes"), sbuf([P, PASS], U8, name + "_plane")
+        def gpsimd_round(out, in_):
+            nc.gpsimd.tensor_scalar(out=out, in0=in_, scalar1=1.0, scalar2=0.0, op0=MULT, op1=ADD)
 
-        def quantise_dealt(raw, q, t0, room):
-            grouped = room.bitcast(BF16).rearrange("p (t m i) -> p t m i", t=2, i=PACK)
-            nc.scalar.copy(
-                out=grouped.rearrange("p t m i -> p m i t"),
-                in_=raw.rearrange("p i (m t) -> p m i t", t=PACK)[:, :, :, t0 : t0 + 2],
-            )
-            cols = slice(P * t0, P * (t0 + 2))
-            quantise(grouped.rearrange("p t m i -> p (t m i)"), q[0][:, cols], q[1][:, cols])
+        weights = {}
 
-        def quantise_plain(raw, q, c0, copy, tag):
-            width = raw.shape[2]
-            grouped = sbuf([P, width, PACK], BF16, tag)
-            copy(out=grouped, in_=raw.rearrange("p i c -> p c i"))
-            quantise(grouped.rearrange("p c i -> p (c i)"), q[0][:, c0 : c0 + width], q[1][:, c0 : c0 + width])
+        def quantised(s0, count):
+            codes = sbuf([P, 2, count, P], U32, "codes%d" % s0)
+            plane = sbuf([P, 2, count, P], U8, "plane%d" % s0)
+            for t in range(count):
+                weights[s0 + t] = [(codes[:, n, t, :].bitcast(FP8X4), plane[:, n, t, :]) for n in range(2)]
+            return codes.rearrange("p n t m -> p (n t m)"), plane.rearrange("p n t m -> p (n t m)")
 
-        q1 = [quantised_weight("w1a"), quantised_weight("w1b")]
-        q3 = [quantised_weight("w3a"), quantised_weight("w3b")]
+        def quantise_early(s, copy, tags):
+            codes, plane = quantised(s, 1)
+            for n, raw in enumerate((raw1[s], raw3[s])):
+                grouped = sbuf([P, P, PACK], BF16, tags[n])
+                copy(out=grouped, in_=raw.rearrange("p i c -> p c i"))
+                quantise(grouped.rearrange("p c i -> p (c i)"), codes[:, P * n : P * (n + 1)], plane[:, P * n : P * (n + 1)])
+
+        staging = arena[:, LEAD + (FINAL - 1) * PICKS :].bitcast(BF16)
+
+        def quantise_late(s0, count, sources):
+            width = count * PASS
+            both = staging[:, S - width : S + width]
+            for n, source in enumerate(sources):
+                grouped = both[:, width * n : width * (n + 1)].rearrange("p (t m i) -> p m i t", t=count, i=PACK)
+                nc.scalar.copy(out=grouped, in_=source)
+            quantise(both, *quantised(s0, count))
+
         v_plane = sbuf([P, S], U8, "v_plane")
         nc.vector.tensor_copy(v_plane, tab_plane[:].indirect(idx[:]))
         w2_dealt = sbuf([P, 2 * PASS], U8, "w2_dealt")
@@ -181,8 +190,7 @@ def tile_list_burst_derotation_kernel(
             v_codes.append(words)
 
         gather_words(0)
-        quantise_plain(raw1[0], q1[0], 0, nc.vector.tensor_copy, "cast0")
-        quantise_plain(raw3[0], q3[0], 0, nc.vector.tensor_copy, "v_codes1")
+        quantise_early(0, nc.vector.tensor_copy, ("cast0", "v_codes1"))
         gather_words(1)
         w2_plane = sbuf([P, PASS], U8, "w2_plane")
         nc.vector.tensor_copy(
@@ -212,9 +220,9 @@ def tile_list_burst_derotation_kernel(
         def features(s, j0, j1):
             b, t = divmod(s, PACK)
             cols = slice(P * t, P * (t + 1))
-            phase = first_product(j0, j1, "phase", q1[b][0][:, cols].bitcast(FP8X4), q1[b][1][:, cols])
+            phase = first_product(j0, j1, "phase", *weights[s][0])
             inph = first_product(j0, j1, "inph", q2[b][0][:, 2 * P * t : 2 * P * (t + 1)].bitcast(FP4X4), q2[b][1][:, cols])
-            quad = first_product(j0, j1, "quad", q3[b][0][:, cols].bitcast(FP8X4), q3[b][1][:, cols])
+            quad = first_product(j0, j1, "quad", *weights[s][1])
             return phase, inph, quad
 
         def cosine(out, size):
@@ -269,13 +277,11 @@ def tile_list_burst_derotation_kernel(
         rooms = [sbuf([P, S], F32, tag) for tag in ("z0_codes", "z1_codes", "last_h")]
         derotate_on_vector(*opening[0], sbuf([P, HALF], F32, "grouped0"), rooms[0])
         derotate_on_vector(*opening[1], sbuf([P, HALF], F32, "grouped%d" % PIECE), rooms[1])
-        quantise_plain(raw1[1], q1[0], P, nc.scalar.copy, "cast0")
-        quantise_plain(raw3[1], q3[0], P, nc.scalar.copy, "cast1")
+        quantise_early(1, nc.vector.tensor_copy, ("cast0", "cast1"))
         for u, (j0, j1) in enumerate(opening):
             if u == 0:
                 derotate_on_vector(*opening[2], sbuf([P, S], F32, "trig_b"), rooms[2])
-                quantise_plain(raw1[2], q1[0], 2 * P, nc.vector.tensor_copy, "cast2")
-                quantise_plain(raw3[2], q3[0], 2 * P, nc.vector.tensor_copy, "cast3")
+                quantise_early(2, gpsimd_round, ("cast2", "cast3"))
             if u == 2:
                 room_a = sbuf([P, S], F32, "w4_codes")
                 pair_a = sbuf([P, S], F32, "z_plane")
@@ -292,7 +298,7 @@ def tile_list_burst_derotation_kernel(
         for s in range(1, SLICES):
             trig_b = sbuf([P, S], F32, "z0_codes" if s == FINAL else "trig_b")
             pair_b = sbuf([P, S], F32, "ref3" if s == FINAL else "pair_b")
-            spare = 2 * FINAL + 1
+            spare = 2 * FINAL + 2
             room_b = halves[:, 2 * s : spare + 1 : spare - 2 * s, :]
             unload(s, 0, trig_b, pair_b)
             multiply(room_b, parts(pair_b), parts(trig_b))
@@ -304,19 +310,11 @@ def tile_list_burst_derotation_kernel(
                 trig_a = sbuf([P, S], F32, "rounded%d" % HALF)
                 unload(s + 1, HALF, trig_a, spans[0][:, HALF:])
                 multiply(room_a, spans[0][:, HALF:], trig_a)
-                quantise_plain(raw1[3], q1[0], 3 * P, nc.scalar.copy, "cast4")
-                quantise_plain(raw3[3], q3[0], 3 * P, nc.scalar.copy, "cast5")
             else:
                 unload(s + 1, HALF, factors[s][:, HALF:], spans[s - 1][:, HALF:])
                 multiply(arena[:, PICKS * (s - 1) - HALF : PICKS * s], spans[s - 1], factors[s])
             if PACK < s + 3 < FINAL:
                 load_factors(s + 3)
-            if s in DEALT_CASTS:
-                quantise_dealt(later[:, 0], q1[1], DEALT_CASTS[s], sbuf([P, HALF], F32, "cast2"))
-                quantise_dealt(later[:, 1], q3[1], DEALT_CASTS[s], sbuf([P, HALF], F32, "cast3"))
-            if s == PACK - 1:
-                z1 = sbuf([P, 2 * PICKS + HALF], F32, "later")
-                spans.extend([z1[:, PICKS * t : PICKS * t + HALF + S] for t in range(2)])
             if s in ROUNDS:
                 rounded = sbuf([P, HALF, PACK], BF16, "rounded%d" % ROUNDS[s])
                 round_planes(rounded, z_back[:, :, ROUNDS[s] : ROUNDS[s] + HALF], nc.scalar.copy)
@@ -328,6 +326,15 @@ def tile_list_burst_derotation_kernel(
             else:
                 gained = arena[:, PICKS * (s - 2) : PICKS * (s - 1)]
             nc.vector.tensor_tensor(out=gained[:, 0:HALF], in0=hsum_b, in1=gains[s][:, 0:HALF], op=MULT)
+            if s == 1:
+                quantise_late(3, 1, [raw[3].rearrange("p i (m t) -> p m i t", t=1) for raw in (raw1, raw3)])
+            if s in DEALT_CASTS:
+                t0 = DEALT_CASTS[s]
+                dealt = [later[:, n].rearrange("p i (m t) -> p m i t", t=PACK)[:, :, :, t0 : t0 + 2] for n in range(2)]
+                quantise_late(PACK + t0, 2, dealt)
+            if s == PACK - 1:
+                z1 = sbuf([P, 2 * PICKS + HALF], F32, "later")
+                spans.extend([z1[:, PICKS * t : PICKS * t + HALF + S] for t in range(2)])
             hsum_a = turn(parts(room_a), HALF)
             if s + 1 == FINAL:
                 last_h = sbuf([P, S], F32, "last_h")

@@ -36,6 +36,10 @@ SCALAR_ROUNDS = 512
 VECTOR_BANKS = (6, 7)
 
 
+def page_of(s):
+    return (max(s, 1) + 1) % PAGES
+
+
 def load_scale_rows(queue, plane, rows):
     for q in range(4):
         queue.dma_start(out=plane[32 * q : 32 * q + 4].bitcast(I32), in_=rows[4 * q : 4 * q + 4].bitcast(I32))
@@ -263,10 +267,10 @@ def tile_list_burst_derotation_kernel(
             return hsum[:]
 
         def place(s, j0, j1, gained):
-            nc.vector.tensor_copy(pages[s // FINAL][:].indirect(idx2[:, j0 // 16 : j1 // 16]), gained)
+            nc.vector.tensor_copy(pages[page_of(s)][:].indirect(idx2[:, j0 // 16 : j1 // 16]), gained)
 
         def fetch(dst, s, m0, m1):
-            nc.vector.tensor_tensor(dst, pages[s // FINAL][:].indirect(idx3[:, m0 // 16 : m1 // 16]), refs[s][:, m0:m1], ADD)
+            nc.vector.tensor_tensor(dst, pages[page_of(s)][:].indirect(idx3[:, m0 // 16 : m1 // 16]), refs[s][:, m0:m1], ADD)
 
         def round_planes(out, z, copy):
             copy(out=out.rearrange("p (c e) t -> p c t e", e=4), in_=z.rearrange("p t (c e) -> p c t e", e=4))
@@ -359,7 +363,7 @@ def tile_list_burst_derotation_kernel(
         z_plane = sbuf([P, PASSES, PICKS], U8, "z_plane")
         for m0, rounded in zip((0, HALF), z0_rounded):
             quantise(rounded.rearrange("p m t -> p (m t)"), z_codes[0][:, m0 : m0 + HALF], z_plane[:, 0, m0 : m0 + HALF])
-        nc.vector.tensor_tensor(pages[1][:].indirect(idx2[:]), last_h, last_gains, MULT)
+        nc.vector.tensor_tensor(pages[page_of(FINAL)][:].indirect(idx2[:]), last_h, last_gains, MULT)
         w4_codes = sbuf([P, PASSES, N], I32, "w4_codes")
         nc.sync.dma_start(out=w4_codes, in_=w4_words.rearrange("a p c i -> p a (c i)").bitcast(I32))
         banks = ["phase", "phase", "inph", "inph", "quad", "quad", "hsum", "hsum"]

@@ -33,7 +33,6 @@ LEAD = 3 * HALF
 DEALT_CASTS = {2: 0, 3: 2}
 ROUNDS = {5: 0, 6: HALF}
 SCALAR_ROUNDS = 512
-VECTOR_BANKS = (6, 7)
 
 
 def page_of(s):
@@ -100,9 +99,9 @@ def tile_list_burst_derotation_kernel(
         raw3 = [load_weight(w3, 0, P, "raw3a")]
         load_scale_rows(nc.sync, w2_rows, w2_scales[0])
         plain_gains = keep.tile([P, S], F32)
-        nc.sync.dma_start(out=plain_gains[:, 0:HALF], in_=wgs[:, 0:HALF])
         raw1.append(load_weight(w1, P, 2 * P, "raw1b"))
         raw3.append(load_weight(w3, P, 2 * P, "raw3b"))
+        nc.sync.dma_start(out=plain_gains[:, 0:HALF], in_=wgs[:, 0:HALF])
         raw1.append(load_weight(w1, 2 * P, 3 * P, "raw1c"))
         raw3.append(load_weight(w3, 2 * P, 3 * P, "raw3c"))
         nc.sync.dma_start(out=plain_gains[:, HALF:S], in_=wgs[:, HALF:S])
@@ -162,10 +161,13 @@ def tile_list_burst_derotation_kernel(
                 weights[s0 + t] = [(codes[:, n, t, :].bitcast(FP8X4), plane[:, n, t, :]) for n in range(2)]
             return codes.rearrange("p n t m -> p (n t m)"), plane.rearrange("p n t m -> p (n t m)")
 
-        def quantise_early(s, copy, tags):
+        def cast_rooms(*tags):
+            return [sbuf([P, PIECE], F32, tag) for tag in tags]
+
+        def quantise_early(s, copy, rooms):
             codes, plane = quantised(s, 1)
             for n, raw in enumerate((raw1[s], raw3[s])):
-                grouped = sbuf([P, P, PACK], BF16, tags[n])
+                grouped = rooms[n].bitcast(BF16).rearrange("p (c i) -> p c i", i=PACK)
                 copy(out=grouped, in_=raw.rearrange("p i c -> p c i"))
                 quantise(grouped.rearrange("p c i -> p (c i)"), codes[:, P * n : P * (n + 1)], plane[:, P * n : P * (n + 1)])
 
@@ -173,7 +175,7 @@ def tile_list_burst_derotation_kernel(
 
         def quantise_late(s0, count, sources):
             width = count * PASS
-            both = staging[:, S - width : S + width]
+            both = staging[:, 2 * (S - width) : 2 * S]
             for n, source in enumerate(sources):
                 grouped = both[:, width * n : width * (n + 1)].rearrange("p (t m i) -> p m i t", t=count, i=PACK)
                 nc.scalar.copy(out=grouped, in_=source)
@@ -194,7 +196,7 @@ def tile_list_burst_derotation_kernel(
             v_codes.append(words)
 
         gather_words(0)
-        quantise_early(0, nc.vector.tensor_copy, ("cast0", "v_codes1"))
+        quantise_early(0, nc.vector.tensor_copy, cast_rooms("cast0", "v_codes1"))
         gather_words(1)
         w2_plane = sbuf([P, PASS], U8, "w2_plane")
         nc.vector.tensor_copy(
@@ -279,13 +281,14 @@ def tile_list_burst_derotation_kernel(
 
         opening = ((0, PIECE), (PIECE, HALF), (HALF, S))
         rooms = [sbuf([P, S], F32, tag) for tag in ("z0_codes", "z1_codes", "last_h")]
-        derotate_on_vector(*opening[0], sbuf([P, HALF], F32, "grouped0"), rooms[0])
-        derotate_on_vector(*opening[1], sbuf([P, HALF], F32, "grouped%d" % PIECE), rooms[1])
-        quantise_early(1, nc.vector.tensor_copy, ("cast0", "cast1"))
+        trigs = [sbuf([P, HALF], F32, "grouped0"), sbuf([P, HALF], F32, "grouped%d" % PIECE), sbuf([P, S], F32, "trig_0")]
+        derotate_on_vector(*opening[0], trigs[0], rooms[0])
+        quantise_early(1, nc.vector.tensor_copy, [rooms[1][:, 0:PIECE], rooms[1][:, PIECE:HALF]])
+        derotate_on_vector(*opening[1], trigs[1], rooms[1])
         for u, (j0, j1) in enumerate(opening):
             if u == 0:
-                derotate_on_vector(*opening[2], sbuf([P, S], F32, "trig_b"), rooms[2])
-                quantise_early(2, gpsimd_round, ("cast2", "cast3"))
+                derotate_on_vector(*opening[2], trigs[2], rooms[2])
+                quantise_early(2, gpsimd_round, cast_rooms("cast2", "cast3"))
             if u == 2:
                 room_a = sbuf([P, S], F32, "w4_codes")
                 pair_a = sbuf([P, S], F32, "z_plane")
@@ -293,7 +296,7 @@ def tile_list_burst_derotation_kernel(
                 unload(1, HALF, trig_a, pair_a)
                 multiply(room_a, pair_a, trig_a)
             hsum = turn(parts(rooms[u], j1 - j0), j1 - j0)
-            gained = sbuf([P, j1 - j0], F32, ("gained_a", "cast3", "gained_c")[u])
+            gained = trigs[u + 1][:, 0:PIECE] if u < 2 else sbuf([P, HALF], F32, "cast3")
             nc.vector.tensor_tensor(out=gained, in0=hsum, in1=gains[0][:, j0:j1], op=MULT)
             place(0, j0, j1, gained)
 
@@ -366,40 +369,48 @@ def tile_list_burst_derotation_kernel(
         nc.vector.tensor_tensor(pages[page_of(FINAL)][:].indirect(idx2[:]), last_h, last_gains, MULT)
         w4_codes = sbuf([P, PASSES, N], I32, "w4_codes")
         nc.sync.dma_start(out=w4_codes, in_=w4_words.rearrange("a p c i -> p a (c i)").bitcast(I32))
-        banks = ["phase", "phase", "inph", "inph", "quad", "quad", "hsum", "hsum"]
+        rings = ["phase", "phase", "inph", "inph", "quad", "quad", "hsum", "hsum", "phase"]
+        sums = [(m0, m0 + PIECE, n0, n0 + 2) for m0 in CUTS[:3] for n0 in (0, 2)]
+        sums.extend([(CUTS[3], CUTS[4], 0, 4), (CUTS[4], CUTS[5], 0, 2), (CUTS[4], CUTS[5], 2, 4)])
+        accs = []
 
-        def last_product(c, b, m0, m1):
-            base = PIECE * (c // 2)
-            for n in range(2):
-                rows = slice(P * (2 * (c % 2) + n), P * (2 * (c % 2) + n + 1))
+        def last_product(c, b):
+            m0, m1, n0, n1 = sums[c]
+            for n in range(n0, n1):
+                rows = slice(P * n, P * (n + 1))
                 nc.tensor.matmul_mx(
-                    out=accs[c][:, n, m0 - base : m1 - base],
+                    out=accs[c][:, n - n0, :],
                     lhsT=w4_codes[:, b, rows].bitcast(FP8X4),
                     lhsT_scale=w4_plane[:, b, rows],
                     rhs=z_codes[b][:, m0:m1].bitcast(FP8X4),
                     rhs_scale=z_plane[:, b, m0:m1],
-                    start=(b == 0 and n == 0),
-                    stop=(b == PASSES - 1 and n == 1 and m1 == base + PIECE),
+                    start=(b == 0 and n == n0),
+                    stop=(b == PASSES - 1 and n == n1 - 1),
                 )
 
-        accs = []
-        for c, tag in enumerate(banks):
-            acc = psum.tile([P, 2, PIECE], F32, name="acc", tag=tag, bufs=2)
+        def open_sum(c):
+            m0, m1, n0, n1 = sums[c]
+            acc = psum.tile([P, n1 - n0, m1 - m0], F32, name="acc", tag=rings[c], bufs=2)
             accs.append(acc)
-            last_product(c, 0, PIECE * (c // 2), PIECE * (c // 2 + 1))
-        result = sbuf([P, len(banks), 2, PIECE], F32, "wide")
-        for n, (m0, m1) in enumerate(pieces):
+            last_product(c, 0)
+
+        for c in range(len(sums) - 1):
+            open_sum(c)
+        result = sbuf([P, PACK * PICKS], F32, "wide")
+        stored = 0
+        for k, (m0, m1) in enumerate(pieces):
             picked = sbuf([P, 2, m1 - m0], F32, "picked", 2)
             for t in range(2):
                 fetch(picked[:, t, :], FINAL - 1 + t, m0, m1)
-            round_planes(grouped[n][:, :, 2:4], picked, nc.scalar.copy if m0 < SCALAR_ROUNDS else nc.vector.tensor_copy)
-            quantise(grouped[n].rearrange("p m t -> p (m t)"), z_codes[1][:, m0:m1], z_plane[:, 1, m0:m1])
-            for c in (2 * (m0 // PIECE), 2 * (m0 // PIECE) + 1):
-                last_product(c, 1, m0, m1)
-                if m1 % PIECE == 0:
-                    copy = nc.vector.tensor_copy if c in VECTOR_BANKS else nc.scalar.copy
-                    copy(out=result[:, c], in_=accs[c][:])
-                    nc.sync.dma_start(
-                        out=out.rearrange("(n p) m -> p n m", p=P)[:, 2 * (c % 2) : 2 * (c % 2) + 2, PIECE * (c // 2) : PIECE * (c // 2 + 1)],
-                        in_=result[:, c],
-                    )
+            round_planes(grouped[k][:, :, 2:4], picked, nc.scalar.copy if m0 < SCALAR_ROUNDS else nc.vector.tensor_copy)
+            quantise(grouped[k].rearrange("p m t -> p (m t)"), z_codes[1][:, m0:m1], z_plane[:, 1, m0:m1])
+            for c in [c for c in range(len(sums)) if sums[c][0] == m0]:
+                n0, n1 = sums[c][2:]
+                last_product(c, 1)
+                leaving = result[:, stored : stored + (n1 - n0) * (m1 - m0)].rearrange("p (n m) -> p n m", n=n1 - n0)
+                stored = stored + (n1 - n0) * (m1 - m0)
+                copy = nc.vector.tensor_copy if c == len(sums) - 1 else nc.scalar.copy
+                copy(out=leaving, in_=accs[c][:])
+                nc.sync.dma_start(out=out.rearrange("(n p) m -> p n m", p=P)[:, n0:n1, m0:m1], in_=leaving)
+                if c == 0:
+                    open_sum(len(sums) - 1)

@@ -102,11 +102,11 @@ def tile_list_burst_derotation_kernel(
         raw1.append(load_weight(w1, P, 2 * P, "raw1b"))
         raw3.append(load_weight(w3, P, 2 * P, "raw3b"))
         nc.sync.dma_start(out=plain_gains[:, 0:HALF], in_=wgs[:, 0:HALF])
-        raw1.append(load_weight(w1, 2 * P, 3 * P, "raw1c"))
-        raw3.append(load_weight(w3, 2 * P, 3 * P, "raw3c"))
+        raw_both = sbuf([P, 2, PACK, P], F32, "raw_both")
+        for n, w in enumerate((w1, w3)):
+            nc.sync.dma_start(out=raw_both[:, n], in_=w[:, 2 * P : 3 * P].rearrange("(p i) c -> p i c", i=PACK))
         nc.sync.dma_start(out=plain_gains[:, HALF:S], in_=wgs[:, HALF:S])
-        raw1.append(load_weight(w1, 3 * P, PASS, "raw1d"))
-        raw3.append(load_weight(w3, 3 * P, PASS, "raw3d"))
+        raw_last = [load_weight(w1, 3 * P, PASS, "raw1d"), load_weight(w3, 3 * P, PASS, "raw3d")]
         idx3 = lists.tile([P, PICKS // 16], U16)
         nc.sync.dma_start(idx3[:], offs3)
         arena = sbuf([P, LEAD + FINAL * PICKS], F32, "arena")
@@ -148,9 +148,6 @@ def tile_list_burst_derotation_kernel(
 
         def quantise(grouped, codes, plane):
             nc.vector.quantize_mx(out=codes.bitcast(FP8X4), scales=plane, in_=grouped)
-
-        def gpsimd_round(out, in_):
-            nc.gpsimd.tensor_scalar(out=out, in0=in_, scalar1=1.0, scalar2=0.0, op0=MULT, op1=ADD)
 
         weights = {}
 
@@ -281,22 +278,25 @@ def tile_list_burst_derotation_kernel(
 
         opening = ((0, PIECE), (PIECE, HALF), (HALF, S))
         rooms = [sbuf([P, S], F32, tag) for tag in ("z0_codes", "z1_codes", "last_h")]
-        trigs = [sbuf([P, HALF], F32, "grouped0"), sbuf([P, HALF], F32, "grouped%d" % PIECE), sbuf([P, S], F32, "trig_0")]
+        early = sbuf([P, PIECE + S], F32, "early")
+        trigs = [sbuf([P, HALF], F32, "grouped0"), early[:, 0:HALF], sbuf([P, S], F32, "trig_0")]
         derotate_on_vector(*opening[0], trigs[0], rooms[0])
         quantise_early(1, nc.vector.tensor_copy, [rooms[1][:, 0:PIECE], rooms[1][:, PIECE:HALF]])
         derotate_on_vector(*opening[1], trigs[1], rooms[1])
         for u, (j0, j1) in enumerate(opening):
             if u == 0:
                 derotate_on_vector(*opening[2], trigs[2], rooms[2])
-                quantise_early(2, gpsimd_round, cast_rooms("cast2", "cast3"))
+                both = trigs[1].bitcast(BF16)
+                nc.vector.tensor_copy(both.rearrange("p (n c i) -> p n c i", n=2, i=PACK), raw_both.rearrange("p n i c -> p n c i"))
+                quantise(both, *quantised(2, 1))
             if u == 2:
-                room_a = sbuf([P, S], F32, "w4_codes")
+                room_a = early[:, PIECE:]
                 pair_a = sbuf([P, S], F32, "z_plane")
                 trig_a = sbuf([P, S], F32, "trig_a")
                 unload(1, HALF, trig_a, pair_a)
                 multiply(room_a, pair_a, trig_a)
             hsum = turn(parts(rooms[u], j1 - j0), j1 - j0)
-            gained = trigs[u + 1][:, 0:PIECE] if u < 2 else sbuf([P, HALF], F32, "cast3")
+            gained = (trigs[0][:, 0:PIECE], early[:, 0:PIECE], trigs[2][:, 0:HALF])[u]
             nc.vector.tensor_tensor(out=gained, in0=hsum, in1=gains[0][:, j0:j1], op=MULT)
             place(0, j0, j1, gained)
 
@@ -334,7 +334,7 @@ def tile_list_burst_derotation_kernel(
                 gained = arena[:, PICKS * (s - 2) : PICKS * (s - 1)]
             nc.vector.tensor_tensor(out=gained[:, 0:HALF], in0=hsum_b, in1=gains[s][:, 0:HALF], op=MULT)
             if s == 1:
-                quantise_late(3, 1, [raw[3].rearrange("p i (m t) -> p m i t", t=1) for raw in (raw1, raw3)])
+                quantise_late(3, 1, [raw.rearrange("p i (m t) -> p m i t", t=1) for raw in raw_last])
             if s in DEALT_CASTS:
                 t0 = DEALT_CASTS[s]
                 dealt = [later[:, n].rearrange("p i (m t) -> p m i t", t=PACK)[:, :, :, t0 : t0 + 2] for n in range(2)]

@@ -33,6 +33,7 @@ LEAD = 3 * HALF
 DEALT_CASTS = {2: 0, 3: 2}
 ROUNDS = {5: 0, 6: HALF}
 SCALAR_ROUNDS = 512
+VECTOR_BANKS = (6, 7)
 
 
 def page_of(s):
@@ -369,48 +370,40 @@ def tile_list_burst_derotation_kernel(
         nc.vector.tensor_tensor(pages[page_of(FINAL)][:].indirect(idx2[:]), last_h, last_gains, MULT)
         w4_codes = sbuf([P, PASSES, N], I32, "w4_codes")
         nc.sync.dma_start(out=w4_codes, in_=w4_words.rearrange("a p c i -> p a (c i)").bitcast(I32))
-        rings = ["phase", "phase", "inph", "inph", "quad", "quad", "hsum", "hsum", "phase"]
-        sums = [(m0, m0 + PIECE, n0, n0 + 2) for m0 in CUTS[:3] for n0 in (0, 2)]
-        sums.extend([(CUTS[3], CUTS[4], 0, 4), (CUTS[4], CUTS[5], 0, 2), (CUTS[4], CUTS[5], 2, 4)])
-        accs = []
+        banks = ["phase", "phase", "inph", "inph", "quad", "quad", "hsum", "hsum"]
 
-        def last_product(c, b):
-            m0, m1, n0, n1 = sums[c]
-            for n in range(n0, n1):
-                rows = slice(P * n, P * (n + 1))
+        def last_product(c, b, m0, m1):
+            base = PIECE * (c // 2)
+            for n in range(2):
+                rows = slice(P * (2 * (c % 2) + n), P * (2 * (c % 2) + n + 1))
                 nc.tensor.matmul_mx(
-                    out=accs[c][:, n - n0, :],
+                    out=accs[c][:, n, m0 - base : m1 - base],
                     lhsT=w4_codes[:, b, rows].bitcast(FP8X4),
                     lhsT_scale=w4_plane[:, b, rows],
                     rhs=z_codes[b][:, m0:m1].bitcast(FP8X4),
                     rhs_scale=z_plane[:, b, m0:m1],
-                    start=(b == 0 and n == n0),
-                    stop=(b == PASSES - 1 and n == n1 - 1),
+                    start=(b == 0 and n == 0),
+                    stop=(b == PASSES - 1 and n == 1 and m1 == base + PIECE),
                 )
 
-        def open_sum(c):
-            m0, m1, n0, n1 = sums[c]
-            acc = psum.tile([P, n1 - n0, m1 - m0], F32, name="acc", tag=rings[c], bufs=2)
+        accs = []
+        for c, tag in enumerate(banks):
+            acc = psum.tile([P, 2, PIECE], F32, name="acc", tag=tag, bufs=2)
             accs.append(acc)
-            last_product(c, 0)
-
-        for c in range(len(sums) - 1):
-            open_sum(c)
-        result = sbuf([P, PACK * PICKS], F32, "wide")
-        stored = 0
-        for k, (m0, m1) in enumerate(pieces):
+            last_product(c, 0, PIECE * (c // 2), PIECE * (c // 2 + 1))
+        result = sbuf([P, len(banks), 2, PIECE], F32, "wide")
+        for n, (m0, m1) in enumerate(pieces):
             picked = sbuf([P, 2, m1 - m0], F32, "picked", 2)
             for t in range(2):
                 fetch(picked[:, t, :], FINAL - 1 + t, m0, m1)
-            round_planes(grouped[k][:, :, 2:4], picked, nc.scalar.copy if m0 < SCALAR_ROUNDS else nc.vector.tensor_copy)
-            quantise(grouped[k].rearrange("p m t -> p (m t)"), z_codes[1][:, m0:m1], z_plane[:, 1, m0:m1])
-            for c in [c for c in range(len(sums)) if sums[c][0] == m0]:
-                n0, n1 = sums[c][2:]
-                last_product(c, 1)
-                leaving = result[:, stored : stored + (n1 - n0) * (m1 - m0)].rearrange("p (n m) -> p n m", n=n1 - n0)
-                stored = stored + (n1 - n0) * (m1 - m0)
-                copy = nc.vector.tensor_copy if c == len(sums) - 1 else nc.scalar.copy
-                copy(out=leaving, in_=accs[c][:])
-                nc.sync.dma_start(out=out.rearrange("(n p) m -> p n m", p=P)[:, n0:n1, m0:m1], in_=leaving)
-                if c == 0:
-                    open_sum(len(sums) - 1)
+            round_planes(grouped[n][:, :, 2:4], picked, nc.scalar.copy if m0 < SCALAR_ROUNDS else nc.vector.tensor_copy)
+            quantise(grouped[n].rearrange("p m t -> p (m t)"), z_codes[1][:, m0:m1], z_plane[:, 1, m0:m1])
+            for c in (2 * (m0 // PIECE), 2 * (m0 // PIECE) + 1):
+                last_product(c, 1, m0, m1)
+                if m1 % PIECE == 0:
+                    copy = nc.vector.tensor_copy if c in VECTOR_BANKS else nc.scalar.copy
+                    copy(out=result[:, c], in_=accs[c][:])
+                    nc.sync.dma_start(
+                        out=out.rearrange("(n p) m -> p n m", p=P)[:, 2 * (c % 2) : 2 * (c % 2) + 2, PIECE * (c // 2) : PIECE * (c // 2 + 1)],
+                        in_=result[:, c],
+                    )

@@ -150,6 +150,9 @@ def tile_list_burst_derotation_kernel(
         def quantise(grouped, codes, plane):
             nc.vector.quantize_mx(out=codes.bitcast(FP8X4), scales=plane, in_=grouped)
 
+        def gpsimd_round(out, in_):
+            nc.gpsimd.tensor_scalar(out=out, in0=in_, scalar1=1.0, scalar2=0.0, op0=MULT, op1=ADD)
+
         weights = {}
 
         def quantised(s0, count):
@@ -288,7 +291,7 @@ def tile_list_burst_derotation_kernel(
             if u == 0:
                 derotate_on_vector(*opening[2], trigs[2], rooms[2])
                 both = trigs[1].bitcast(BF16)
-                nc.vector.tensor_copy(both.rearrange("p (n c i) -> p n c i", n=2, i=PACK), raw_both.rearrange("p n i c -> p n c i"))
+                gpsimd_round(both.rearrange("p (n c i) -> p n c i", n=2, i=PACK), raw_both.rearrange("p n i c -> p n c i"))
                 quantise(both, *quantised(2, 1))
             if u == 2:
                 room_a = early[:, PIECE:]

@@ -350,7 +350,8 @@ def tile_list_burst_derotation_kernel(
             if s + 1 == FINAL:
                 last_h = sbuf([P, S], F32, "last_h")
                 nc.scalar.copy(out=last_h[:, HALF:S], in_=hsum_a)
-            fetch(spans[s - 1][:, 0:PICKS], s - 1, 0, PICKS)
+            for m0, m1 in ((0, PICKS),) if s == 1 else ((HALF, PICKS), (0, HALF)):
+                fetch(spans[s - 1][:, m0:m1], s - 1, m0, m1)
             if s + 1 < FINAL:
                 nc.scalar.copy(out=spans[s][:, 0:HALF], in_=hsum_a)
             if s <= PACK:

@@ -27,17 +27,18 @@ SLICES = H // P
 HALF = S // 2
 PIECE = 256
 CUTS = (0, 256, 512, 768, 896, 1024)
-PAGES = 2
+PAGES = PACK
 FINAL = SLICES - 1
+STEPPED = FINAL - 1
 LEAD = 3 * HALF
 DEALT_CASTS = {2: 0, 3: 2}
-ROUNDS = {5: 0, 6: HALF}
-SCALAR_ROUNDS = 512
-VECTOR_BANKS = (6, 7)
+SCALAR_ROUNDS = 896
 
 
 def page_of(s):
-    return (max(s, 1) + 1) % PAGES
+    if s < PACK:
+        return (max(s, 1) + 1) % 2
+    return (s + 1) % PAGES
 
 
 def load_scale_rows(queue, plane, rows):
@@ -52,6 +53,7 @@ def tile_list_burst_derotation_kernel(
     with ExitStack() as ctx:
         lists = ctx.enter_context(tc.tile_pool(name="lists", bufs=1))
         keep = ctx.enter_context(tc.tile_pool(name="keep", bufs=1))
+        frames = ctx.enter_context(tc.tile_pool(name="frames", bufs=1))
         psum = ctx.enter_context(tc.psum_pool(name="psum", bufs=1))
 
         def sbuf(shape, dtype, tag, bufs=1):
@@ -65,8 +67,7 @@ def tile_list_burst_derotation_kernel(
         w4_plane = keep.tile([P, PASSES, N], U8, align_bytes=64)
         nc.vector.memset(w4_plane[:].rearrange("p a n -> p (a n)").bitcast(I32), 0)
         pages = []
-
-        def clear_page(t):
+        for t in range(2):
             page = keep.tile([P, T2], F32, name="page%d" % t, align_bytes=64)
             nc.vector.memset(page[:], 0.0)
             pages.append(page)
@@ -79,20 +80,15 @@ def tile_list_burst_derotation_kernel(
             nc.sync.dma_start(out=raw[:], in_=w[:, c0:c1].rearrange("(p i) c -> p i c", i=PACK))
             return raw[:]
 
-        def load_ref(view, t0, tag):
-            rows = keep.tile([P, 2, PICKS], F32, name="rows", tag=tag, align_bytes=64)
-            nc.sync.dma_start(out=rows[:], in_=view[:, t0 : t0 + 2])
-            return [rows[:, 0, :], rows[:, 1, :]]
-
         plain_ref = ref[0:PASS].rearrange("(t p) m -> p t m", p=P)
         dealt_ref = ref[PASS:H].rearrange("(p t) m -> p t m", t=PACK)
 
         idx = lists.tile([P, S // 16], U16)
         nc.sync.dma_start(idx[:], offs)
-        w2_raw = keep.tile([P, 2 * H], U8, align_bytes=64)
-        nc.sync.dma_start(out=w2_raw[:].bitcast(I32), in_=w2_words[0].bitcast(I32))
-        idx2 = lists.tile([P, S // 16], U16)
-        nc.sync.dma_start(idx2[:], offs2)
+        w2_late = frames.tile([P, 2 * PASS], U8, align_bytes=64, offset=4 * T2 - PASS)
+        nc.sync.dma_start(out=w2_late[:].bitcast(I32), in_=w2_words[0][:, 2 * PASS : 2 * H].bitcast(I32))
+        w2_raw = keep.tile([P, 2 * PASS], U8, align_bytes=64)
+        nc.sync.dma_start(out=w2_raw[:].bitcast(I32), in_=w2_words[0][:, 0 : 2 * PASS].bitcast(I32))
         load_scale_rows(nc.sync, tab_plane, tab_scales[0])
         tab = keep.tile([P, T], I32, tag="wide", align_bytes=64)
         nc.sync.dma_start(out=tab[:], in_=tab_words[0].rearrange("p t i -> p (t i)").bitcast(I32))
@@ -103,6 +99,8 @@ def tile_list_burst_derotation_kernel(
         raw1.append(load_weight(w1, P, 2 * P, "raw1b"))
         raw3.append(load_weight(w3, P, 2 * P, "raw3b"))
         nc.sync.dma_start(out=plain_gains[:, 0:HALF], in_=wgs[:, 0:HALF])
+        idx2 = lists.tile([P, S // 16], U16)
+        nc.sync.dma_start(idx2[:], offs2)
         raw_both = sbuf([P, 2, PACK, P], F32, "raw_both")
         for n, w in enumerate((w1, w3)):
             nc.sync.dma_start(out=raw_both[:, n], in_=w[:, 2 * P : 3 * P].rearrange("(p i) c -> p i c", i=PACK))
@@ -110,7 +108,7 @@ def tile_list_burst_derotation_kernel(
         raw_last = [load_weight(w1, 3 * P, PASS, "raw1d"), load_weight(w3, 3 * P, PASS, "raw3d")]
         idx3 = lists.tile([P, PICKS // 16], U16)
         nc.sync.dma_start(idx3[:], offs3)
-        arena = sbuf([P, LEAD + FINAL * PICKS], F32, "arena")
+        arena = sbuf([P, LEAD + (PACK + 1) * PICKS], F32, "arena")
         halves = arena.rearrange("p (n c) -> p n c", c=HALF)
         refs = []
 
@@ -139,12 +137,11 @@ def tile_list_burst_derotation_kernel(
         load_factors(3)
         load_ref_pair(plain_ref, 2)
         load_factors(4)
-        dealt_gains = sbuf([P, PACK - 1, HALF], F32, "dealt_gains")
-        load_dealt(dealt_gains, slice(0, PACK - 1), 0, HALF)
-        load_ref_pair(dealt_ref, 0)
-        last_gains = sbuf([P, S], F32, "last_gains")
-        load_dealt(last_gains, PACK - 1, 0, S)
-        gains = [plain_gains[:]] * PACK + [dealt_gains[:, t, :] for t in range(PACK - 1)]
+        dealt_gains = sbuf([P, 2, HALF], F32, "dealt_gains")
+        load_dealt(dealt_gains, slice(0, 2), 0, HALF)
+        last_gains = sbuf([P, 2, S], F32, "last_gains")
+        load_dealt(last_gains, slice(2, PACK), 0, S)
+        gains = [plain_gains[:]] * PACK + [dealt_gains[:, t, :] for t in range(2)]
         load_scale_rows(nc.sync, w4_plane, w4_scales.rearrange("a q n -> q a n"))
 
         def quantise(grouped, codes, plane):
@@ -172,7 +169,7 @@ def tile_list_burst_derotation_kernel(
                 copy(out=grouped, in_=raw.rearrange("p i c -> p c i"))
                 quantise(grouped.rearrange("p c i -> p (c i)"), codes[:, P * n : P * (n + 1)], plane[:, P * n : P * (n + 1)])
 
-        staging = arena[:, LEAD + (FINAL - 1) * PICKS :].bitcast(BF16)
+        staging = arena[:, LEAD + PACK * PICKS :].bitcast(BF16)
 
         def quantise_late(s0, count, sources):
             width = count * PASS
@@ -187,8 +184,12 @@ def tile_list_burst_derotation_kernel(
         w2_dealt = sbuf([P, 2 * PASS], U8, "w2_dealt")
         nc.vector.tensor_copy(
             out=w2_dealt.bitcast(U16).rearrange("p (t m) -> p t m", t=PACK),
-            in_=w2_raw[:, 2 * PASS : 2 * H].bitcast(U16).rearrange("p (m t) -> p t m", t=PACK),
+            in_=w2_late[:].bitcast(U16).rearrange("p (m t) -> p t m", t=PACK),
         )
+        for t in range(2, PAGES):
+            page = frames.tile([P, T2], F32, name="page%d" % t, align_bytes=64, offset=4 * T2 * (t - 2))
+            nc.gpsimd.memset(page[:], 0.0)
+            pages.append(page)
         v_codes = []
 
         def gather_words(g):
@@ -205,8 +206,6 @@ def tile_list_burst_derotation_kernel(
             in_=w2_rows[:, PASS:H].rearrange("p (m t) -> p t m", t=PACK),
         )
         q2 = [(w2_raw, w2_rows), (w2_dealt, w2_plane)]
-        for n in range(PAGES):
-            clear_page(n)
         z0 = sbuf([P, PACK * PICKS + HALF], F32, "wide")
         spans = [z0[:, PICKS * t : PICKS * t + HALF + S] for t in range(PACK)]
 
@@ -283,7 +282,8 @@ def tile_list_burst_derotation_kernel(
         opening = ((0, PIECE), (PIECE, HALF), (HALF, S))
         rooms = [sbuf([P, S], F32, tag) for tag in ("z0_codes", "z1_codes", "last_h")]
         early = sbuf([P, PIECE + S], F32, "early")
-        trigs = [sbuf([P, HALF], F32, "grouped0"), early[:, 0:HALF], sbuf([P, S], F32, "trig_0")]
+        opening_trig = sbuf([P, 2 * S], F32, "opening_trig")
+        trigs = [sbuf([P, HALF], F32, "grouped0"), early[:, 0:HALF], opening_trig[:, 0:S]]
         derotate_on_vector(*opening[0], trigs[0], rooms[0])
         quantise_early(1, nc.vector.tensor_copy, [rooms[1][:, 0:PIECE], rooms[1][:, PIECE:HALF]])
         derotate_on_vector(*opening[1], trigs[1], rooms[1])
@@ -296,7 +296,7 @@ def tile_list_burst_derotation_kernel(
             if u == 2:
                 room_a = early[:, PIECE:]
                 pair_a = sbuf([P, S], F32, "z_plane")
-                trig_a = sbuf([P, S], F32, "trig_a")
+                trig_a = opening_trig[:, S:]
                 unload(1, HALF, trig_a, pair_a)
                 multiply(room_a, pair_a, trig_a)
             hsum = turn(parts(rooms[u], j1 - j0), j1 - j0)
@@ -305,34 +305,27 @@ def tile_list_burst_derotation_kernel(
             place(0, j0, j1, gained)
 
         hsum_a = turn(parts(room_a), HALF)
-        z0_rounded = []
-        for s in range(1, SLICES):
-            trig_b = sbuf([P, S], F32, "z0_codes" if s == FINAL else "trig_b")
-            pair_b = sbuf([P, S], F32, "ref3" if s == FINAL else "pair_b")
-            spare = 2 * FINAL + 2
+        for s in range(1, STEPPED):
+            lower = sbuf([P, 2 * S], F32, "lower")
+            trig_b = lower[:, 0:S]
+            pair_b = lower[:, S:]
+            spare = 2 * PACK + 4
             room_b = halves[:, 2 * s : spare + 1 : spare - 2 * s, :]
             unload(s, 0, trig_b, pair_b)
             multiply(room_b, parts(pair_b), parts(trig_b))
-            if s == FINAL:
-                nc.scalar.copy(out=last_h[:, 0:HALF], in_=turn(room_b, HALF))
-                break
             room_a = arena[:, PICKS * (s - 1) : PICKS * s]
             if s == 1:
-                trig_a = sbuf([P, S], F32, "rounded%d" % HALF)
-                unload(s + 1, HALF, trig_a, spans[0][:, HALF:])
-                multiply(room_a, spans[0][:, HALF:], trig_a)
+                second = sbuf([P, 2 * S], F32, "sixth")
+                unload(s + 1, HALF, second[:, S:], spans[0][:, HALF:])
+                multiply(room_a, spans[0][:, HALF:], second[:, S:])
             else:
                 unload(s + 1, HALF, factors[s][:, HALF:], spans[s - 1][:, HALF:])
                 multiply(arena[:, PICKS * (s - 1) - HALF : PICKS * s], spans[s - 1], factors[s])
-            if PACK < s + 3 < FINAL:
+            if s + 3 == STEPPED - 1:
                 load_factors(s + 3)
-            if s in ROUNDS:
-                rounded = sbuf([P, HALF, PACK], BF16, "rounded%d" % ROUNDS[s])
-                round_planes(rounded, z_back[:, :, ROUNDS[s] : ROUNDS[s] + HALF], nc.scalar.copy)
-                z0_rounded.append(rounded)
             hsum_b = turn(room_b, HALF)
             if s == 1:
-                gained = sbuf([P, S], F32, "rounded0")
+                gained = second[:, 0:S]
                 nc.vector.tensor_tensor(out=gained[:, HALF:S], in0=hsum_a, in1=gains[s][:, HALF:S], op=MULT)
             else:
                 gained = arena[:, PICKS * (s - 2) : PICKS * (s - 1)]
@@ -344,15 +337,13 @@ def tile_list_burst_derotation_kernel(
                 dealt = [later[:, n].rearrange("p i (m t) -> p m i t", t=PACK)[:, :, :, t0 : t0 + 2] for n in range(2)]
                 quantise_late(PACK + t0, 2, dealt)
             if s == PACK - 1:
-                z1 = sbuf([P, 2 * PICKS + HALF], F32, "later")
-                spans.extend([z1[:, PICKS * t : PICKS * t + HALF + S] for t in range(2)])
+                late = sbuf([P, PACK * S], F32, "later")
+                spans.append(late[:, 0 : HALF + S])
             hsum_a = turn(parts(room_a), HALF)
-            if s + 1 == FINAL:
-                last_h = sbuf([P, S], F32, "last_h")
-                nc.scalar.copy(out=last_h[:, HALF:S], in_=hsum_a)
-            for m0, m1 in ((0, PICKS),) if s == 1 else ((HALF, PICKS), (0, HALF)):
-                fetch(spans[s - 1][:, m0:m1], s - 1, m0, m1)
-            if s + 1 < FINAL:
+            if s <= PACK:
+                for m0, m1 in ((0, PICKS),) if s == 1 else ((HALF, PICKS), (0, HALF)):
+                    fetch(spans[s - 1][:, m0:m1], s - 1, m0, m1)
+            if s + 1 < STEPPED:
                 nc.scalar.copy(out=spans[s][:, 0:HALF], in_=hsum_a)
             if s <= PACK:
                 nc.sync.dma_start(out=out[P * (s - 1) : P * s, :], in_=spans[s - 1][:, 0:PICKS])
@@ -360,54 +351,83 @@ def tile_list_burst_derotation_kernel(
                 z_back = sbuf([P, PACK, PICKS], F32, "wide")
                 nc.sync.dma_start(out=z_back, in_=out.rearrange("(p t) m -> p t m", t=PACK))
             place(s, 0, S, gained)
-            if s + 1 == FINAL:
-                grouped = [sbuf([P, m1 - m0, PACK], BF16, "grouped%d" % m0) for m0, m1 in pieces]
-                planes = z1[:, 0 : 2 * PICKS].rearrange("p (t m) -> p t m", t=2)
-                for n, (m0, m1) in enumerate(pieces):
-                    round_planes(grouped[n][:, :, 0:2], planes[:, :, m0:m1], nc.scalar.copy)
 
-        refs.extend(load_ref(dealt_ref, 2, "ref3"))
-        z_codes = [sbuf([P, PICKS], U32, "z0_codes"), sbuf([P, PICKS], U32, "z1_codes")]
-        z_plane = sbuf([P, PASSES, PICKS], U8, "z_plane")
-        for m0, rounded in zip((0, HALF), z0_rounded):
-            quantise(rounded.rearrange("p m t -> p (m t)"), z_codes[0][:, m0 : m0 + HALF], z_plane[:, 0, m0 : m0 + HALF])
-        nc.vector.tensor_tensor(pages[page_of(FINAL)][:].indirect(idx2[:]), last_h, last_gains, MULT)
+        sixth = sbuf([P, 2 * S], F32, "sixth")
+        sixth_h = sixth[:, 0:S]
+        last_h = sbuf([P, S], F32, "last_h")
+        nc.scalar.copy(out=sixth_h[:, HALF:S], in_=hsum_a)
+        trig_two = sbuf([P, 2 * S], F32, "opening_trig")
+        pair_two = late[:, HALF + S : HALF + 3 * S]
+        room_two = sbuf([P, 2 * S], F32, "lower")
+        unload(STEPPED, 0, trig_two[:, 0:S], pair_two[:, 0:S])
+        unload(FINAL, HALF, trig_two[:, S:], pair_two[:, S:])
+        multiply(room_two, pair_two, trig_two)
+        unload(FINAL, 0, sixth[:, S:], late[:, 0:S])
+        multiply(arena[:, 2 * S : 3 * S], late[:, 0:S], sixth[:, S:])
+        nc.scalar.copy(out=sixth_h[:, 0:HALF], in_=turn(parts(room_two[:, 0:S]), HALF))
+        nc.scalar.copy(out=last_h[:, HALF:S], in_=turn(parts(room_two[:, S:]), HALF))
+        nc.scalar.copy(out=last_h[:, 0:HALF], in_=turn(parts(arena[:, 2 * S : 3 * S]), HALF))
+        for t, h in enumerate((sixth_h, last_h)):
+            nc.vector.tensor_tensor(pages[page_of(STEPPED + t)][:].indirect(idx2[:]), h, last_gains[:, t, :], MULT)
+
         w4_codes = sbuf([P, PASSES, N], I32, "w4_codes")
         nc.sync.dma_start(out=w4_codes, in_=w4_words.rearrange("a p c i -> p a (c i)").bitcast(I32))
-        banks = ["phase", "phase", "inph", "inph", "quad", "quad", "hsum", "hsum"]
+        late_refs = sbuf([P, PACK, PICKS], F32, "arena")
+        nc.sync.dma_start(out=late_refs, in_=dealt_ref)
+        refs.extend([late_refs[:, t, :] for t in range(PACK)])
+        z_codes = [sbuf([P, PICKS], U32, "z0_codes"), sbuf([P, PICKS], U32, "z1_codes")]
+        z_plane = sbuf([P, PASSES, PICKS], U8, "z_plane")
+        rounded = sbuf([P, PICKS * PACK], BF16, "later")
+        for m0 in (0, HALF):
+            half = rounded[:, PACK * m0 : PACK * (m0 + HALF)]
+            round_planes(half.rearrange("p (m t) -> p m t", t=PACK), z_back[:, :, m0 : m0 + HALF], nc.scalar.copy)
+        quantise(rounded, z_codes[0], z_plane[:, 0, :])
 
-        def last_product(c, b, m0, m1):
-            base = PIECE * (c // 2)
-            for n in range(2):
-                rows = slice(P * (2 * (c % 2) + n), P * (2 * (c % 2) + n + 1))
+        def last_product(acc, rows, b, m0, m1):
+            for n, row in enumerate(rows):
                 nc.tensor.matmul_mx(
-                    out=accs[c][:, n, m0 - base : m1 - base],
-                    lhsT=w4_codes[:, b, rows].bitcast(FP8X4),
-                    lhsT_scale=w4_plane[:, b, rows],
+                    out=acc[:, n, :],
+                    lhsT=w4_codes[:, b, P * row : P * (row + 1)].bitcast(FP8X4),
+                    lhsT_scale=w4_plane[:, b, P * row : P * (row + 1)],
                     rhs=z_codes[b][:, m0:m1].bitcast(FP8X4),
                     rhs_scale=z_plane[:, b, m0:m1],
                     start=(b == 0 and n == 0),
-                    stop=(b == PASSES - 1 and n == 1 and m1 == base + PIECE),
+                    stop=(b == PASSES - 1 and n == len(rows) - 1),
                 )
 
+        blocks = N // P
+        sums = []
+        for m0, m1 in pieces:
+            count = blocks if m1 - m0 == P and m1 < PICKS else blocks // 2
+            sums.append([range(r, r + count) for r in range(0, blocks, count)])
+        tags = ["phase", "phase", "inph", "inph", "quad", "quad", "hsum", "hsum", "phase"]
         accs = []
-        for c, tag in enumerate(banks):
-            acc = psum.tile([P, 2, PIECE], F32, name="acc", tag=tag, bufs=2)
+
+        def open_sum(rows, m0, m1):
+            acc = psum.tile([P, len(rows), m1 - m0], F32, name="acc", tag=tags[len(accs)], bufs=2)
             accs.append(acc)
-            last_product(c, 0, PIECE * (c // 2), PIECE * (c // 2 + 1))
-        result = sbuf([P, len(banks), 2, PIECE], F32, "wide")
+            last_product(acc, rows, 0, m0, m1)
+
         for n, (m0, m1) in enumerate(pieces):
-            picked = sbuf([P, 2, m1 - m0], F32, "picked", 2)
-            for t in range(2):
-                fetch(picked[:, t, :], FINAL - 1 + t, m0, m1)
-            round_planes(grouped[n][:, :, 2:4], picked, nc.scalar.copy if m0 < SCALAR_ROUNDS else nc.vector.tensor_copy)
-            quantise(grouped[n].rearrange("p m t -> p (m t)"), z_codes[1][:, m0:m1], z_plane[:, 1, m0:m1])
-            for c in (2 * (m0 // PIECE), 2 * (m0 // PIECE) + 1):
-                last_product(c, 1, m0, m1)
-                if m1 % PIECE == 0:
-                    copy = nc.vector.tensor_copy if c in VECTOR_BANKS else nc.scalar.copy
-                    copy(out=result[:, c], in_=accs[c][:])
-                    nc.sync.dma_start(
-                        out=out.rearrange("(n p) m -> p n m", p=P)[:, 2 * (c % 2) : 2 * (c % 2) + 2, PIECE * (c // 2) : PIECE * (c // 2 + 1)],
-                        in_=result[:, c],
-                    )
+            for rows in sums[n]:
+                if len(accs) < len(tags) - 1:
+                    open_sum(rows, m0, m1)
+        result = sbuf([P, blocks * PICKS], F32, "wide")
+        c = 0
+        for n, (m0, m1) in enumerate(pieces):
+            picked = sbuf([P, PACK, m1 - m0], F32, ("last_h", "last_gains")[n % 2])
+            for t in range(PACK):
+                fetch(picked[:, t, :], PACK + t, m0, m1)
+            grouped = sbuf([P, m1 - m0, PACK], BF16, "grouped%d" % m0)
+            round_planes(grouped, picked, nc.scalar.copy if m0 < SCALAR_ROUNDS else nc.vector.tensor_copy)
+            quantise(grouped.rearrange("p m t -> p (m t)"), z_codes[1][:, m0:m1], z_plane[:, 1, m0:m1])
+            for rows in sums[n]:
+                if c == len(accs):
+                    open_sum(rows, m0, m1)
+                last_product(accs[c], rows, 1, m0, m1)
+                first = blocks * m0 + rows.start * (m1 - m0)
+                done = result[:, first : first + len(rows) * (m1 - m0)].rearrange("p (n m) -> p n m", n=len(rows))
+                copy = nc.vector.tensor_copy if c == len(tags) - 1 else nc.scalar.copy
+                copy(out=done, in_=accs[c][:])
+                nc.sync.dma_start(out=out.rearrange("(n p) m -> p n m", p=P)[:, rows.start : rows.stop, m0:m1], in_=done)
+                c = c + 1

@@ -85,14 +85,12 @@ def tile_list_burst_derotation_kernel(
 
         idx = lists.tile([P, S // 16], U16)
         nc.sync.dma_start(idx[:], offs)
-        w2_late = frames.tile([P, 2 * PASS], U8, align_bytes=64, offset=4 * T2 - PASS)
-        nc.sync.dma_start(out=w2_late[:].bitcast(I32), in_=w2_words[0][:, 2 * PASS : 2 * H].bitcast(I32))
-        w2_raw = keep.tile([P, 2 * PASS], U8, align_bytes=64)
-        nc.sync.dma_start(out=w2_raw[:].bitcast(I32), in_=w2_words[0][:, 0 : 2 * PASS].bitcast(I32))
+        raw1 = [load_weight(w1, 0, P, "raw1a")]
+        w2_raw = keep.tile([P, 2 * H], U8, align_bytes=64)
+        nc.sync.dma_start(out=w2_raw[:].bitcast(I32), in_=w2_words[0].bitcast(I32))
         load_scale_rows(nc.sync, tab_plane, tab_scales[0])
         tab = keep.tile([P, T], I32, tag="wide", align_bytes=64)
         nc.sync.dma_start(out=tab[:], in_=tab_words[0].rearrange("p t i -> p (t i)").bitcast(I32))
-        raw1 = [load_weight(w1, 0, P, "raw1a")]
         raw3 = [load_weight(w3, 0, P, "raw3a")]
         load_scale_rows(nc.sync, w2_rows, w2_scales[0])
         plain_gains = keep.tile([P, S], F32)
@@ -159,15 +157,11 @@ def tile_list_burst_derotation_kernel(
                 weights[s0 + t] = [(codes[:, n, t, :].bitcast(FP8X4), plane[:, n, t, :]) for n in range(2)]
             return codes.rearrange("p n t m -> p (n t m)"), plane.rearrange("p n t m -> p (n t m)")
 
-        def cast_rooms(*tags):
-            return [sbuf([P, PIECE], F32, tag) for tag in tags]
+        def round_early(room, raw):
+            nc.vector.tensor_copy(out=room.bitcast(BF16).rearrange("p (c i) -> p c i", i=PACK), in_=raw.rearrange("p i c -> p c i"))
 
-        def quantise_early(s, copy, rooms):
-            codes, plane = quantised(s, 1)
-            for n, raw in enumerate((raw1[s], raw3[s])):
-                grouped = rooms[n].bitcast(BF16).rearrange("p (c i) -> p c i", i=PACK)
-                copy(out=grouped, in_=raw.rearrange("p i c -> p c i"))
-                quantise(grouped.rearrange("p c i -> p (c i)"), codes[:, P * n : P * (n + 1)], plane[:, P * n : P * (n + 1)])
+        def quantise_early(room, n, codes, plane):
+            quantise(room.bitcast(BF16), codes[:, P * n : P * (n + 1)], plane[:, P * n : P * (n + 1)])
 
         staging = arena[:, LEAD + PACK * PICKS :].bitcast(BF16)
 
@@ -179,13 +173,17 @@ def tile_list_burst_derotation_kernel(
                 nc.scalar.copy(out=grouped, in_=source)
             quantise(both, *quantised(s0, count))
 
-        v_plane = sbuf([P, S], U8, "v_plane")
-        nc.vector.tensor_copy(v_plane, tab_plane[:].indirect(idx[:]))
+        first_weights = quantised(0, 1)
+        first_room = frames.tile([P, PIECE], F32, align_bytes=64, offset=4 * T2 - PASS)
+        round_early(first_room[:], raw1[0])
         w2_dealt = sbuf([P, 2 * PASS], U8, "w2_dealt")
         nc.vector.tensor_copy(
             out=w2_dealt.bitcast(U16).rearrange("p (t m) -> p t m", t=PACK),
-            in_=w2_late[:].bitcast(U16).rearrange("p (m t) -> p t m", t=PACK),
+            in_=w2_raw[:, 2 * PASS : 2 * H].bitcast(U16).rearrange("p (m t) -> p t m", t=PACK),
         )
+        quantise_early(first_room[:], 0, *first_weights)
+        v_plane = sbuf([P, S], U8, "v_plane")
+        nc.vector.tensor_copy(v_plane, tab_plane[:].indirect(idx[:]))
         for t in range(2, PAGES):
             page = frames.tile([P, T2], F32, name="page%d" % t, align_bytes=64, offset=4 * T2 * (t - 2))
             nc.gpsimd.memset(page[:], 0.0)
@@ -198,7 +196,9 @@ def tile_list_burst_derotation_kernel(
             v_codes.append(words)
 
         gather_words(0)
-        quantise_early(0, nc.vector.tensor_copy, cast_rooms("cast0", "v_codes1"))
+        second_room = sbuf([P, PIECE], F32, "v_codes1")
+        round_early(second_room, raw3[0])
+        quantise_early(second_room, 1, *first_weights)
         gather_words(1)
         w2_plane = sbuf([P, PASS], U8, "w2_plane")
         nc.vector.tensor_copy(
@@ -285,7 +285,10 @@ def tile_list_burst_derotation_kernel(
         opening_trig = sbuf([P, 2 * S], F32, "opening_trig")
         trigs = [sbuf([P, HALF], F32, "grouped0"), early[:, 0:HALF], opening_trig[:, 0:S]]
         derotate_on_vector(*opening[0], trigs[0], rooms[0])
-        quantise_early(1, nc.vector.tensor_copy, [rooms[1][:, 0:PIECE], rooms[1][:, PIECE:HALF]])
+        second_weights = quantised(1, 1)
+        for n, raw in enumerate((raw1[1], raw3[1])):
+            round_early(rooms[1][:, PIECE * n : PIECE * (n + 1)], raw)
+            quantise_early(rooms[1][:, PIECE * n : PIECE * (n + 1)], n, *second_weights)
         derotate_on_vector(*opening[1], trigs[1], rooms[1])
         for u, (j0, j1) in enumerate(opening):
             if u == 0:

@@ -32,7 +32,6 @@ FINAL = SLICES - 1
 STEPPED = FINAL - 1
 LEAD = 3 * HALF
 DEALT_CASTS = {2: 0, 3: 2}
-SCALAR_ROUNDS = 896
 
 
 def page_of(s):
@@ -209,8 +208,7 @@ def tile_list_burst_derotation_kernel(
         z0 = sbuf([P, PACK * PICKS + HALF], F32, "wide")
         spans = [z0[:, PICKS * t : PICKS * t + HALF + S] for t in range(PACK)]
 
-        def first_product(j0, j1, tag, codes, plane):
-            bank = psum.tile([P, j1 - j0], F32, name=tag, tag=tag, bufs=2)
+        def first_product(j0, j1, bank, codes, plane):
             for j in range(j0, j1, P):
                 nc.tensor.matmul_mx(
                     out=bank[:, j - j0 : j - j0 + P],
@@ -221,31 +219,37 @@ def tile_list_burst_derotation_kernel(
                     start=True,
                     stop=True,
                 )
+
+        def new_bank(tag):
+            bank = psum.tile([P, HALF], F32, name=tag, tag=tag, bufs=2)
             return bank[:]
 
-        def features(s, j0, j1):
+        def features(s, j0, j1, phase, inph, quad):
             b, t = divmod(s, PACK)
             cols = slice(P * t, P * (t + 1))
-            phase = first_product(j0, j1, "phase", *weights[s][0])
-            inph = first_product(j0, j1, "inph", q2[b][0][:, 2 * P * t : 2 * P * (t + 1)].bitcast(FP4X4), q2[b][1][:, cols])
-            quad = first_product(j0, j1, "quad", *weights[s][1])
-            return phase, inph, quad
+            first_product(j0, j1, phase, *weights[s][0])
+            first_product(j0, j1, inph, q2[b][0][:, 2 * P * t : 2 * P * (t + 1)].bitcast(FP4X4), q2[b][1][:, cols])
+            first_product(j0, j1, quad, *weights[s][1])
 
         def cosine(out, size):
             nc.scalar.activation(out=out, in_=size, func=ACT.Sin, scale=-1.0, bias=math.pi / 2)
 
-        def derotate_on_vector(j0, j1, trig, room):
+        def derotate_on_vector(j0, j1, trig, room, tags):
             width = j1 - j0
-            phase, inph, quad = features(0, j0, j1)
+            phase = new_bank("phase")[:, 0:width]
+            banks = [new_bank(tag) for tag in tags]
+            features(0, j0, j1, phase, banks[0][:, 0:width], banks[-1][:, HALF - width : HALF])
             size = sbuf([P, width], F32, "size", 2)
             nc.scalar.activation(out=trig[:, width : 2 * width], in_=phase, func=ACT.Sin)
             nc.scalar.activation(out=size, in_=phase, func=ACT.Abs)
             cosine(trig[:, 0:width], size)
-            nc.vector.tensor_tensor(out=room[:, 0:width], in0=inph, in1=trig[:, 0:width], op=MULT)
-            nc.vector.tensor_tensor(out=room[:, width : 2 * width], in0=quad, in1=trig[:, width : 2 * width], op=MULT)
+            for n, bank in enumerate(banks):
+                cols = slice(HALF * n, HALF * (n + 1))
+                nc.vector.tensor_tensor(out=room[:, cols], in0=bank, in1=trig[:, cols], op=MULT)
 
         def unload(s, j0, trig, pair):
-            phase, inph, quad = features(s, j0, j0 + HALF)
+            phase, inph, quad = new_bank("phase"), new_bank("inph"), new_bank("quad")
+            features(s, j0, j0 + HALF, phase, inph, quad)
             size = sbuf([P, HALF], F32, "size", 2)
             nc.scalar.activation(out=size, in_=phase, func=ACT.Abs)
             nc.scalar.activation(out=trig[:, HALF:S], in_=phase, func=ACT.Sin)
@@ -284,15 +288,15 @@ def tile_list_burst_derotation_kernel(
         early = sbuf([P, PIECE + S], F32, "early")
         opening_trig = sbuf([P, 2 * S], F32, "opening_trig")
         trigs = [sbuf([P, HALF], F32, "grouped0"), early[:, 0:HALF], opening_trig[:, 0:S]]
-        derotate_on_vector(*opening[0], trigs[0], rooms[0])
+        derotate_on_vector(*opening[0], trigs[0], rooms[0], ["inph"])
         second_weights = quantised(1, 1)
         for n, raw in enumerate((raw1[1], raw3[1])):
             round_early(rooms[1][:, PIECE * n : PIECE * (n + 1)], raw)
             quantise_early(rooms[1][:, PIECE * n : PIECE * (n + 1)], n, *second_weights)
-        derotate_on_vector(*opening[1], trigs[1], rooms[1])
+        derotate_on_vector(*opening[1], trigs[1], rooms[1], ["quad"])
         for u, (j0, j1) in enumerate(opening):
             if u == 0:
-                derotate_on_vector(*opening[2], trigs[2], rooms[2])
+                derotate_on_vector(*opening[2], trigs[2], rooms[2], ["inph", "quad"])
                 both = trigs[1].bitcast(BF16)
                 gpsimd_round(both.rearrange("p (n c i) -> p n c i", n=2, i=PACK), raw_both.rearrange("p n i c -> p n c i"))
                 quantise(both, *quantised(2, 1))
@@ -378,59 +382,67 @@ def tile_list_burst_derotation_kernel(
         late_refs = sbuf([P, PACK, PICKS], F32, "arena")
         nc.sync.dma_start(out=late_refs, in_=dealt_ref)
         refs.extend([late_refs[:, t, :] for t in range(PACK)])
-        z_codes = [sbuf([P, PICKS], U32, "z0_codes"), sbuf([P, PICKS], U32, "z1_codes")]
-        z_plane = sbuf([P, PASSES, PICKS], U8, "z_plane")
-        rounded = sbuf([P, PICKS * PACK], BF16, "later")
-        for m0 in (0, HALF):
-            half = rounded[:, PACK * m0 : PACK * (m0 + HALF)]
-            round_planes(half.rearrange("p (m t) -> p m t", t=PACK), z_back[:, :, m0 : m0 + HALF], nc.scalar.copy)
-        quantise(rounded, z_codes[0], z_plane[:, 0, :])
+        z_codes = sbuf([P, PASSES * PICKS], U32, "sixth")
+        z_plane = sbuf([P, PASSES * PICKS], U8, "z_plane")
+        rounded = sbuf([P, PASSES * PICKS * PACK], BF16, "later")
+        first_pass = [(m0, m0 + PIECE) for m0 in range(0, PICKS, PIECE)]
+
+        def z_column(b, m):
+            return PIECE * (m // PIECE + b) + m
+
+        def rounded_columns(b, m0, m1):
+            return rounded[:, PACK * z_column(b, m0) : PACK * (z_column(b, m0) + m1 - m0)].rearrange("p (m t) -> p m t", t=PACK)
+
+        for m0, m1 in first_pass:
+            round_planes(rounded_columns(0, m0, m1), z_back[:, :, m0:m1], nc.scalar.copy)
 
         def last_product(acc, rows, b, m0, m1):
+            cols = slice(z_column(b, m0), z_column(b, m0) + m1 - m0)
             for n, row in enumerate(rows):
                 nc.tensor.matmul_mx(
                     out=acc[:, n, :],
                     lhsT=w4_codes[:, b, P * row : P * (row + 1)].bitcast(FP8X4),
                     lhsT_scale=w4_plane[:, b, P * row : P * (row + 1)],
-                    rhs=z_codes[b][:, m0:m1].bitcast(FP8X4),
-                    rhs_scale=z_plane[:, b, m0:m1],
+                    rhs=z_codes[:, cols].bitcast(FP8X4),
+                    rhs_scale=z_plane[:, cols],
                     start=(b == 0 and n == 0),
                     stop=(b == PASSES - 1 and n == len(rows) - 1),
                 )
 
         blocks = N // P
-        sums = []
-        for m0, m1 in pieces:
-            count = blocks if m1 - m0 == P and m1 < PICKS else blocks // 2
-            sums.append([range(r, r + count) for r in range(0, blocks, count)])
-        tags = ["phase", "phase", "inph", "inph", "quad", "quad", "hsum", "hsum", "phase"]
-        accs = []
-
-        def open_sum(rows, m0, m1):
-            acc = psum.tile([P, len(rows), m1 - m0], F32, name="acc", tag=tags[len(accs)], bufs=2)
-            accs.append(acc)
-            last_product(acc, rows, 0, m0, m1)
-
-        for n, (m0, m1) in enumerate(pieces):
-            for rows in sums[n]:
-                if len(accs) < len(tags) - 1:
-                    open_sum(rows, m0, m1)
         result = sbuf([P, blocks * PICKS], F32, "wide")
-        c = 0
-        for n, (m0, m1) in enumerate(pieces):
+
+        def pick(n):
+            m0, m1 = pieces[n]
             picked = sbuf([P, PACK, m1 - m0], F32, ("last_h", "last_gains")[n % 2])
             for t in range(PACK):
                 fetch(picked[:, t, :], PACK + t, m0, m1)
-            grouped = sbuf([P, m1 - m0, PACK], BF16, "grouped%d" % m0)
-            round_planes(grouped, picked, nc.scalar.copy if m0 < SCALAR_ROUNDS else nc.vector.tensor_copy)
-            quantise(grouped.rearrange("p m t -> p (m t)"), z_codes[1][:, m0:m1], z_plane[:, 1, m0:m1])
-            for rows in sums[n]:
-                if c == len(accs):
-                    open_sum(rows, m0, m1)
-                last_product(accs[c], rows, 1, m0, m1)
-                first = blocks * m0 + rows.start * (m1 - m0)
-                done = result[:, first : first + len(rows) * (m1 - m0)].rearrange("p (n m) -> p n m", n=len(rows))
-                copy = nc.vector.tensor_copy if c == len(tags) - 1 else nc.scalar.copy
-                copy(out=done, in_=accs[c][:])
-                nc.sync.dma_start(out=out.rearrange("(n p) m -> p n m", p=P)[:, rows.start : rows.stop, m0:m1], in_=done)
-                c = c + 1
+            return picked
+
+        def finish(n, banks, source):
+            m0, m1 = pieces[n]
+            c0 = z_column(0 if m0 % PIECE == 0 else 1, m0)
+            c1 = z_column(1, m0) + m1 - m0
+            quantise(rounded[:, PACK * source : PACK * (source + c1 - c0)], z_codes[:, c0:c1], z_plane[:, c0:c1])
+            count = blocks // len(banks)
+            for r, (tag, copy) in zip(range(0, blocks, count), banks):
+                acc = psum.tile([P, count, m1 - m0], F32, name="acc", tag=tag, bufs=2)
+                for b in range(PASSES):
+                    last_product(acc, range(r, r + count), b, m0, m1)
+                first = blocks * m0 + r * (m1 - m0)
+                done = result[:, first : first + count * (m1 - m0)].rearrange("p (n m) -> p n m", n=count)
+                copy(out=done, in_=acc[:])
+                nc.sync.dma_start(out=out.rearrange("(n p) m -> p n m", p=P)[:, r : r + count, m0:m1], in_=done)
+
+        banks = [[(tag, nc.scalar.copy)] * 2 for tag in ("phase", "inph", "quad")]
+        banks.append([("hsum", nc.scalar.copy)])
+        banks.append([("hsum", nc.scalar.copy), ("phase", nc.vector.tensor_copy)])
+        last = len(pieces) - 1
+        round_planes(rounded_columns(1, *pieces[0]), pick(0), nc.scalar.copy)
+        for n in range(last):
+            picked = pick(n + 1)
+            if n + 1 < last:
+                round_planes(rounded_columns(1, *pieces[n + 1]), picked, nc.scalar.copy)
+            finish(n, banks[n], z_column(0, pieces[n][0]))
+        round_planes(rounded_columns(0, *pieces[last - 1]), picked, nc.vector.tensor_copy)
+        finish(last, banks[last], z_column(0, pieces[last - 1][0]))

@@ -30,14 +30,13 @@ CUTS = (0, 256, 512, 768, 896, 1024)
 PAGES = PACK
 FINAL = SLICES - 1
 STEPPED = FINAL - 1
-LEAD = 3 * HALF
 DEALT_CASTS = {2: 0, 3: 2}
 
 
 def page_of(s):
     if s < PACK:
-        return (max(s, 1) + 1) % 2
-    return (s + 1) % PAGES
+        return s % 2
+    return (0, 2, 3, 1)[s - PACK]
 
 
 def load_scale_rows(queue, plane, rows):
@@ -53,6 +52,7 @@ def tile_list_burst_derotation_kernel(
         lists = ctx.enter_context(tc.tile_pool(name="lists", bufs=1))
         keep = ctx.enter_context(tc.tile_pool(name="keep", bufs=1))
         frames = ctx.enter_context(tc.tile_pool(name="frames", bufs=1))
+        staged = ctx.enter_context(tc.tile_pool(name="staged", bufs=1))
         psum = ctx.enter_context(tc.psum_pool(name="psum", bufs=1))
 
         def sbuf(shape, dtype, tag, bufs=1):
@@ -74,9 +74,9 @@ def tile_list_burst_derotation_kernel(
         ident = keep.tile([P, P], F32)
         make_identity(nc, ident[:])
 
-        def load_weight(w, c0, c1, tag):
-            raw = keep.tile([P, PACK, c1 - c0], F32, name="raw", tag=tag, align_bytes=64)
-            nc.sync.dma_start(out=raw[:], in_=w[:, c0:c1].rearrange("(p i) c -> p i c", i=PACK))
+        def load_weight(n, s):
+            raw = staged.tile([P, PACK, P], F32, name="raw%d_%d" % (n, s), align_bytes=64, offset=4 * PASS * (2 * s + n))
+            nc.sync.dma_start(out=raw[:], in_=(w1, w3)[n][:, P * s : P * (s + 1)].rearrange("(p i) c -> p i c", i=PACK))
             return raw[:]
 
         plain_ref = ref[0:PASS].rearrange("(t p) m -> p t m", p=P)
@@ -84,35 +84,32 @@ def tile_list_burst_derotation_kernel(
 
         idx = lists.tile([P, S // 16], U16)
         nc.sync.dma_start(idx[:], offs)
-        raw1 = [load_weight(w1, 0, P, "raw1a")]
+        raw1 = [load_weight(0, 0)]
         w2_raw = keep.tile([P, 2 * H], U8, align_bytes=64)
         nc.sync.dma_start(out=w2_raw[:].bitcast(I32), in_=w2_words[0].bitcast(I32))
         load_scale_rows(nc.sync, tab_plane, tab_scales[0])
         tab = keep.tile([P, T], I32, tag="wide", align_bytes=64)
         nc.sync.dma_start(out=tab[:], in_=tab_words[0].rearrange("p t i -> p (t i)").bitcast(I32))
-        raw3 = [load_weight(w3, 0, P, "raw3a")]
+        raw3 = [load_weight(1, 0)]
         load_scale_rows(nc.sync, w2_rows, w2_scales[0])
         plain_gains = keep.tile([P, S], F32)
-        raw1.append(load_weight(w1, P, 2 * P, "raw1b"))
-        raw3.append(load_weight(w3, P, 2 * P, "raw3b"))
+        raw1.append(load_weight(0, 1))
+        raw3.append(load_weight(1, 1))
         nc.sync.dma_start(out=plain_gains[:, 0:HALF], in_=wgs[:, 0:HALF])
         idx2 = lists.tile([P, S // 16], U16)
         nc.sync.dma_start(idx2[:], offs2)
-        raw_both = sbuf([P, 2, PACK, P], F32, "raw_both")
+        raw_both = staged.tile([P, 2, PACK, P], F32, name="raw_both", align_bytes=64, offset=16 * PASS)[:]
         for n, w in enumerate((w1, w3)):
             nc.sync.dma_start(out=raw_both[:, n], in_=w[:, 2 * P : 3 * P].rearrange("(p i) c -> p i c", i=PACK))
         nc.sync.dma_start(out=plain_gains[:, HALF:S], in_=wgs[:, HALF:S])
-        raw_last = [load_weight(w1, 3 * P, PASS, "raw1d"), load_weight(w3, 3 * P, PASS, "raw3d")]
+        raw_last = [load_weight(0, 3), load_weight(1, 3)]
         idx3 = lists.tile([P, PICKS // 16], U16)
         nc.sync.dma_start(idx3[:], offs3)
-        arena = sbuf([P, LEAD + (PACK + 1) * PICKS], F32, "arena")
-        halves = arena.rearrange("p (n c) -> p n c", c=HALF)
-        refs = []
-
-        def load_ref_pair(view, t0):
-            rows = arena[:, LEAD + PICKS * len(refs) : LEAD + PICKS * (len(refs) + 2)].rearrange("p (t m) -> p t m", t=2)
-            nc.sync.dma_start(out=rows, in_=view[:, t0 : t0 + 2])
-            refs.extend([rows[:, 0, :], rows[:, 1, :]])
+        arena = sbuf([P, HALF + S + (PACK - 1) * PICKS + 4 * S], F32, "arena")
+        lower_h = arena[:, 0:HALF]
+        starts = {1: HALF, 2: HALF + S + PICKS, 3: HALF + 3 * S + 2 * PICKS}
+        starts.update({4: starts[2], 5: starts[3]})
+        picked_first = {s: arena[:, c : c + PICKS] for s, c in ((1, starts[2] - PICKS), (2, starts[3] - PICKS), (3, starts[3] + 2 * S))}
 
         def load_dealt(dst, t, j0, j1):
             for q in (0, 2, 1, 3):
@@ -126,13 +123,11 @@ def tile_list_burst_derotation_kernel(
                 load_dealt(factors[s][:, 0:HALF], s - PACK, HALF, S)
 
         factors = {}
-        load_ref_pair(plain_ref, 0)
         load_factors(2)
         later = keep.tile([P, 2, PACK, PASS], F32, tag="later", align_bytes=64)
         for n, w in enumerate((w1, w3)):
             nc.sync.dma_start(out=later[:, n], in_=w[:, PASS:H].rearrange("(p i) c -> p i c", i=PACK))
         load_factors(3)
-        load_ref_pair(plain_ref, 2)
         load_factors(4)
         dealt_gains = sbuf([P, 2, HALF], F32, "dealt_gains")
         load_dealt(dealt_gains, slice(0, 2), 0, HALF)
@@ -162,11 +157,8 @@ def tile_list_burst_derotation_kernel(
         def quantise_early(room, n, codes, plane):
             quantise(room.bitcast(BF16), codes[:, P * n : P * (n + 1)], plane[:, P * n : P * (n + 1)])
 
-        staging = arena[:, LEAD + PACK * PICKS :].bitcast(BF16)
-
-        def quantise_late(s0, count, sources):
+        def quantise_late(s0, count, sources, both):
             width = count * PASS
-            both = staging[:, 2 * (S - width) : 2 * S]
             for n, source in enumerate(sources):
                 grouped = both[:, width * n : width * (n + 1)].rearrange("p (t m i) -> p m i t", t=count, i=PACK)
                 nc.scalar.copy(out=grouped, in_=source)
@@ -205,8 +197,8 @@ def tile_list_burst_derotation_kernel(
             in_=w2_rows[:, PASS:H].rearrange("p (m t) -> p t m", t=PACK),
         )
         q2 = [(w2_raw, w2_rows), (w2_dealt, w2_plane)]
-        z0 = sbuf([P, PACK * PICKS + HALF], F32, "wide")
-        spans = [z0[:, PICKS * t : PICKS * t + HALF + S] for t in range(PACK)]
+        inputs = sbuf([P, PACK * S], F32, "wide")
+        spans = [inputs[:, (HALF + S) * t : (HALF + S) * (t + 1)] for t in range(2)]
 
         def first_product(j0, j1, bank, codes, plane):
             for j in range(j0, j1, P):
@@ -276,7 +268,7 @@ def tile_list_burst_derotation_kernel(
             nc.vector.tensor_copy(pages[page_of(s)][:].indirect(idx2[:, j0 // 16 : j1 // 16]), gained)
 
         def fetch(dst, s, m0, m1):
-            nc.vector.tensor_tensor(dst, pages[page_of(s)][:].indirect(idx3[:, m0 // 16 : m1 // 16]), refs[s][:, m0:m1], ADD)
+            nc.vector.tensor_tensor(dst, pages[page_of(s)][:].indirect(idx3[:, m0 // 16 : m1 // 16]), late_refs[:, s - PACK, m0:m1], ADD)
 
         def round_planes(out, z, copy):
             copy(out=out.rearrange("p (c e) t -> p c t e", e=4), in_=z.rearrange("p t (c e) -> p c t e", e=4))
@@ -312,76 +304,73 @@ def tile_list_burst_derotation_kernel(
             place(0, j0, j1, gained)
 
         hsum_a = turn(parts(room_a), HALF)
+        picked_first[0] = sbuf([P, PICKS], F32, "early")
         for s in range(1, STEPPED):
             lower = sbuf([P, 2 * S], F32, "lower")
-            trig_b = lower[:, 0:S]
-            pair_b = lower[:, S:]
-            spare = 2 * PACK + 4
-            room_b = halves[:, 2 * s : spare + 1 : spare - 2 * s, :]
-            unload(s, 0, trig_b, pair_b)
-            multiply(room_b, parts(pair_b), parts(trig_b))
-            room_a = arena[:, PICKS * (s - 1) : PICKS * s]
+            gained = arena[:, starts[s] : starts[s] + S]
+            room_b = arena.rearrange("p (n c) -> p n c", c=HALF)[:, 0 : starts[s] // HALF + 1 : starts[s] // HALF, :]
+            unload(s, 0, lower[:, 0:S], lower[:, S:])
+            multiply(room_b, parts(lower[:, S:]), parts(lower[:, 0:S]))
+            if s > 1:
+                nc.scalar.copy(out=spans[s % 2][:, 0:HALF], in_=hsum_a)
             if s == 1:
-                second = sbuf([P, 2 * S], F32, "sixth")
-                unload(s + 1, HALF, second[:, S:], spans[0][:, HALF:])
-                multiply(room_a, spans[0][:, HALF:], second[:, S:])
+                room_a = arena[:, starts[3] + S : starts[3] + 2 * S]
+                trig_a = sbuf([P, S], F32, "sixth")
+                unload(s + 1, HALF, trig_a, inputs[:, 3 * S :])
+                multiply(room_a, inputs[:, 3 * S :], trig_a)
             else:
-                unload(s + 1, HALF, factors[s][:, HALF:], spans[s - 1][:, HALF:])
-                multiply(arena[:, PICKS * (s - 1) - HALF : PICKS * s], spans[s - 1], factors[s])
+                room_a = arena[:, starts[s] + S : starts[s] + 2 * S]
+                unload(s + 1, HALF, factors[s][:, HALF:], spans[s % 2][:, HALF:])
+                multiply(arena[:, starts[s] + HALF : starts[s] + 2 * S], spans[s % 2], factors[s])
             if s + 3 == STEPPED - 1:
                 load_factors(s + 3)
             hsum_b = turn(room_b, HALF)
             if s == 1:
-                gained = second[:, 0:S]
                 nc.vector.tensor_tensor(out=gained[:, HALF:S], in0=hsum_a, in1=gains[s][:, HALF:S], op=MULT)
+                sources = [raw.rearrange("p i (m t) -> p m i t", t=1) for raw in raw_last]
+                quantise_late(3, 1, sources, arena[:, PIECE : PIECE + HALF].bitcast(BF16))
             else:
-                gained = arena[:, PICKS * (s - 2) : PICKS * (s - 1)]
-            nc.vector.tensor_tensor(out=gained[:, 0:HALF], in0=hsum_b, in1=gains[s][:, 0:HALF], op=MULT)
-            if s == 1:
-                quantise_late(3, 1, [raw.rearrange("p i (m t) -> p m i t", t=1) for raw in raw_last])
+                nc.scalar.copy(out=lower_h, in_=hsum_b)
             if s in DEALT_CASTS:
                 t0 = DEALT_CASTS[s]
                 dealt = [later[:, n].rearrange("p i (m t) -> p m i t", t=PACK)[:, :, :, t0 : t0 + 2] for n in range(2)]
-                quantise_late(PACK + t0, 2, dealt)
-            if s == PACK - 1:
-                late = sbuf([P, PACK * S], F32, "later")
-                spans.append(late[:, 0 : HALF + S])
+                quantise_late(PACK + t0, 2, dealt, arena[:, starts[s] - HALF : starts[s] + HALF].bitcast(BF16))
+            if s <= PACK:
+                nc.vector.tensor_copy(picked_first[s - 1], pages[page_of(s - 1)][:].indirect(idx3[:]))
+            if s == 1:
+                nc.vector.tensor_tensor(out=gained[:, 0:HALF], in0=hsum_b, in1=gains[s][:, 0:HALF], op=MULT)
+            else:
+                multiply(gained[:, 0:HALF], lower_h, gains[s][:, 0:HALF])
             hsum_a = turn(parts(room_a), HALF)
-            if s <= PACK:
-                for m0, m1 in ((0, PICKS),) if s == 1 else ((HALF, PICKS), (0, HALF)):
-                    fetch(spans[s - 1][:, m0:m1], s - 1, m0, m1)
-            if s + 1 < STEPPED:
-                nc.scalar.copy(out=spans[s][:, 0:HALF], in_=hsum_a)
-            if s <= PACK:
-                nc.sync.dma_start(out=out[P * (s - 1) : P * s, :], in_=spans[s - 1][:, 0:PICKS])
-            if s == PACK:
-                z_back = sbuf([P, PACK, PICKS], F32, "wide")
-                nc.sync.dma_start(out=z_back, in_=out.rearrange("(p t) m -> p t m", t=PACK))
             place(s, 0, S, gained)
 
         sixth = sbuf([P, 2 * S], F32, "sixth")
         sixth_h = sixth[:, 0:S]
         last_h = sbuf([P, S], F32, "last_h")
-        nc.scalar.copy(out=sixth_h[:, HALF:S], in_=hsum_a)
         trig_two = sbuf([P, 2 * S], F32, "opening_trig")
-        pair_two = late[:, HALF + S : HALF + 3 * S]
+        late = sbuf([P, 3 * S], F32, "later")
         room_two = sbuf([P, 2 * S], F32, "lower")
-        unload(STEPPED, 0, trig_two[:, 0:S], pair_two[:, 0:S])
-        unload(FINAL, HALF, trig_two[:, S:], pair_two[:, S:])
-        multiply(room_two, pair_two, trig_two)
-        unload(FINAL, 0, sixth[:, S:], late[:, 0:S])
-        multiply(arena[:, 2 * S : 3 * S], late[:, 0:S], sixth[:, S:])
-        nc.scalar.copy(out=sixth_h[:, 0:HALF], in_=turn(parts(room_two[:, 0:S]), HALF))
-        nc.scalar.copy(out=last_h[:, HALF:S], in_=turn(parts(room_two[:, S:]), HALF))
-        nc.scalar.copy(out=last_h[:, 0:HALF], in_=turn(parts(arena[:, 2 * S : 3 * S]), HALF))
+        last_room = arena[:, starts[4] + S : starts[4] + 2 * S]
+        units = (
+            (STEPPED, 0, trig_two[:, 0:S], room_two[:, 0:S]),
+            (FINAL, HALF, trig_two[:, S:], room_two[:, S:]),
+            (FINAL, 0, sixth[:, S:], last_room),
+        )
+        for u, (s, j0, trig, room) in enumerate(units):
+            unload(s, j0, trig, late[:, S * u : S * (u + 1)])
+            multiply(room, late[:, S * u : S * (u + 1)], trig)
+        nc.scalar.copy(out=sixth_h[:, HALF:S], in_=hsum_a)
+        for (s, j0, trig, room), h in zip(units, (sixth_h, last_h, last_h)):
+            nc.scalar.copy(out=h[:, j0 : j0 + HALF], in_=turn(parts(room), HALF))
         for t, h in enumerate((sixth_h, last_h)):
             nc.vector.tensor_tensor(pages[page_of(STEPPED + t)][:].indirect(idx2[:]), h, last_gains[:, t, :], MULT)
 
         w4_codes = sbuf([P, PASSES, N], I32, "w4_codes")
         nc.sync.dma_start(out=w4_codes, in_=w4_words.rearrange("a p c i -> p a (c i)").bitcast(I32))
-        late_refs = sbuf([P, PACK, PICKS], F32, "arena")
+        late_refs = staged.tile([P, PACK, PICKS], F32, name="late_refs", align_bytes=64, offset=0)[:]
         nc.sync.dma_start(out=late_refs, in_=dealt_ref)
-        refs.extend([late_refs[:, t, :] for t in range(PACK)])
+        first_refs = sbuf([P, PACK, PICKS], F32, "wide")
+        nc.sync.dma_start(out=first_refs, in_=plain_ref)
         z_codes = sbuf([P, PASSES * PICKS], U32, "sixth")
         z_plane = sbuf([P, PASSES * PICKS], U8, "z_plane")
         rounded = sbuf([P, PASSES * PICKS * PACK], BF16, "later")
@@ -394,7 +383,26 @@ def tile_list_burst_derotation_kernel(
             return rounded[:, PACK * z_column(b, m0) : PACK * (z_column(b, m0) + m1 - m0)].rearrange("p (m t) -> p m t", t=PACK)
 
         for m0, m1 in first_pass:
-            round_planes(rounded_columns(0, m0, m1), z_back[:, :, m0:m1], nc.scalar.copy)
+            words = psum.tile([P, 2, 2, P], F32, name="words", tag="quad", bufs=2)
+            for b in range(2):
+                cols = slice(m0 + P * b, m0 + P * (b + 1))
+                turned = new_bank(("phase", "inph")[b])
+                for s in range(PACK):
+                    for n, term in enumerate((picked_first[s], first_refs[:, s, :])):
+                        nc.tensor.matmul(
+                            out=turned[:, P * s : P * (s + 1)], lhsT=term[:, cols], rhs=ident[:], is_transpose=True,
+                            start=(s == 0 and n == 0), stop=(s == PACK - 1 and n == 1),
+                        )
+                pairs = sbuf([P, PASS], BF16, "pairs", 2)
+                nc.scalar.copy(out=pairs, in_=turned)
+                for u in range(2):
+                    nc.tensor.matmul(
+                        out=words[:, b, u, :], lhsT=pairs.bitcast(F32)[:, u : PASS // 2 : 2], rhs=ident[:], is_transpose=True,
+                        start=True, stop=True,
+                    )
+            c0 = PACK * z_column(0, m0)
+            target = rounded[:, c0 : c0 + PACK * PIECE].bitcast(F32).rearrange("p (b m u) -> p b m u", b=2, u=2)
+            nc.scalar.copy(out=target, in_=words[:].rearrange("p b u m -> p b m u"))
 
         def last_product(acc, rows, b, m0, m1):
             cols = slice(z_column(b, m0), z_column(b, m0) + m1 - m0)

@@ -101,8 +101,11 @@ def tile_list_burst_derotation_kernel(
         raw_both = staged.tile([P, 2, PACK, P], F32, name="raw_both", align_bytes=64, offset=16 * PASS)[:]
         for n, w in enumerate((w1, w3)):
             nc.sync.dma_start(out=raw_both[:, n], in_=w[:, 2 * P : 3 * P].rearrange("(p i) c -> p i c", i=PACK))
+        raw_end = 8 * PASS * (PACK + 1)
+        raw_last = staged.tile([P, 2, PACK, P], F32, name="raw_last", align_bytes=64, offset=raw_end - 8 * PASS)[:]
+        for n, w in enumerate((w1, w3)):
+            nc.sync.dma_start(out=raw_last[:, n], in_=w[:, 3 * P : PASS].rearrange("(p i) c -> p i c", i=PACK))
         nc.sync.dma_start(out=plain_gains[:, HALF:S], in_=wgs[:, HALF:S])
-        raw_last = [load_weight(0, 3), load_weight(1, 3)]
         idx3 = lists.tile([P, PICKS // 16], U16)
         nc.sync.dma_start(idx3[:], offs3)
         arena = sbuf([P, HALF + S + (PACK - 1) * PICKS + 4 * S], F32, "arena")
@@ -157,12 +160,9 @@ def tile_list_burst_derotation_kernel(
         def quantise_early(room, n, codes, plane):
             quantise(room.bitcast(BF16), codes[:, P * n : P * (n + 1)], plane[:, P * n : P * (n + 1)])
 
-        def quantise_late(s0, count, sources, both):
-            width = count * PASS
-            for n, source in enumerate(sources):
-                grouped = both[:, width * n : width * (n + 1)].rearrange("p (t m i) -> p m i t", t=count, i=PACK)
-                nc.scalar.copy(out=grouped, in_=source)
-            quantise(both, *quantised(s0, count))
+        def round_dealt(n, t0, both, copy, walk):
+            source = later[:, n].rearrange("p i (m t) -> p i m t", t=PACK)[:, :, :, t0 : t0 + 2].rearrange("p i m t -> " + walk)
+            copy(out=both[:, S * n : S * (n + 1)].rearrange("p (t m i) -> " + walk, t=2, i=PACK), in_=source)
 
         first_weights = quantised(0, 1)
         first_room = frames.tile([P, PIECE], F32, align_bytes=64, offset=4 * T2 - PASS)
@@ -277,7 +277,7 @@ def tile_list_burst_derotation_kernel(
 
         opening = ((0, PIECE), (PIECE, HALF), (HALF, S))
         rooms = [sbuf([P, S], F32, tag) for tag in ("z0_codes", "z1_codes", "last_h")]
-        early = sbuf([P, PIECE + S], F32, "early")
+        early = staged.tile([P, HALF], F32, align_bytes=64, offset=raw_end)
         opening_trig = sbuf([P, 2 * S], F32, "opening_trig")
         trigs = [sbuf([P, HALF], F32, "grouped0"), early[:, 0:HALF], opening_trig[:, 0:S]]
         derotate_on_vector(*opening[0], trigs[0], rooms[0], ["inph"])
@@ -292,30 +292,40 @@ def tile_list_burst_derotation_kernel(
                 both = trigs[1].bitcast(BF16)
                 gpsimd_round(both.rearrange("p (n c i) -> p n c i", n=2, i=PACK), raw_both.rearrange("p n i c -> p n c i"))
                 quantise(both, *quantised(2, 1))
+                third = arena[:, PIECE : PIECE + HALF].bitcast(BF16)
+                gpsimd_round(third.rearrange("p (n c i) -> p n c i", n=2, i=PACK), raw_last.rearrange("p n i c -> p n c i"))
             if u == 2:
-                room_a = early[:, PIECE:]
+                room_a = staged.tile([P, S], F32, name="first_room_a", align_bytes=64, offset=raw_end + 4 * (PIECE - S))[:]
                 pair_a = sbuf([P, S], F32, "z_plane")
                 trig_a = opening_trig[:, S:]
                 unload(1, HALF, trig_a, pair_a)
                 multiply(room_a, pair_a, trig_a)
             hsum = turn(parts(rooms[u], j1 - j0), j1 - j0)
-            gained = (trigs[0][:, 0:PIECE], early[:, 0:PIECE], trigs[2][:, 0:HALF])[u]
+            if u == 1:
+                gained = staged.tile([P, PIECE], F32, name="second_gained", align_bytes=64, offset=raw_end + 4 * PIECE)[:]
+            else:
+                gained = trigs[u][:, 0 : j1 - j0]
             nc.vector.tensor_tensor(out=gained, in0=hsum, in1=gains[0][:, j0:j1], op=MULT)
             place(0, j0, j1, gained)
 
         hsum_a = turn(parts(room_a), HALF)
-        picked_first[0] = sbuf([P, PICKS], F32, "early")
+        picked_first[0] = staged.tile([P, PICKS], F32, name="first_picked", align_bytes=64, offset=raw_end + 4 * (PIECE - S))[:]
         for s in range(1, STEPPED):
             lower = sbuf([P, 2 * S], F32, "lower")
             gained = arena[:, starts[s] : starts[s] + S]
             room_b = arena.rearrange("p (n c) -> p n c", c=HALF)[:, 0 : starts[s] // HALF + 1 : starts[s] // HALF, :]
+            if s == 1:
+                room_b = parts(arena[:, starts[2] + S : starts[2] + 2 * S])
             unload(s, 0, lower[:, 0:S], lower[:, S:])
             multiply(room_b, parts(lower[:, S:]), parts(lower[:, 0:S]))
+            if s in DEALT_CASTS:
+                both = arena[:, starts[s] - HALF : starts[s] + HALF].bitcast(BF16)
+                round_dealt(0, DEALT_CASTS[s], both, gpsimd_round, "p m t i")
             if s > 1:
                 nc.scalar.copy(out=spans[s % 2][:, 0:HALF], in_=hsum_a)
             if s == 1:
                 room_a = arena[:, starts[3] + S : starts[3] + 2 * S]
-                trig_a = sbuf([P, S], F32, "sixth")
+                trig_a = sbuf([P, S], F32, "codes3")
                 unload(s + 1, HALF, trig_a, inputs[:, 3 * S :])
                 multiply(room_a, inputs[:, 3 * S :], trig_a)
             else:
@@ -327,14 +337,12 @@ def tile_list_burst_derotation_kernel(
             hsum_b = turn(room_b, HALF)
             if s == 1:
                 nc.vector.tensor_tensor(out=gained[:, HALF:S], in0=hsum_a, in1=gains[s][:, HALF:S], op=MULT)
-                sources = [raw.rearrange("p i (m t) -> p m i t", t=1) for raw in raw_last]
-                quantise_late(3, 1, sources, arena[:, PIECE : PIECE + HALF].bitcast(BF16))
+                quantise(third, *quantised(3, 1))
             else:
                 nc.scalar.copy(out=lower_h, in_=hsum_b)
             if s in DEALT_CASTS:
-                t0 = DEALT_CASTS[s]
-                dealt = [later[:, n].rearrange("p i (m t) -> p m i t", t=PACK)[:, :, :, t0 : t0 + 2] for n in range(2)]
-                quantise_late(PACK + t0, 2, dealt, arena[:, starts[s] - HALF : starts[s] + HALF].bitcast(BF16))
+                round_dealt(1, DEALT_CASTS[s], both, nc.scalar.copy, "p m i t")
+                quantise(both, *quantised(PACK + DEALT_CASTS[s], 2))
             if s <= PACK:
                 nc.vector.tensor_copy(picked_first[s - 1], pages[page_of(s - 1)][:].indirect(idx3[:]))
             if s == 1:
@@ -348,7 +356,6 @@ def tile_list_burst_derotation_kernel(
         sixth_h = sixth[:, 0:S]
         last_h = sbuf([P, S], F32, "last_h")
         trig_two = sbuf([P, 2 * S], F32, "opening_trig")
-        late = sbuf([P, 3 * S], F32, "later")
         room_two = sbuf([P, 2 * S], F32, "lower")
         last_room = arena[:, starts[4] + S : starts[4] + 2 * S]
         units = (
@@ -356,9 +363,9 @@ def tile_list_burst_derotation_kernel(
             (FINAL, HALF, trig_two[:, S:], room_two[:, S:]),
             (FINAL, 0, sixth[:, S:], last_room),
         )
-        for u, (s, j0, trig, room) in enumerate(units):
-            unload(s, j0, trig, late[:, S * u : S * (u + 1)])
-            multiply(room, late[:, S * u : S * (u + 1)], trig)
+        for (s, j0, trig, room), pair in zip(units, (inputs[:, 3 * S :], spans[0][:, 0:S], spans[1][:, 0:S])):
+            unload(s, j0, trig, pair)
+            multiply(room, pair, trig)
         nc.scalar.copy(out=sixth_h[:, HALF:S], in_=hsum_a)
         for (s, j0, trig, room), h in zip(units, (sixth_h, last_h, last_h)):
             nc.scalar.copy(out=h[:, j0 : j0 + HALF], in_=turn(parts(room), HALF))
@@ -369,11 +376,11 @@ def tile_list_burst_derotation_kernel(
         nc.sync.dma_start(out=w4_codes, in_=w4_words.rearrange("a p c i -> p a (c i)").bitcast(I32))
         late_refs = staged.tile([P, PACK, PICKS], F32, name="late_refs", align_bytes=64, offset=0)[:]
         nc.sync.dma_start(out=late_refs, in_=dealt_ref)
-        first_refs = sbuf([P, PACK, PICKS], F32, "wide")
+        first_refs = sbuf([P, PACK, PICKS], F32, "later")
         nc.sync.dma_start(out=first_refs, in_=plain_ref)
         z_codes = sbuf([P, PASSES * PICKS], U32, "sixth")
         z_plane = sbuf([P, PASSES * PICKS], U8, "z_plane")
-        rounded = sbuf([P, PASSES * PICKS * PACK], BF16, "later")
+        rounded = sbuf([P, PASSES * PICKS * PACK], BF16, "wide")
         first_pass = [(m0, m0 + PIECE) for m0 in range(0, PICKS, PIECE)]
 
         def z_column(b, m):
@@ -393,11 +400,12 @@ def tile_list_burst_derotation_kernel(
                             out=turned[:, P * s : P * (s + 1)], lhsT=term[:, cols], rhs=ident[:], is_transpose=True,
                             start=(s == 0 and n == 0), stop=(s == PACK - 1 and n == 1),
                         )
-                pairs = sbuf([P, PASS], BF16, "pairs", 2)
-                nc.scalar.copy(out=pairs, in_=turned)
+                start = PACK * z_column(1, PIECE * b) + PASS * (m0 // PIECE % 2)
+                pairs = rounded[:, start : start + PASS]
+                nc.scalar.copy(out=pairs.rearrange("p (u q e) -> p u q e", u=2, e=2), in_=turned.rearrange("p (q u e) -> p u q e", u=2, e=2))
                 for u in range(2):
                     nc.tensor.matmul(
-                        out=words[:, b, u, :], lhsT=pairs.bitcast(F32)[:, u : PASS // 2 : 2], rhs=ident[:], is_transpose=True,
+                        out=words[:, b, u, :], lhsT=pairs.bitcast(F32)[:, P * u : P * (u + 1)], rhs=ident[:], is_transpose=True,
                         start=True, stop=True,
                     )
             c0 = PACK * z_column(0, m0)
@@ -418,7 +426,7 @@ def tile_list_burst_derotation_kernel(
                 )
 
         blocks = N // P
-        result = sbuf([P, blocks * PICKS], F32, "wide")
+        result = sbuf([P, blocks * PICKS], F32, "later")
 
         def pick(n):
             m0, m1 = pieces[n]

@@ -160,9 +160,9 @@ def tile_list_burst_derotation_kernel(
         def quantise_early(room, n, codes, plane):
             quantise(room.bitcast(BF16), codes[:, P * n : P * (n + 1)], plane[:, P * n : P * (n + 1)])
 
-        def round_dealt(n, t0, both, copy, walk):
-            source = later[:, n].rearrange("p i (m t) -> p i m t", t=PACK)[:, :, :, t0 : t0 + 2].rearrange("p i m t -> " + walk)
-            copy(out=both[:, S * n : S * (n + 1)].rearrange("p (t m i) -> " + walk, t=2, i=PACK), in_=source)
+        def round_dealt(n, t0, both):
+            source = later[:, n].rearrange("p i (m t) -> p m i t", t=PACK)[:, :, :, t0 : t0 + 2]
+            nc.scalar.copy(out=both[:, S * n : S * (n + 1)].rearrange("p (t m i) -> p m i t", t=2, i=PACK), in_=source)
 
         first_weights = quantised(0, 1)
         first_room = frames.tile([P, PIECE], F32, align_bytes=64, offset=4 * T2 - PASS)
@@ -318,9 +318,6 @@ def tile_list_burst_derotation_kernel(
                 room_b = parts(arena[:, starts[2] + S : starts[2] + 2 * S])
             unload(s, 0, lower[:, 0:S], lower[:, S:])
             multiply(room_b, parts(lower[:, S:]), parts(lower[:, 0:S]))
-            if s in DEALT_CASTS:
-                both = arena[:, starts[s] - HALF : starts[s] + HALF].bitcast(BF16)
-                round_dealt(0, DEALT_CASTS[s], both, gpsimd_round, "p m t i")
             if s > 1:
                 nc.scalar.copy(out=spans[s % 2][:, 0:HALF], in_=hsum_a)
             if s == 1:
@@ -341,7 +338,9 @@ def tile_list_burst_derotation_kernel(
             else:
                 nc.scalar.copy(out=lower_h, in_=hsum_b)
             if s in DEALT_CASTS:
-                round_dealt(1, DEALT_CASTS[s], both, nc.scalar.copy, "p m i t")
+                both = arena[:, starts[s] - HALF : starts[s] + HALF].bitcast(BF16)
+                for n in range(2):
+                    round_dealt(n, DEALT_CASTS[s], both)
                 quantise(both, *quantised(PACK + DEALT_CASTS[s], 2))
             if s <= PACK:
                 nc.vector.tensor_copy(picked_first[s - 1], pages[page_of(s - 1)][:].indirect(idx3[:]))

@@ -316,6 +316,8 @@ def tile_list_burst_derotation_kernel(
             room_b = arena.rearrange("p (n c) -> p n c", c=HALF)[:, 0 : starts[s] // HALF + 1 : starts[s] // HALF, :]
             if s == 1:
                 room_b = parts(arena[:, starts[2] + S : starts[2] + 2 * S])
+            if s == STEPPED - 1:
+                room_b = parts(arena[:, 0:S])
             unload(s, 0, lower[:, 0:S], lower[:, S:])
             multiply(room_b, parts(lower[:, S:]), parts(lower[:, 0:S]))
             if s > 1:
@@ -335,13 +337,13 @@ def tile_list_burst_derotation_kernel(
             if s == 1:
                 nc.vector.tensor_tensor(out=gained[:, HALF:S], in0=hsum_a, in1=gains[s][:, HALF:S], op=MULT)
                 quantise(third, *quantised(3, 1))
-            else:
-                nc.scalar.copy(out=lower_h, in_=hsum_b)
             if s in DEALT_CASTS:
                 both = arena[:, starts[s] - HALF : starts[s] + HALF].bitcast(BF16)
                 for n in range(2):
                     round_dealt(n, DEALT_CASTS[s], both)
                 quantise(both, *quantised(PACK + DEALT_CASTS[s], 2))
+            if s > 1:
+                nc.scalar.copy(out=lower_h, in_=hsum_b)
             if s <= PACK:
                 nc.vector.tensor_copy(picked_first[s - 1], pages[page_of(s - 1)][:].indirect(idx3[:]))
             if s == 1:
@@ -434,30 +436,46 @@ def tile_list_burst_derotation_kernel(
                 fetch(picked[:, t, :], PACK + t, m0, m1)
             return picked
 
-        def finish(n, banks, source):
-            m0, m1 = pieces[n]
-            c0 = z_column(0 if m0 % PIECE == 0 else 1, m0)
-            c1 = z_column(1, m0) + m1 - m0
+        def quantise_z(source, c0, c1):
             quantise(rounded[:, PACK * source : PACK * (source + c1 - c0)], z_codes[:, c0:c1], z_plane[:, c0:c1])
-            count = blocks // len(banks)
-            for r, (tag, copy) in zip(range(0, blocks, count), banks):
+
+        def open_sums(n):
+            m0, m1 = pieces[n]
+            count = blocks // len(banks[n])
+            for r, (tag, copy) in zip(range(0, blocks, count), banks[n]):
                 acc = psum.tile([P, count, m1 - m0], F32, name="acc", tag=tag, bufs=2)
-                for b in range(PASSES):
-                    last_product(acc, range(r, r + count), b, m0, m1)
-                first = blocks * m0 + r * (m1 - m0)
-                done = result[:, first : first + count * (m1 - m0)].rearrange("p (n m) -> p n m", n=count)
+                last_product(acc, range(r, r + count), 0, m0, m1)
+                sums.setdefault(n, []).append((acc, range(r, r + count), copy))
+
+        def close_sums(n):
+            m0, m1 = pieces[n]
+            for acc, rows, copy in sums[n]:
+                last_product(acc, rows, 1, m0, m1)
+                first = blocks * m0 + rows.start * (m1 - m0)
+                done = result[:, first : first + len(rows) * (m1 - m0)].rearrange("p (n m) -> p n m", n=len(rows))
                 copy(out=done, in_=acc[:])
-                nc.sync.dma_start(out=out.rearrange("(n p) m -> p n m", p=P)[:, r : r + count, m0:m1], in_=done)
+                nc.sync.dma_start(out=out.rearrange("(n p) m -> p n m", p=P)[:, rows.start : rows.stop, m0:m1], in_=done)
 
         banks = [[(tag, nc.scalar.copy)] * 2 for tag in ("phase", "inph", "quad")]
         banks.append([("hsum", nc.scalar.copy)])
         banks.append([("hsum", nc.scalar.copy), ("phase", nc.vector.tensor_copy)])
+        sums = {}
         last = len(pieces) - 1
+        quantise_z(0, 0, PIECE)
+        open_sums(0)
         round_planes(rounded_columns(1, *pieces[0]), pick(0), nc.scalar.copy)
         for n in range(last):
+            m0, m1 = pieces[n]
             picked = pick(n + 1)
             if n + 1 < last:
                 round_planes(rounded_columns(1, *pieces[n + 1]), picked, nc.scalar.copy)
-            finish(n, banks[n], z_column(0, pieces[n][0]))
-        round_planes(rounded_columns(0, *pieces[last - 1]), picked, nc.vector.tensor_copy)
-        finish(last, banks[last], z_column(0, pieces[last - 1][0]))
+            ahead = PIECE if n + 1 < last else 0
+            quantise_z(z_column(1, m0), z_column(1, m0), z_column(1, m0) + m1 - m0 + ahead)
+            close_sums(n)
+            for later_piece in range(n + 1, last + 1):
+                if pieces[later_piece][0] // PIECE == m0 // PIECE + 1:
+                    open_sums(later_piece)
+        round_planes(rounded_columns(1, *pieces[last - 1]), picked, nc.vector.tensor_copy)
+        c0 = z_column(1, pieces[last][0])
+        quantise_z(z_column(1, pieces[last - 1][0]), c0, c0 + P)
+        close_sums(last)

@@ -101,7 +101,7 @@ def tile_list_burst_derotation_kernel(
         raw_both = staged.tile([P, 2, PACK, P], F32, name="raw_both", align_bytes=64, offset=16 * PASS)[:]
         for n, w in enumerate((w1, w3)):
             nc.sync.dma_start(out=raw_both[:, n], in_=w[:, 2 * P : 3 * P].rearrange("(p i) c -> p i c", i=PACK))
-        raw_end = 8 * PASS * (PACK + 1)
+        raw_end = 8 * PASS * PACK
         raw_last = staged.tile([P, 2, PACK, P], F32, name="raw_last", align_bytes=64, offset=raw_end - 8 * PASS)[:]
         for n, w in enumerate((w1, w3)):
             nc.sync.dma_start(out=raw_last[:, n], in_=w[:, 3 * P : PASS].rearrange("(p i) c -> p i c", i=PACK))
@@ -292,30 +292,26 @@ def tile_list_burst_derotation_kernel(
                 both = trigs[1].bitcast(BF16)
                 gpsimd_round(both.rearrange("p (n c i) -> p n c i", n=2, i=PACK), raw_both.rearrange("p n i c -> p n c i"))
                 quantise(both, *quantised(2, 1))
-                third = arena[:, PIECE : PIECE + HALF].bitcast(BF16)
-                gpsimd_round(third.rearrange("p (n c i) -> p n c i", n=2, i=PACK), raw_last.rearrange("p n i c -> p n c i"))
             if u == 2:
-                room_a = staged.tile([P, S], F32, name="first_room_a", align_bytes=64, offset=raw_end + 4 * (PIECE - S))[:]
+                room_a = staged.tile([P, S], F32, name="first_room_a", align_bytes=64, offset=raw_end + 4 * PIECE)[:]
                 pair_a = sbuf([P, S], F32, "z_plane")
                 trig_a = opening_trig[:, S:]
                 unload(1, HALF, trig_a, pair_a)
                 multiply(room_a, pair_a, trig_a)
             hsum = turn(parts(rooms[u], j1 - j0), j1 - j0)
             if u == 1:
-                gained = staged.tile([P, PIECE], F32, name="second_gained", align_bytes=64, offset=raw_end + 4 * PIECE)[:]
+                gained = staged.tile([P, PIECE], F32, name="second_gained", align_bytes=64, offset=raw_end)[:]
             else:
                 gained = trigs[u][:, 0 : j1 - j0]
             nc.vector.tensor_tensor(out=gained, in0=hsum, in1=gains[0][:, j0:j1], op=MULT)
             place(0, j0, j1, gained)
 
         hsum_a = turn(parts(room_a), HALF)
-        picked_first[0] = staged.tile([P, PICKS], F32, name="first_picked", align_bytes=64, offset=raw_end + 4 * (PIECE - S))[:]
+        picked_first[0] = staged.tile([P, PICKS], F32, name="first_picked", align_bytes=64, offset=raw_end + 4 * PIECE)[:]
         for s in range(1, STEPPED):
             lower = sbuf([P, 2 * S], F32, "lower")
             gained = arena[:, starts[s] : starts[s] + S]
             room_b = arena.rearrange("p (n c) -> p n c", c=HALF)[:, 0 : starts[s] // HALF + 1 : starts[s] // HALF, :]
-            if s == 1:
-                room_b = parts(arena[:, starts[2] + S : starts[2] + 2 * S])
             if s == STEPPED - 1:
                 room_b = parts(arena[:, 0:S])
             unload(s, 0, lower[:, 0:S], lower[:, S:])
@@ -336,6 +332,8 @@ def tile_list_burst_derotation_kernel(
             hsum_b = turn(room_b, HALF)
             if s == 1:
                 nc.vector.tensor_tensor(out=gained[:, HALF:S], in0=hsum_a, in1=gains[s][:, HALF:S], op=MULT)
+                third = arena[:, PIECE : PIECE + HALF].bitcast(BF16)
+                nc.scalar.copy(out=third.rearrange("p (n c i) -> p n c i", n=2, i=PACK), in_=raw_last.rearrange("p n i c -> p n c i"))
                 quantise(third, *quantised(3, 1))
             if s in DEALT_CASTS:
                 both = arena[:, starts[s] - HALF : starts[s] + HALF].bitcast(BF16)

import math
from contextlib import ExitStack

import concourse.mybir as mybir
from concourse.masks import make_identity

K, H, N, T, S, T2, PICKS = 512, 1024, 512, 4096, 1024, 2048, 1024
FLOPS = 2 * 3 * K * H * S + 2 * H * N * PICKS

F32 = mybir.dt.float32
BF16 = mybir.dt.bfloat16
I32 = mybir.dt.int32
U32 = mybir.dt.uint32
U16 = mybir.dt.uint16
U8 = mybir.dt.uint8
FP8X4 = mybir.dt.float8_e4m3fn_x4
FP4X4 = mybir.dt.float4_e2m1fn_x4
ACT = mybir.ActivationFunctionType
MULT = mybir.AluOpType.mult
ADD = mybir.AluOpType.add

P = 128
PACK = 4
PASS = P * PACK
PASSES = H // PASS
SLICES = H // P
HALF = S // 2
PIECE = 256
CUTS = (0, 256, 512, 768, 896, 1024)
PAGES = PACK
FINAL = SLICES - 1
STEPPED = FINAL - 1
DEALT_CASTS = {2: 0, 3: 2}


def page_of(s):
    if s < PACK:
        return s % 2
    return (0, 2, 3, 1)[s - PACK]


def load_scale_rows(queue, plane, rows):
    for q in range(4):
        queue.dma_start(out=plane[32 * q : 32 * q + 4].bitcast(I32), in_=rows[4 * q : 4 * q + 4].bitcast(I32))


def tile_list_burst_derotation_kernel(
    tc, tab_words, tab_scales, offs, w1, w2_words, w2_scales, w3, wgs, offs2, offs3, ref, w4_words, w4_scales, out
):
    nc = tc.nc
    with ExitStack() as ctx:
        lists = ctx.enter_context(tc.tile_pool(name="lists", bufs=1))
        keep = ctx.enter_context(tc.tile_pool(name="keep", bufs=1))
        frames = ctx.enter_context(tc.tile_pool(name="frames", bufs=1))
        staged = ctx.enter_context(tc.tile_pool(name="staged", bufs=1))
        psum = ctx.enter_context(tc.psum_pool(name="psum", bufs=1))

        def sbuf(shape, dtype, tag, bufs=1):
            tile = keep.tile(shape, dtype, name=tag, tag=tag, bufs=bufs, align_bytes=64)
            return tile[:]

        tab_plane = keep.tile([P, T], U8, align_bytes=64)
        nc.vector.memset(tab_plane[:].bitcast(I32), 0)
        w2_rows = keep.tile([P, H], U8, align_bytes=64)
        nc.vector.memset(w2_rows[:].bitcast(I32), 0)
        w4_plane = keep.tile([P, PASSES, N], U8, align_bytes=64)
        nc.vector.memset(w4_plane[:].rearrange("p a n -> p (a n)").bitcast(I32), 0)
        pages = []
        for t in range(2):
            page = keep.tile([P, T2], F32, name="page%d" % t, align_bytes=64)
            nc.vector.memset(page[:], 0.0)
            pages.append(page)

        ident = keep.tile([P, P], F32)
        make_identity(nc, ident[:])

        def load_weight(n, s):
            raw = staged.tile([P, PACK, P], F32, name="raw%d_%d" % (n, s), align_bytes=64, offset=4 * PASS * (2 * s + n))
            nc.sync.dma_start(out=raw[:], in_=(w1, w3)[n][:, P * s : P * (s + 1)].rearrange("(p i) c -> p i c", i=PACK))
            return raw[:]

        plain_ref = ref[0:PASS].rearrange("(t p) m -> p t m", p=P)
        dealt_ref = ref[PASS:H].rearrange("(p t) m -> p t m", t=PACK)

        idx = lists.tile([P, S // 16], U16)
        nc.sync.dma_start(idx[:], offs)
        raw1 = [load_weight(0, 0)]
        w2_raw = keep.tile([P, 2 * H], U8, align_bytes=64)
        nc.sync.dma_start(out=w2_raw[:].bitcast(I32), in_=w2_words[0].bitcast(I32))
        load_scale_rows(nc.sync, tab_plane, tab_scales[0])
        tab = keep.tile([P, T], I32, tag="wide", align_bytes=64)
        nc.sync.dma_start(out=tab[:], in_=tab_words[0].rearrange("p t i -> p (t i)").bitcast(I32))
        raw3 = [load_weight(1, 0)]
        load_scale_rows(nc.sync, w2_rows, w2_scales[0])
        plain_gains = keep.tile([P, S], F32)
        raw1.append(load_weight(0, 1))
        raw3.append(load_weight(1, 1))
        nc.sync.dma_start(out=plain_gains[:, 0:HALF], in_=wgs[:, 0:HALF])
        idx2 = lists.tile([P, S // 16], U16)
        nc.sync.dma_start(idx2[:], offs2)
        raw_both = staged.tile([P, 2, PACK, P], F32, name="raw_both", align_bytes=64, offset=16 * PASS)[:]
        for n, w in enumerate((w1, w3)):
            nc.sync.dma_start(out=raw_both[:, n], in_=w[:, 2 * P : 3 * P].rearrange("(p i) c -> p i c", i=PACK))
        raw_end = 8 * PASS * PACK
        raw_last = staged.tile([P, 2, PACK, P], F32, name="raw_last", align_bytes=64, offset=raw_end - 8 * PASS)[:]
        for n, w in enumerate((w1, w3)):
            nc.sync.dma_start(out=raw_last[:, n], in_=w[:, 3 * P : PASS].rearrange("(p i) c -> p i c", i=PACK))
        nc.sync.dma_start(out=plain_gains[:, HALF:S], in_=wgs[:, HALF:S])
        idx3 = lists.tile([P, PICKS // 16], U16)
        nc.sync.dma_start(idx3[:], offs3)
        arena = sbuf([P, HALF + S + (PACK - 1) * PICKS + 4 * S], F32, "arena")
        lower_h = arena[:, 0:HALF]
        starts = {1: HALF, 2: HALF + S + PICKS, 3: HALF + 3 * S + 2 * PICKS}
        starts.update({4: starts[2], 5: starts[3]})
        picked_first = {s: arena[:, c : c + PICKS] for s, c in ((1, starts[2] - PICKS), (2, starts[3] - PICKS), (3, starts[3] + 2 * S))}

        def load_dealt(dst, t, j0, j1):
            for q in (0, 2, 1, 3):
                nc.sync.dma_start(out=dst[32 * q : 32 * (q + 1)], in_=wgs.rearrange("(q t) j -> q t j", t=PACK)[:, t, j0:j1])

        def load_factors(s):
            factors[s] = sbuf([P, HALF + S], F32, "factors", 3)
            if s < PACK:
                nc.sync.dma_start(out=factors[s][:, 0:HALF], in_=wgs[:, HALF:S])
            else:
                load_dealt(factors[s][:, 0:HALF], s - PACK, HALF, S)

        factors = {}
        load_factors(2)
        later = keep.tile([P, 2, PACK, PASS], F32, tag="later", align_bytes=64)
        for n, w in enumerate((w1, w3)):
            nc.sync.dma_start(out=later[:, n], in_=w[:, PASS:H].rearrange("(p i) c -> p i c", i=PACK))
        load_factors(3)
        load_factors(4)
        dealt_gains = sbuf([P, 2, HALF], F32, "dealt_gains")
        load_dealt(dealt_gains, slice(0, 2), 0, HALF)
        last_gains = sbuf([P, 2, S], F32, "last_gains")
        load_dealt(last_gains, slice(2, PACK), 0, S)
        gains = [plain_gains[:]] * PACK + [dealt_gains[:, t, :] for t in range(2)]
        load_scale_rows(nc.sync, w4_plane, w4_scales.rearrange("a q n -> q a n"))

        def quantise(grouped, codes, plane):
            nc.vector.quantize_mx(out=codes.bitcast(FP8X4), scales=plane, in_=grouped)

        def gpsimd_round(out, in_):
            nc.gpsimd.tensor_scalar(out=out, in0=in_, scalar1=1.0, scalar2=0.0, op0=MULT, op1=ADD)

        weights = {}

        def quantised(s0, count):
            codes = sbuf([P, 2, count, P], U32, "codes%d" % s0)
            plane = sbuf([P, 2, count, P], U8, "plane%d" % s0)
            for t in range(count):
                weights[s0 + t] = [(codes[:, n, t, :].bitcast(FP8X4), plane[:, n, t, :]) for n in range(2)]
            return codes.rearrange("p n t m -> p (n t m)"), plane.rearrange("p n t m -> p (n t m)")

        def round_early(room, raw):
            nc.vector.tensor_copy(out=room.bitcast(BF16).rearrange("p (c i) -> p c i", i=PACK), in_=raw.rearrange("p i c -> p c i"))

        def quantise_early(room, n, codes, plane):
            quantise(room.bitcast(BF16), codes[:, P * n : P * (n + 1)], plane[:, P * n : P * (n + 1)])

        def round_dealt(n, t0, both):
            source = later[:, n].rearrange("p i (m t) -> p m i t", t=PACK)[:, :, :, t0 : t0 + 2]
            nc.scalar.copy(out=both[:, S * n : S * (n + 1)].rearrange("p (t m i) -> p m i t", t=2, i=PACK), in_=source)

        first_weights = quantised(0, 1)
        first_room = frames.tile([P, PIECE], F32, align_bytes=64, offset=4 * T2 - PASS)
        round_early(first_room[:], raw1[0])
        w2_dealt = sbuf([P, 2 * PASS], U8, "w2_dealt")
        nc.vector.tensor_copy(
            out=w2_dealt.bitcast(U16).rearrange("p (t m) -> p t m", t=PACK),
            in_=w2_raw[:, 2 * PASS : 2 * H].bitcast(U16).rearrange("p (m t) -> p t m", t=PACK),
        )
        quantise_early(first_room[:], 0, *first_weights)
        v_plane = sbuf([P, S], U8, "v_plane")
        nc.vector.tensor_copy(v_plane, tab_plane[:].indirect(idx[:]))
        for t in range(2, PAGES):
            page = frames.tile([P, T2], F32, name="page%d" % t, align_bytes=64, offset=4 * T2 * (t - 2))
            nc.gpsimd.memset(page[:], 0.0)
            pages.append(page)
        v_codes = []

        def gather_words(g):
            words = sbuf([P, HALF], U32, "v_codes%d" % g)
            nc.vector.tensor_copy(words, tab[:].bitcast(U32).indirect(idx[:, 32 * g : 32 * g + 32]))
            v_codes.append(words)

        gather_words(0)
        second_room = sbuf([P, PIECE], F32, "v_codes1")
        round_early(second_room, raw3[0])
        quantise_early(second_room, 1, *first_weights)
        gather_words(1)
        w2_plane = sbuf([P, PASS], U8, "w2_plane")
        nc.vector.tensor_copy(
            out=w2_plane.rearrange("p (t m) -> p t m", t=PACK),
            in_=w2_rows[:, PASS:H].rearrange("p (m t) -> p t m", t=PACK),
        )
        q2 = [(w2_raw, w2_rows), (w2_dealt, w2_plane)]
        inputs = sbuf([P, PACK * S], F32, "wide")
        spans = [inputs[:, (HALF + S) * t : (HALF + S) * (t + 1)] for t in range(2)]

        def first_product(j0, j1, bank, codes, plane):
            for j in range(j0, j1, P):
                nc.tensor.matmul_mx(
                    out=bank[:, j - j0 : j - j0 + P],
                    lhsT=v_codes[j // HALF][:, j % HALF : j % HALF + P].bitcast(FP8X4),
                    lhsT_scale=v_plane[:, j : j + P],
                    rhs=codes,
                    rhs_scale=plane,
                    start=True,
                    stop=True,
                )

        def new_bank(tag):
            bank = psum.tile([P, HALF], F32, name=tag, tag=tag, bufs=2)
            return bank[:]

        def features(s, j0, j1, phase, inph, quad):
            b, t = divmod(s, PACK)
            cols = slice(P * t, P * (t + 1))
            first_product(j0, j1, phase, *weights[s][0])
            first_product(j0, j1, inph, q2[b][0][:, 2 * P * t : 2 * P * (t + 1)].bitcast(FP4X4), q2[b][1][:, cols])
            first_product(j0, j1, quad, *weights[s][1])

        def cosine(out, size):
            nc.scalar.activation(out=out, in_=size, func=ACT.Sin, scale=-1.0, bias=math.pi / 2)

        def derotate_on_vector(j0, j1, trig, room, tags):
            width = j1 - j0
            phase = new_bank("phase")[:, 0:width]
            banks = [new_bank(tag) for tag in tags]
            features(0, j0, j1, phase, banks[0][:, 0:width], banks[-1][:, HALF - width : HALF])
            size = sbuf([P, width], F32, "size", 2)
            nc.scalar.activation(out=trig[:, width : 2 * width], in_=phase, func=ACT.Sin)
            nc.scalar.activation(out=size, in_=phase, func=ACT.Abs)
            cosine(trig[:, 0:width], size)
            for n, bank in enumerate(banks):
                cols = slice(HALF * n, HALF * (n + 1))
                nc.vector.tensor_tensor(out=room[:, cols], in0=bank, in1=trig[:, cols], op=MULT)

        def unload(s, j0, trig, pair):
            phase, inph, quad = new_bank("phase"), new_bank("inph"), new_bank("quad")
            features(s, j0, j0 + HALF, phase, inph, quad)
            size = sbuf([P, HALF], F32, "size", 2)
            nc.scalar.activation(out=size, in_=phase, func=ACT.Abs)
            nc.scalar.activation(out=trig[:, HALF:S], in_=phase, func=ACT.Sin)
            nc.scalar.copy(out=pair[:, 0:HALF], in_=inph)
            cosine(trig[:, 0:HALF], size)
            nc.scalar.copy(out=pair[:, HALF:S], in_=quad)

        def multiply(out, in0, in1):
            nc.gpsimd.tensor_tensor(out=out, in0=in0, in1=in1, op=MULT)

        def parts(ap, width=HALF):
            return ap[:, 0 : 2 * width].rearrange("p (n c) -> p n c", n=2)

        def turn(room, width):
            hsum = psum.tile([P, width], F32, name="hsum", tag="hsum", bufs=2)
            for j in range(0, 2 * width, P):
                nc.tensor.matmul(
                    out=hsum[:, j % width : j % width + P], lhsT=room[:, j // width, j % width : j % width + P], rhs=ident[:], is_transpose=True,
                    start=(j == 0), stop=(j == 2 * width - P),
                )
            return hsum[:]

        def place(s, j0, j1, gained):
            nc.vector.tensor_copy(pages[page_of(s)][:].indirect(idx2[:, j0 // 16 : j1 // 16]), gained)

        def fetch(dst, s, m0, m1):
            nc.vector.tensor_tensor(dst, pages[page_of(s)][:].indirect(idx3[:, m0 // 16 : m1 // 16]), late_refs[:, s - PACK, m0:m1], ADD)

        def round_planes(out, z, copy):
            copy(out=out.rearrange("p (c e) t -> p c t e", e=4), in_=z.rearrange("p t (c e) -> p c t e", e=4))

        pieces = list(zip(CUTS, CUTS[1:]))

        opening = ((0, PIECE), (PIECE, HALF), (HALF, S))
        rooms = [sbuf([P, S], F32, tag) for tag in ("z0_codes", "z1_codes", "last_h")]
        early = staged.tile([P, HALF], F32, align_bytes=64, offset=raw_end)
        opening_trig = sbuf([P, 2 * S], F32, "opening_trig")
        trigs = [sbuf([P, HALF], F32, "grouped0"), early[:, 0:HALF], opening_trig[:, 0:S]]
        derotate_on_vector(*opening[0], trigs[0], rooms[0], ["inph"])
        second_weights = quantised(1, 1)
        for n, raw in enumerate((raw1[1], raw3[1])):
            round_early(rooms[1][:, PIECE * n : PIECE * (n + 1)], raw)
            quantise_early(rooms[1][:, PIECE * n : PIECE * (n + 1)], n, *second_weights)
        derotate_on_vector(*opening[1], trigs[1], rooms[1], ["quad"])
        for u, (j0, j1) in enumerate(opening):
            if u == 0:
                derotate_on_vector(*opening[2], trigs[2], rooms[2], ["inph", "quad"])
                both = trigs[1].bitcast(BF16)
                gpsimd_round(both.rearrange("p (n c i) -> p n c i", n=2, i=PACK), raw_both.rearrange("p n i c -> p n c i"))
                quantise(both, *quantised(2, 1))
            if u == 2:
                room_a = staged.tile([P, S], F32, name="first_room_a", align_bytes=64, offset=raw_end + 4 * PIECE)[:]
                pair_a = sbuf([P, S], F32, "z_plane")
                trig_a = opening_trig[:, S:]
                unload(1, HALF, trig_a, pair_a)
                multiply(room_a, pair_a, trig_a)
            hsum = turn(parts(rooms[u], j1 - j0), j1 - j0)
            if u == 1:
                gained = staged.tile([P, PIECE], F32, name="second_gained", align_bytes=64, offset=raw_end)[:]
            else:
                gained = trigs[u][:, 0 : j1 - j0]
            nc.vector.tensor_tensor(out=gained, in0=hsum, in1=gains[0][:, j0:j1], op=MULT)
            place(0, j0, j1, gained)

        hsum_a = turn(parts(room_a), HALF)
        picked_first[0] = staged.tile([P, PICKS], F32, name="first_picked", align_bytes=64, offset=raw_end + 4 * PIECE)[:]
        for s in range(1, STEPPED):
            lower = sbuf([P, 2 * S], F32, "lower")
            gained = arena[:, starts[s] : starts[s] + S]
            room_b = arena.rearrange("p (n c) -> p n c", c=HALF)[:, 0 : starts[s] // HALF + 1 : starts[s] // HALF, :]
            if s == STEPPED - 1:
                room_b = parts(arena[:, 0:S])
            unload(s, 0, lower[:, 0:S], lower[:, S:])
            multiply(room_b, parts(lower[:, S:]), parts(lower[:, 0:S]))
            if s > 1:
                nc.scalar.copy(out=spans[s % 2][:, 0:HALF], in_=hsum_a)
            if s == 1:
                room_a = arena[:, starts[3] + S : starts[3] + 2 * S]
                trig_a = sbuf([P, S], F32, "codes3")
                unload(s + 1, HALF, trig_a, inputs[:, 3 * S :])
                multiply(room_a, inputs[:, 3 * S :], trig_a)
            else:
                room_a = arena[:, starts[s] + S : starts[s] + 2 * S]
                unload(s + 1, HALF, factors[s][:, HALF:], spans[s % 2][:, HALF:])
                multiply(arena[:, starts[s] + HALF : starts[s] + 2 * S], spans[s % 2], factors[s])
            if s + 3 == STEPPED - 1:
                load_factors(s + 3)
            hsum_b = turn(room_b, HALF)
            if s == 1:
                nc.vector.tensor_tensor(out=gained[:, HALF:S], in0=hsum_a, in1=gains[s][:, HALF:S], op=MULT)
                third = arena[:, PIECE : PIECE + HALF].bitcast(BF16)
                nc.scalar.copy(out=third.rearrange("p (n c i) -> p n c i", n=2, i=PACK), in_=raw_last.rearrange("p n i c -> p n c i"))
                quantise(third, *quantised(3, 1))
            if s in DEALT_CASTS:
                both = arena[:, starts[s] - HALF : starts[s] + HALF].bitcast(BF16)
                for n in range(2):
                    round_dealt(n, DEALT_CASTS[s], both)
                quantise(both, *quantised(PACK + DEALT_CASTS[s], 2))
            if s > 1:
                nc.scalar.copy(out=lower_h, in_=hsum_b)
            if s <= PACK:
                nc.vector.tensor_copy(picked_first[s - 1], pages[page_of(s - 1)][:].indirect(idx3[:]))
            if s == 1:
                nc.vector.tensor_tensor(out=gained[:, 0:HALF], in0=hsum_b, in1=gains[s][:, 0:HALF], op=MULT)
            else:
                multiply(gained[:, 0:HALF], lower_h, gains[s][:, 0:HALF])
            hsum_a = turn(parts(room_a), HALF)
            place(s, 0, S, gained)

        sixth = sbuf([P, 2 * S], F32, "sixth")
        sixth_h = sixth[:, 0:S]
        last_h = sbuf([P, S], F32, "last_h")
        trig_two = sbuf([P, 2 * S], F32, "opening_trig")
        room_two = sbuf([P, 2 * S], F32, "lower")
        last_room = arena[:, starts[4] + S : starts[4] + 2 * S]
        units = (
            (STEPPED, 0, trig_two[:, 0:S], room_two[:, 0:S]),
            (FINAL, HALF, trig_two[:, S:], room_two[:, S:]),
            (FINAL, 0, sixth[:, S:], last_room),
        )
        for (s, j0, trig, room), pair in zip(units, (inputs[:, 3 * S :], spans[0][:, 0:S], spans[1][:, 0:S])):
            unload(s, j0, trig, pair)
            multiply(room, pair, trig)
        nc.scalar.copy(out=sixth_h[:, HALF:S], in_=hsum_a)
        for (s, j0, trig, room), h in zip(units, (sixth_h, last_h, last_h)):
            nc.scalar.copy(out=h[:, j0 : j0 + HALF], in_=turn(parts(room), HALF))
        for t, h in enumerate((sixth_h, last_h)):
            nc.vector.tensor_tensor(pages[page_of(STEPPED + t)][:].indirect(idx2[:]), h, last_gains[:, t, :], MULT)

        w4_codes = sbuf([P, PASSES, N], I32, "w4_codes")
        nc.sync.dma_start(out=w4_codes, in_=w4_words.rearrange("a p c i -> p a (c i)").bitcast(I32))
        late_refs = staged.tile([P, PACK, PICKS], F32, name="late_refs", align_bytes=64, offset=0)[:]
        nc.sync.dma_start(out=late_refs, in_=dealt_ref)
        first_refs = sbuf([P, PACK, PICKS], F32, "later")
        nc.sync.dma_start(out=first_refs, in_=plain_ref)
        z_codes = sbuf([P, PASSES * PICKS], U32, "sixth")
        z_plane = sbuf([P, PASSES * PICKS], U8, "z_plane")
        rounded = sbuf([P, PASSES * PICKS * PACK], BF16, "wide")
        first_pass = [(m0, m0 + PIECE) for m0 in range(0, PICKS, PIECE)]

        def z_column(b, m):
            return PIECE * (m // PIECE + b) + m

        def rounded_columns(b, m0, m1):
            return rounded[:, PACK * z_column(b, m0) : PACK * (z_column(b, m0) + m1 - m0)].rearrange("p (m t) -> p m t", t=PACK)

        for m0, m1 in first_pass:
            words = psum.tile([P, 2, 2, P], F32, name="words", tag="quad", bufs=2)
            for b in range(2):
                cols = slice(m0 + P * b, m0 + P * (b + 1))
                turned = new_bank(("phase", "inph")[b])
                for s in range(PACK):
                    for n, term in enumerate((picked_first[s], first_refs[:, s, :])):
                        nc.tensor.matmul(
                            out=turned[:, P * s : P * (s + 1)], lhsT=term[:, cols], rhs=ident[:], is_transpose=True,
                            start=(s == 0 and n == 0), stop=(s == PACK - 1 and n == 1),
                        )
                start = PACK * z_column(1, PIECE * b) + PASS * (m0 // PIECE % 2)
                pairs = rounded[:, start : start + PASS]
                nc.scalar.copy(out=pairs.rearrange("p (u q e) -> p u q e", u=2, e=2), in_=turned.rearrange("p (q u e) -> p u q e", u=2, e=2))
                for u in range(2):
                    nc.tensor.matmul(
                        out=words[:, b, u, :], lhsT=pairs.bitcast(F32)[:, P * u : P * (u + 1)], rhs=ident[:], is_transpose=True,
                        start=True, stop=True,
                    )
            c0 = PACK * z_column(0, m0)
            target = rounded[:, c0 : c0 + PACK * PIECE].bitcast(F32).rearrange("p (b m u) -> p b m u", b=2, u=2)
            nc.scalar.copy(out=target, in_=words[:].rearrange("p b u m -> p b m u"))

        def last_product(acc, rows, b, m0, m1):
            cols = slice(z_column(b, m0), z_column(b, m0) + m1 - m0)
            for n, row in enumerate(rows):
                nc.tensor.matmul_mx(
                    out=acc[:, n, :],
                    lhsT=w4_codes[:, b, P * row : P * (row + 1)].bitcast(FP8X4),
                    lhsT_scale=w4_plane[:, b, P * row : P * (row + 1)],
                    rhs=z_codes[:, cols].bitcast(FP8X4),
                    rhs_scale=z_plane[:, cols],
                    start=(b == 0 and n == 0),
                    stop=(b == PASSES - 1 and n == len(rows) - 1),
                )

        blocks = N // P
        result = sbuf([P, blocks * PICKS], F32, "later")

        def pick(n):
            m0, m1 = pieces[n]
            picked = sbuf([P, PACK, m1 - m0], F32, ("last_h", "last_gains")[n % 2])
            for t in range(PACK):
                fetch(picked[:, t, :], PACK + t, m0, m1)
            return picked

        def quantise_z(source, c0, c1):
            quantise(rounded[:, PACK * source : PACK * (source + c1 - c0)], z_codes[:, c0:c1], z_plane[:, c0:c1])

        def open_sums(n):
            m0, m1 = pieces[n]
            count = blocks // len(banks[n])
            for r, (tag, copy) in zip(range(0, blocks, count), banks[n]):
                acc = psum.tile([P, count, m1 - m0], F32, name="acc", tag=tag, bufs=2)
                last_product(acc, range(r, r + count), 0, m0, m1)
                sums.setdefault(n, []).append((acc, range(r, r + count), copy))

        def close_sums(n):
            m0, m1 = pieces[n]
            for acc, rows, copy in sums[n]:
                last_product(acc, rows, 1, m0, m1)
                first = blocks * m0 + rows.start * (m1 - m0)
                done = result[:, first : first + len(rows) * (m1 - m0)].rearrange("p (n m) -> p n m", n=len(rows))
                copy(out=done, in_=acc[:])
                nc.sync.dma_start(out=out.rearrange("(n p) m -> p n m", p=P)[:, rows.start : rows.stop, m0:m1], in_=done)

        banks = [[(tag, nc.scalar.copy)] * 2 for tag in ("phase", "inph", "quad")]
        banks.append([("hsum", nc.scalar.copy)])
        banks.append([("hsum", nc.scalar.copy), ("phase", nc.vector.tensor_copy)])
        sums = {}
        last = len(pieces) - 1
        quantise_z(0, 0, PIECE)
        open_sums(0)
        round_planes(rounded_columns(1, *pieces[0]), pick(0), nc.scalar.copy)
        for n in range(last):
            m0, m1 = pieces[n]
            picked = pick(n + 1)
            if n + 1 < last:
                round_planes(rounded_columns(1, *pieces[n + 1]), picked, nc.scalar.copy)
            ahead = PIECE if n + 1 < last else 0
            quantise_z(z_column(1, m0), z_column(1, m0), z_column(1, m0) + m1 - m0 + ahead)
            close_sums(n)
            for later_piece in range(n + 1, last + 1):
                if pieces[later_piece][0] // PIECE == m0 // PIECE + 1:
                    open_sums(later_piece)
        round_planes(rounded_columns(1, *pieces[last - 1]), picked, nc.vector.tensor_copy)
        c0 = z_column(1, pieces[last][0])
        quantise_z(z_column(1, pieces[last - 1][0]), c0, c0 + P)
        close_sums(last)
